import numpy as np, ml_dtypes
CORES = [16,17,18,19,150,151]
N = 6
BF = ml_dtypes.bfloat16
V, B, L, CAP, RO = 512, 512, 256, 48, 4
W, NB = N * V, N * B
def by_good(a):
    return np.ascontiguousarray(a.reshape(N, 8, 16, -1).transpose(1, 0, 3, 2)).reshape(8, -1, 16)
def by_rank(a):
    return np.ascontiguousarray(a.reshape(8, N, -1, 16).transpose(1, 0, 3, 2)).reshape(N, 128, -1)
def money(rng, lo, hi):
    return (0.5 + 0.5 * rng.random((8, NB, 16))) * np.exp2(rng.integers(lo, hi, (8, NB, 1)))
def rooms(rng):
    n = rng.choice(np.array([0, 1, 2, 3, 6, 16]), (8, W, 1), p=[0.1, 0.35, 0.25, 0.15, 0.1, 0.05])
    return np.argsort(rng.random((8, W, 16)), axis=-1) < n
def lodge(rng, room, stay, first, old, fixed=()):
    H = np.where(room, 0, NB + 1).astype(np.int64); hold = np.full((8, NB), W, np.int64)
    for g in range(8):
        h = H[g].reshape(-1).copy(); free = room[g].reshape(-1).copy(); st = stay[g].copy()
        for m, x, s, b, sign in fixed:
            if m == g: h[16 * x + s] = sign * (b + 1); free[16 * x + s] = False; st[b] = False; hold[g, b] = x
        key = np.where(free, rng.random(16 * W) + np.repeat(first[g], 16), 1e9)
        names = rng.permutation(np.flatnonzero(st)); n = min(len(names), int(np.count_nonzero(free)))
        names = names[:n]; pl = np.argsort(key)[:n]
        h[pl] = (names + 1) * np.where(rng.random(n) < old[g][pl // 16], -1, 1); hold[g, names] = pl // 16
        H[g] = h.reshape(W, 16)
    return H, hold
def parts(rng):
    n = W // 8; hot = np.argsort(rng.random((8, W)), axis=1)[:, :n]; F = rng.integers(0, W, (8, NB, 16)); first = np.ones((8, W))
    for g in range(8):
        F[g] = np.where(rng.random((NB, 16)) < 0.5, hot[g][rng.integers(0, n, (NB, 16))], F[g]); first[g, hot[g]] = 0.0
    U = rng.integers(1, 16, (8, NB, 16)); A = rng.random((8, W, 16), dtype=np.float32) * np.float32(0.75) + np.float32(0.25)
    return F, U, A, money(rng, -1, 2), rooms(rng), rng.random((8, NB)) < 0.42, first, rng.random((8, W))
def pack(F, U, M, A, H, hold):
    return {"ft": by_rank(F).astype(np.int32), "ut": by_rank(U).astype(np.float32).astype(BF), "mon": by_rank(M).astype(np.float32).astype(BF), "al": by_rank(A).astype(np.float32),
            "hn": by_rank(H).astype(np.int32), "hb": np.ascontiguousarray(hold.reshape(8, N, B).transpose(1, 0, 2)).astype(np.int32)}
def chain(n, k):
    c = np.float32(1.0)
    for i in range(n): c = c * np.float32(0.9375)
    return c if k == 0 else np.nextafter(c, np.float32(0.0 if k < 0 else 2.0))
def pair(rng, i):
    u = 2 ** int(rng.integers(0, 4)); c = (0.6 + 0.39 * rng.random(4096)).astype(np.float32); w = c.astype(np.float64)
    if i == 0:
        ux, uy = ((15, 13), (9, 15), (13, 11), (11, 9))[int(rng.integers(0, 4))]; lo, hi = 0.5 * max(ux, uy) + 0.01, min(ux, uy) - 0.01
        p = lo + (hi - lo) * rng.random(4096); a = (p * float(ux) ** -1.0).astype(np.float32); b = (p * float(uy) ** -1.0).astype(np.float32)
        k = np.flatnonzero((np.float32(ux) * a == np.float32(uy) * b) & (ux * a.astype(np.float64) < uy * b.astype(np.float64)))[:16]
        return ux, uy, a[k], b[k], False
    if i == 1:
        r = c * np.float32(0.9375); k = np.flatnonzero(r.astype(np.float64) > w * 0.9375)[:16]
        return u, u, c[k], r[k], True
    if i == 2:
        r = c * np.float32(0.9375) * np.float32(0.9375); k = np.flatnonzero(r > (w * 0.87890625).astype(np.float32))[:16]
        return u, u, c[k], r[k], True
    if i == 3:
        a = (rng.integers(2 ** 21, 2 ** 22, 16) * 2.0 ** -24).astype(np.float32)
        return u, u, a, np.nextafter(a, np.float32(1.0)), False
    if i == 4:
        j = rng.integers(3100000, 5500000, 16); a = (j * 2.0 ** -24).astype(np.float32); low = rng.permutation(16) >= int(rng.integers(8, 16))
        return 15, 5, np.where(low, a * np.float32(0.75), a), (3 * j * 2.0 ** -24).astype(np.float32), False
    a = c[:16].copy(); k = int(rng.integers(0, 16)); a[k] = np.nextafter(a[k], np.float32(0.0))
    return u, u, a, c[:16].copy(), False
def setup_inputs(rng):
    F, U, A, M, room, stay, first, old = parts(rng)
    H, hold = lodge(rng, room, stay, first, old)
    return pack(F, U, M, A, H, hold)
def setup_inputs_spread(rng):
    F, U, A, M, room, stay, first, old = parts(rng)
    A = np.clip(np.exp2(-1.5 * (rng.random((8, W, 1)) + rng.random((8, W, 16)))), 0.125, 1.0); M = money(rng, -1, 3)
    F = np.minimum((W * rng.random(F.shape) ** 3).astype(np.int64), W - 1); F[1::2] = W - 1 - F[1::2]
    U = np.minimum(np.exp2(4 * rng.random(U.shape)).astype(np.int64), 15)
    first = np.tile(np.arange(W) * (8.0 / W), (8, 1)); first[1::2] = first[1::2, ::-1]
    H, hold = lodge(rng, room, stay, first, old)
    return pack(F, U, M, A, H, hold)
def setup_inputs_ends(rng):
    F, U, A, M, room, stay, first, old = parts(rng)
    e = rng.random((8, N, B)) < 0.72; e[:, :, B - 1] = True
    F = np.where(e.reshape(8, NB, 1), (W - 1) * rng.integers(0, 2, F.shape), rng.integers(0, W, F.shape))
    U = 1 + 14 * rng.integers(0, 2, U.shape); A = np.where(rng.random(A.shape) < 0.5, 0.125, 1.0)
    A[::2, 0] = 1.0; A[::2, W - 1] = 1.0
    for i in range(16): A[:, W - 2 - i] = 0.125; A[:, W - 2 - i, i] = 1.0
    b = np.arange(7, NB, 32); F[:, b] = W - 2 - np.argsort(rng.random((8, len(b), 16)), axis=-1); U[:, b] = 15
    M = np.where(rng.random(M.shape) < 0.5, 0.25, 4.0)
    stay = rng.random((8, NB)) < 0.36; room[:, 0] = False; room[:, 0, :N] = True; fixed = []
    for g in range(8):
        z = (g % N) * V + V - 1; room[g, z] = False; room[g, z, 15] = True
        if g % 4 == 0: room[g, 0, N] = True; fixed.append((g, 0, N, NB - 1, 1))
        else: fixed.append((g, z, 15, NB - 1, -1))
        for q in range(N): fixed.append((g, 0, q, q * B, 1 if g % 4 == 0 else 1 - 2 * int(rng.integers(0, 2))))
    H, hold = lodge(rng, room, stay, first, old, fixed)
    return pack(F, U, M, A, H, hold)
def setup_inputs_corners(rng):
    F, U, A, M, room, stay, first, old = parts(rng)
    n = rng.choice(np.array([0, 1, 1, 2, 8, 15, 16]), (8, W, 1)); kind = rng.integers(0, 3, (8, W, 1)); i = np.arange(16)
    room = np.where(kind == 0, i < n, np.where(kind == 1, i >= 16 - n, np.argsort(rng.random((8, W, 16)), axis=-1) < n))
    first = 2.0 * n[:, :, 0]; old = rng.choice(np.array([0.0, 0.5, 1.0]), (8, W)); stay = np.ones((8, NB), bool)
    F = np.where(rng.random(F.shape) < 0.1, V * rng.integers(0, N, F.shape) + (V - 1) * rng.integers(0, 2, F.shape), F)
    sh = int(rng.integers(0, 8)); counts = [0, 1, 2, 3, L - 1, L, L + 1, B]
    for g in range(8):
        for q in range(N):
            hm = np.sort(rng.permutation(B)[:counts[(g + q + sh) % 8]]); stay[g, q * B + hm] = False
            lane = hm[:L]; o = (q + 1 + rng.permutation(N - 1)) % N; rest = np.append(o[3:], q)
            to = np.concatenate([np.repeat(o[0], CAP), np.repeat(o[1], CAP + 1), np.repeat(o[2], CAP - 1), rng.choice(rest, L - 3 * CAP)])
            to = rng.permutation(to[:len(lane)])
            v = rng.integers(0, V, (len(lane), 16))
            if g % 2: v = rng.integers(0, 24, v.shape) + (V - 24) * rng.integers(0, 2, v.shape)
            F[g, q * B + lane] = V * to[:, None] + v
    z = rng.random(M.shape)
    M = np.where(z < 0.5, 4.0, np.where(z < 0.7, 0.25, M))
    H, hold = lodge(rng, room, stay, first, old)
    return pack(F, U, M, A, H, hold)
def setup_inputs_crowd(rng):
    F, U, A, M, room, stay, first, old = parts(rng)
    for g, x, y, c in ((0, W - 1, 0, chain(RO - 1, -1)), (1, 0, W - 1, chain(RO - 1, 0)), (2, V, V - 1, chain(RO - 1, 1)), (3, W - 1, V // 2, chain(1, 0))):
        stay[g] = False; F[g] = x; F[g, :, 0] = y; U[g] = 15; A[g, x] = 1.0; A[g, y] = c; room[g, x] = False; room[g, y] = False
        if g == 3: room[g, x, 15] = True
        if g >= 2:
            for q in range(N):
                b = q * B + np.arange(int(rng.integers(0, L)), B, L); F[g, b] = rng.integers(0, W, (len(b), 16)); U[g, b] = rng.integers(1, 16, (len(b), 16))
    few = rng.permutation(W)[:4]; F[4] = few[rng.integers(0, 4, F[4].shape)]; first[4, few] = -1.0
    one = V * np.arange(N) + rng.integers(0, V, N); F[5] = one[rng.integers(0, N, F[5].shape)]; first[5, one] = -1.0
    owner = int(rng.integers(0, N)); home = (owner + 1 + int(rng.integers(0, N - 1))) % N
    pv = owner * V + rng.permutation(V); xs, rest = pv[:N * CAP], pv[N * CAP:]; sl = rng.integers(0, 16, N * CAP); held = home * B + CAP + rng.permutation(B - CAP)[:N * CAP]
    bs = (B * np.arange(N)[:, None] + np.arange(CAP)).reshape(-1)
    for g in (6, 7): stay[g, bs] = False; F[g, bs] = xs[:, None]; room[g, xs] = False
    room[7, rest[:N]] = False
    for q in range(N):
        b = q * B + np.arange(CAP, L); stay[7, b] = False
        F[7, b] = np.append(rng.permutation(np.delete(rest, q))[:L - CAP - 1], rest[q])[:, None]
    room[6, xs, sl] = True; fixed = [(6, int(xs[i]), int(sl[i]), int(held[i]), -1) for i in range(N * CAP)]
    H, hold = lodge(rng, room, stay, first, old, fixed)
    return pack(F, U, M, A, H, hold)
def setup_inputs_calm(rng):
    F, U, A, M, room, stay, first, old = parts(rng); ce = -(-L // N)
    for g in range(4):
        po = [o * V + rng.permutation(V) for o in range(N)]
        for o in range(N):
            sp = po[o][:N * ce]; room[g, sp] = False; room[g, sp, rng.integers(0, 16, len(sp))] = True; first[g, sp] = 50.0
        for q in range(N):
            hm = np.sort(rng.permutation(B)[:L + (g + q) % 4]); stay[g, q * B:(q + 1) * B] = True; stay[g, q * B + hm] = False
            for j in range(L): F[g, q * B + hm[j]] = po[(j + q) % N][q * ce + j // N]
            for r in range(len(hm) - L):
                x, y = po[(q + 1) % N][N * ce + 2 * r], po[(q + 1) % N][N * ce + 2 * r + 1]; b = q * B + hm[L + r]
                room[g, x] = False; room[g, y] = False; F[g, b] = x; F[g, b, 0] = y; U[g, b] = 15
                A[g, x] = 1.0; A[g, y] = chain(1 + (r + q + g) % (RO - 2), int(rng.integers(-1, 2)))
    lo = np.resize(np.array([0, 2, L, 1, 3, L - 1]), N); hi = np.resize(np.array([1, 3, 0, 2, B - L, B - L - 1]), N); S = 8 * (B // L + 1)
    for g in (4, 5):
        pv = np.argsort(rng.random((N, V)), axis=1); turn = rng.permutation(N); stay[g] = True
        for q in range(N):
            n, m = (int(lo[turn[q]]), B - L) if g == 4 else (L, int(hi[turn[q]]))
            b = np.concatenate([rng.permutation(L)[:n], L + rng.permutation(B - L)[:m]]); o = b % N; i = (b + 4) % L
            x = o * V + pv[o, np.where(i < 8, 1 + S * q + 8 * ((b + 4) // L) + i, 0)]
            stay[g, q * B + b] = False; F[g, q * B + b] = x[:, None]; room[g, x] = False
    home = int(rng.integers(0, N)); pv = np.argsort(rng.random((N, V)), axis=1); i = np.arange(B)
    goods = (i % N) * V + pv[i % N, i // N]; held = home * B + rng.permutation(B); sl = rng.integers(0, 16, B)
    stay[6, home * B:(home + 1) * B] = False; room[6, goods] = False; room[6, goods, sl] = True
    fixed = [(6, int(goods[j]), int(sl[j]), int(held[j]), -1) for j in range(B)]
    for j in range(N - 1):
        q = (home + 1 + j) % N; w = goods[j * L:(j + 1) * L]
        stay[6, q * B:q * B + L] = False; F[6, q * B + np.arange(len(w))] = w[:, None]
    xy = rng.permutation(W)[:N * 48].reshape(N, 24, 2); stay[7] = True; room[7, xy.reshape(-1)] = False; first[7, xy.reshape(-1)] = 50.0
    for q in range(N):
        hm = q * B + rng.permutation(B)[:24]; stay[7, hm] = False
        for j in range(24):
            x, y = int(xy[q, j, 0]), int(xy[q, j, 1]); b = int(hm[j]); ux, uy, ax, ay, shut = pair(rng, j % 6)
            F[7, b] = y; F[7, b, 0] = x; U[7, b] = uy; U[7, b, 0] = ux; A[7, x] = ax; A[7, y] = ay
            room[7, y, int(rng.integers(0, 16))] = True
            if not shut: room[7, x, int(rng.integers(0, 16))] = True
    H, hold = lodge(rng, room, stay, first, old, fixed)
    return pack(F, U, M, A, H, hold)
def check_ranges(d):
    bad = []
    for k, lo, hi in (("ft", 0, W - 1), ("ut", 1, 15), ("mon", 0.25, 4.0), ("al", 0.125, 1.0), ("hn", -NB, NB + 1), ("hb", 0, W)):
        v = np.asarray(d[k]).astype(np.float64)
        if not np.all((v >= lo) & (v <= hi)): bad.append("range of " + k)
    u = np.asarray(d["ut"]).astype(np.float64)
    if not np.all(u == np.rint(u)): bad.append("ut isn't whole")
    if not bad:
        H = np.abs(by_good(np.asarray(d["hn"])).astype(np.int64)); hb = np.asarray(d["hb"]).astype(np.int64).transpose(1, 0, 2).reshape(8, NB)
        for g in range(8):
            held = (H[g] > 0) & (H[g] <= NB); names = H[g][held] - 1; hold = np.full(NB, W, np.int64); hold[names] = np.nonzero(held)[0]
            if np.any(np.bincount(names, minlength=NB) > 1) or np.any(hold != hb[g]): bad.append("hn and hb of market %d" % g)
    return bad
def reference(ft, ut, mon, al, hn, hb):
    F = by_good(ft).astype(np.int64); U = by_good(ut).astype(np.float32); M = by_good(mon).astype(np.float64)
    A = by_good(al).astype(np.float32); H = by_good(hn).astype(np.int64)
    hold = np.ascontiguousarray(hb.transpose(1, 0, 2)).astype(np.int64).reshape(8, NB)
    for t in range(RO):
        order = (np.arange(B) + t * L) % B
        for g in range(8):
            goods, who, best = [], [], []
            for q in range(N):
                o = q * B + order; o = o[hold[g, o] == W][:L]; j = np.arange(len(o))
                fk = F[g, o]; e = U[g, o][:, :, None] * A[g][fk]
                top = e == np.max(e, axis=1, keepdims=True)
                k = np.argmax(np.add.reduce(top.astype(np.int64), axis=2), axis=1)
                x = fk[j, k]; to = ((x // V)[:, None] == np.arange(N)).astype(np.int64)
                ok = np.add.reduce(to * (np.add.accumulate(to, axis=0) - to), axis=1) < CAP
                goods.append(x[ok]); who.append(o[ok]); best.append(top[j, k][ok])
            x, at = np.unique(np.concatenate(goods), return_index=True)
            b = np.concatenate(who)[at]; m = np.concatenate(best)[at]; h = H[g, x]
            grade = np.where(h == 0, 0, np.where(h < 0, 16, 32)) + np.arange(16)
            s = np.argmin(grade, axis=1); fits = np.min(grade, axis=1) < 32
            r = np.flatnonzero(fits); out = h[r, s[r]]
            hold[g, -out[out < 0] - 1] = W
            h[r, s[r]] = b[r] + 1; hold[g, b[r]] = x[r]
            r = np.flatnonzero(~fits); h[r] = np.where(h[r] <= NB, -h[r], h[r])
            H[g, x] = h
            A[g, x[r]] = np.where(m[r], A[g, x[r]] * np.float32(0.9375), A[g, x[r]])
    P = np.stack([np.where((hold[g] < W)[:, None], M[g] * A[g][np.minimum(hold[g], W - 1)].astype(np.float64), 0.0) for g in range(8)])
    return {"yal": by_rank(A), "yh": by_rank(H).astype(np.float32), "yp": by_rank(P).astype(np.float32)}

def check_inputs(d):
    bad = list(check_ranges(d))
    if not bad:
        for name, y in reference(**d).items():
            for q in range(N):
                v = np.abs(np.asarray(y[q], np.float64)); s = np.sqrt(np.mean(v * v))
                if v.max() > 9 * s or s < 2.0 ** -3: bad.append('%s of rank %d is uneven or too small' % (name, q))
    return bad

@@ -1,0 +1,674 @@
+import math
+from concourse.bass import DstId, RemoteDMATransfer
+from concourse.mybir import AluOpType as A, ActivationFunctionType as F
+
+N, V, W, RO, CAP = 6, 512, 3072, 4, 48
+WC = W // 16
+AW = W + 8
+S, P = "sbuf", "psum"
+f32, b16, f16, i32, u16 = "float32", "bfloat16", "float16", "int32", "uint16"
+_B = {
+    f32: dict(alpha=AW, qt=AW, ag=4096, sc=4096, colf=512, pf=24, rm=16, dl=16, dj=32, nm1=512, ta=512, tb=512,
+              tc=512, vv=512, ex=512, rem=WC, nh1=WC, fit=WC, aa=WC, nvd=WC, nvt=2 * WC, lk0=2 * WC, lk1=2 * WC, sw=WC, ab=256,
+              ms=256, s1=32, s2=32, s3=32, s4=32, nt=1536, ng=512, xw=1024, idf=128, hh=64, bq=64, hw2=64, cb=128, ps=32),
+    b16: dict(top=4096, utb=512, monb=512, blk=128, nblk=128, idb=128, tri=128, dm=128, kw=128, mp=128, t64=128,
+              t32=128, bvp=128, bvn=128, i4k=128, ipo=128, i64=128, i128=128, zz=144, pd=256, pv=256, l16=256, rs=256, keep=1024,
+              keep64=1024, pa=1024, ones=32, c48=256, pay=256, tab=AW + 256, ba=512, bb=512, bc=512, bd=512,
+              opp=512, hit=512, xb=256, wb=256, sg=256, oh=256, vs=264, eq=1024, es=1024, hw=32, rd=512, j16=256,
+              j64=256, xp=512),
+    f16: dict(blk16=128, z8=144, z16=144, ha=512, uh=256, fm=256, sf=256, th=64, gx=512, lo=32, vl=32),
+    i32: dict(fti=512, hni=512, hbi=512, pi=8, comb=512, lt=1024, ia=512, ib=512, fi=256, ui=256, yi=32, yc=32, yl=32),
+    u16: dict(offu=WC, fu=256, posw=32, colw=32, ku=16, xu=16, nu=32),
+}
+_B[b16]["tabc"] = W
+WIDTH = {n: c for d in _B for n, c in _B[d].items()}
+ALIAS = dict(yc=("yi", 32), yl=("yi", 64), xu=("ku", 16), lo=("th", 64), vl=("th", 96), dl=("dj", 32), j64=("j16", 256),
+             xp=("rd", 0), hbi=("ib", 0), ps=("dj", 48))
+SCRATCH = {n: (S, [128, max([c] + [o + WIDTH[a] for a, (m, o) in ALIAS.items() if m == n])], d)
+           for d in _B for n, c in _B[d].items() if n not in ALIAS}
+SCRATCH["selt"] = (S, [128, 16, 128], f16)
+SCRATCH["gd"] = (S, [128, 6, 128], b16)
+for _t in range(RO):
+    SCRATCH["fac%d" % _t] = (S, [128, 1544], b16)
+    SCRATCH["dn%d" % _t] = (S, [128, 6, 208], f16)
+for _t in range(8):
+    SCRATCH["p%d" % _t] = (P, [128, 512], f32)
+SEMAPHORES = (["cv", "ca", "cp", "cg", "sent", "a0", "q0", "a1", "a2", "a3", "q1", "q2", "q3", "gdr", "st0", "st1",
+               "st2"] + ["ld%d" % i for i in range(6)]
+              + ["%s%d" % (n, t) for t in range(RO) for n in ("fr", "dn", "df", "ar", "as", "tr", "nr", "lr", "ls")])
+SPLIT = True
+VOID, POIS, NONE = 16384.0, 32768.0, 4096.0
+LNR = math.log(1.8)
+
+
+def rank_program(g, core, T, topo):
+    me = T.rank_of(core)
+    if me is None:
+        return
+    cores = list(T.cores)
+    place = lambda c: (topo.host(c), topo.chip(c))
+    other = lambda q: [r for r in range(N) if place(cores[r]) != place(cores[q])]
+    same = lambda q: [r for r in range(N) if place(cores[r]) == place(cores[q]) and r != q]
+    far, mates = other(me), same(me)
+    near = sorted(mates + [me])
+    eng = {"v": g.vector, "a": g.scalar, "p": g.tensor, "g": g, "s": g.sync}
+    cnt = {"v": 0, "a": 0, "p": 0, "g": 0}
+    seen = {e: {} for e in eng}
+    acc = {}
+    total = {}
+
+    def X(n, lo=0, hi=None, st=1):
+        if hi is None:
+            hi = WIDTH[n] if n in WIDTH else SCRATCH[n][1][1]
+        if n in ALIAS:
+            n, lo, hi = ALIAS[n][0], lo + ALIAS[n][1], hi + ALIAS[n][1]
+        return (T[n][:, lo:hi:st] if st > 1 else T[n][:, lo:hi], [(n, lo, hi)])
+
+    def R(n, ap, lo=0, hi=1 << 20):
+        return (ap, [(n, lo, hi)])
+
+    def IND(win, off):
+        return (win[0].indirect(off[0]), win[1], off[1])
+
+    def wait(e, sem, val):
+        if seen[e].get(sem, 0) < val:
+            eng[e].wait_ge(T.sem[sem], val)
+            seen[e][sem] = val
+
+    def order(e, reads, writes):
+        need = {}
+        for regs, wr in ((reads, False), (writes, True)):
+            for n, lo, hi in regs:
+                bank = SCRATCH[n][0] == P
+                for l2, h2, w2, e2, sem, val in acc.get(n, []):
+                    hit = l2 < hi and lo < h2 and (wr or w2)
+                    dep = (e != "p" and hit) if e2 == e else (bank or hit)
+                    if dep and val > need.get(sem, 0):
+                        need[sem] = val
+        for sem in sorted(need):
+            wait(e, sem, need[sem])
+
+    def note(e, reads, writes, sem, val):
+        for regs, wr in ((writes, True), (reads, False)):
+            for n, lo, hi in regs:
+                old = acc.get(n, [])
+                if wr and e != "d":
+                    old = [o for o in old if not (lo <= o[0] and o[1] <= hi)]
+                old = [o for o in old if not (o[:5] == (lo, hi, wr, e, sem))]
+                acc[n] = old + [(lo, hi, wr, e, sem, val)]
+        total[sem] = max(total.get(sem, 0), val)
+
+    def op(e, fn, outs, ins):
+        reads, writes = [], []
+        for o in outs:
+            writes += o[1]
+            if len(o) > 2:
+                reads += o[2]
+        for i in ins:
+            if isinstance(i, tuple):
+                reads += i[1] + (i[2] if len(i) > 2 else [])
+        order(e, reads, writes)
+        cnt[e] += 1
+        fn().then_inc(T.sem["c" + e], 1)
+        note(e, reads, writes, "c" + e, cnt[e])
+
+    ap = lambda x: x[0] if isinstance(x, tuple) else x
+
+    def tt(o, a, b, f):
+        op("v", lambda: g.vector.tensor_tensor(o[0], a[0], b[0], f), [o], [a, b])
+
+    def ts(o, a, s1, f1, s2=None, f2=None):
+        if f2 is None:
+            op("v", lambda: g.vector.tensor_scalar(o[0], a[0], ap(s1), None, f1), [o], [a, s1])
+        else:
+            op("v", lambda: g.vector.tensor_scalar(o[0], a[0], ap(s1), ap(s2), f1, f2), [o], [a, s1, s2])
+
+    def cp(o, a):
+        op("v", lambda: g.vector.tensor_copy(o[0], a[0]), [o], [a])
+
+    def ms(o, c):
+        op("v", lambda: g.vector.memset(o[0], c), [o], [])
+
+    def scan(o, a, b, i, f0, f1):
+        op("v", lambda: g.vector.tensor_tensor_scan(o[0], a[0], b[0], ap(i), f0, f1), [o], [a, b, i])
+
+    consts = {}
+
+    def cb(c):
+        if c not in consts:
+            consts[c] = len(consts)
+            ms(X("cb", consts[c], consts[c] + 1), c)
+        return X("cb", consts[c], consts[c] + 1)
+
+    def act(o, a, f, bias=0.0, scale=1.0):
+        op("a", lambda: g.scalar.activation(o[0], a[0], f, bias=ap(bias), scale=ap(scale)), [o], [a, bias, scale])
+
+    def mm1(o, l, r, first, last):
+        op("p", lambda: g.tensor.matmul(o[0], l[0], r[0], first, last), [o], [l, r])
+
+    def mm(o, pairs, first=True, last=True):
+        for i, (l, r) in enumerate(pairs):
+            mm1(o, l, r, first and i == 0, last and i == len(pairs) - 1)
+
+    def iota(o, pat, base, cm):
+        if SCRATCH[o[1][0][0]][2] == i32:
+            op("g", lambda: g.iota(o[0], pat, base, cm), [o], [])
+        else:
+            op("g", lambda: g.iota(o[0], pat, base, cm, allow_small_or_imprecise_dtypes=True), [o], [])
+
+    def dma(e, sem, o, i):
+        reads = i[1] if isinstance(i, tuple) else []
+        writes = o[1] if isinstance(o, tuple) else []
+        order(e, reads, writes)
+        eng[e].dma_start(ap(o), ap(i)).then_inc(T.sem[sem], 16)
+        note("d", reads, writes, sem, total.get(sem, 0) + 16)
+
+    def pow2(n):
+        return 1 << (n.bit_length() - 1)
+
+    def share(q, n_near, n_far):
+        off = topo.engines(cores[q], cores[other(q)[0]]) if n_far else []
+        on = [k for k in topo.engines(cores[q], cores[same(q)[0]]) if k not in off] if n_near else []
+        return on, off
+
+    def nen(q, n_near, n_far):
+        on, off = share(q, n_near, n_far)
+        return (pow2(len(on) // n_near) if n_near else 0, pow2(len(off) // n_far) if n_far else 0)
+
+    def send(items, lsem):
+        inn = [i for i in items if i[1][0] in near]
+        out = [i for i in items if i[1][0] in far]
+        on, off = share(me, len(inn), len(out))
+        trs, reads, inc = [], [], 0
+        for its, es in ((out, off), (inn, on)):
+            for j, (x, qs, sem) in enumerate(its):
+                k = pow2(len(es) // len(its))
+                m = 0
+                for b in es[j * k:(j + 1) * k]:
+                    m |= 1 << b
+                ids = [DstId(rid=int(topo.addr(cores[q], core)[0]), pnc=int(topo.addr(cores[q], core)[1])) for q in qs]
+                trs.append(RemoteDMATransfer(dst_ids=ids, dma_engine_mask=m, remote_sem=T.sem[sem],
+                                             srcs=[x[0]], dsts=[x[0]] * len(qs)))
+                reads += x[1]
+                inc += k
+        order("g", reads, [])
+        g.remote_dma_fused(trs, local_sem=T.sem[lsem])
+        note("d", reads, [], lsem, total.get(lsem, 0) + inc)
+
+    def lands(regs, sem, val):
+        note("d", [], regs, sem, val)
+
+    def gather_all(piece, s_near, s_far):
+        send([(piece(me), mates, s_near)] + [(piece(me), [q], s_far) for q in far], "sent")
+        kn = sum(nen(q, 1, len(far))[0] for q in mates)
+        kf = sum(nen(q, 1, len(near))[1] for q in far)
+        if s_near == s_far:
+            kn = kf = kn + kf
+        lands(sum([piece(q)[1] for q in mates], []), s_near, kn)
+        lands(sum([piece(q)[1] for q in far], []), s_far, kf)
+
+    def big1(n, s):
+        k = V // len(far)
+        send([(X(n, V * me + k * j, V * me + k * j + k), [q], s + "1") for j, q in enumerate(far)], s + "0")
+        send([(X(n, V * me, V * me + V), mates, s + "2")], s + "0")
+        k, j = V // len(near), near.index(me)
+        lands(sum([X(n, V * q + k * j, V * q + k * j + k)[1] for q in far], []), s + "1",
+              sum(nen(q, 0, len(near))[1] for q in far))
+        lands(sum([X(n, V * q, V * q + V)[1] for q in mates], []), s + "2", sum(nen(q, 1, 0)[0] for q in mates))
+
+    def big2(n, s):
+        k, j = V // len(near), near.index(me)
+        send([(X(n, V * q + k * j, V * q + k * j + k), mates, s + "3") for q in far], s + "0")
+        acc[n] = [o[:5] + (total[s + "0"],) if o[4] == s + "0" else o for o in acc[n]]
+        regs = [X(n, V * q + k * near.index(m), V * q + k * near.index(m) + k)[1][0] for q in far for m in mates]
+        lands(regs, s + "3", sum(len(far) * nen(m, len(far), 0)[0] for m in mates))
+
+    selT = lambda k: R("selt", T["selt"][:, k, :], k, k + 1)
+
+    def wrap(o, src, n, z="zz"):
+        mm(o, [(X(z, 15 - r, 143 - r), X(src, r, n, 16)) for r in range(16)])
+
+    def unwrap(bank, rhs, first=True):
+        for r in range(16):
+            mm1(X(bank, r, 512, 16), selT(r), rhs, first, first or r == 15)
+
+    col1 = lambda n, c: X(n, c, c + 1)
+    own = lambda n: X(n, 32 * me, 32 * me + 32)
+    mine = lambda n: X(n, V * me, V * me + V)
+    h8 = lambda n, a=0, b=512, s=1: R(ALIAS.get(n, (n,))[0], T[ALIAS.get(n, (n,))[0]][0:8, a:b:s])
+
+    dma("s", "ld0", mine("alpha"), T.al[:])
+    dma("a", "ld1", X("hni"), T.hn[:])
+    dma("s", "ld2", h8("hbi"), T.hb[:])
+    dma("a", "ld3", X("fti"), T.ft[:])
+    dma("s", "ld4", X("utb"), T.ut[:])
+    dma("a", "ld5", X("monb"), T.mon[:])
+    iota(col1("pi", 0), [[0, 1]], 0, 1)
+    iota(X("colf"), [[1, 512]], 0, 0)
+    iota(X("ab", 0, 128), [[1, 8], [0, 16]], 0, 0)
+    big1("alpha", "a")
+    iota(X("xp"), [[0, 2], [1, 256]], 0, 0)
+    iota(X("lt"), [[0, 1024]], 4096 + W, 0)
+    iota(X("j16"), [[0, 16], [1, 16]], 0, 0)
+    iota(X("j64"), [[0, 4], [1, 64]], 0, 0)
+    big2("alpha", "a")
+    ms(X("alpha", W), 0.0)
+    ms(X("qt", W), 0.0)
+    ms(X("ones"), 1.0)
+    ms(X("keep"), 1.0)
+    for c in (NONE, 1.0, VOID, 256.0 * (V * me + 1) - 64, -31.0, -160.0, 64.0, 63.0, 33.0, 32.0, 128.0, 64.125, 2048.0,
+              1025.0 / 4096, 64 + 1.0 / 8192):
+        cb(c)
+    for n, c, w in (("tab", NONE, AW + 256), ("keep64", 1.0, 1024)):
+        for a in range(0, w, 1024):
+            b = min(w, a + 1024)
+            act(X(n, a, b), X("keep", 0, b - a), F.Identity, bias=cb(c), scale=0.0)
+    dma("s", "tr0", X("tabc"), X("tab", 0, W))
+    ms(X("c48"), float(CAP))
+    ms(X("vs"), 0.0)
+    for t in range(RO):
+        ms(X("fac%d" % t, 1536), 1.0)
+    ts(col1("pi", 1), col1("pi", 0), 15, A.bitwise_and)
+    ts(col1("pi", 2), col1("pi", 0), 4, A.arith_shift_right)
+    cp(X("pf", 0, 3), X("pi", 0, 3))
+    pp, rr, gg = col1("pf", 0), col1("pf", 1), col1("pf", 2)
+    ts(col1("pf", 3), gg, 16.0, A.mult, 15.0, A.add)
+    ts(col1("pf", 4), pp, 16.0, A.mult, 15.0, A.add)
+    ts(X("blk"), X("ab", 0, 128), gg, A.is_equal)
+    ts(X("idb"), X("colf", 0, 128), pp, A.is_equal)
+    ts(X("tri"), X("colf", 0, 128), pp, A.is_gt)
+    ts(X("zz"), X("colf", 0, 144), col1("pf", 3), A.is_equal)
+    ts(X("z8"), X("colf", 0, 144), col1("pf", 4), A.is_equal)
+    ts(X("rm"), X("colf", 0, 16), rr, A.is_equal)
+    tt(X("tri"), X("tri"), X("blk"), A.mult)
+    for n, c in (("i64", -64.0), ("t32", -32.0), ("mp", -1023.0), ("dm", 2.5), ("i4k", 4096.0), ("ipo", -POIS),
+                 ("i128", -128.0), ("idf", 1.0)):
+        act(X(n), X("idb"), F.Copy, scale=c)
+    for n, c in (("nblk", -1.0), ("bvp", VOID), ("bvn", -VOID)):
+        act(X(n), X("blk"), F.Copy, scale=c)
+    ts(h8("ha"), h8("hbi"), -1024.0, A.add)
+    mm(X("p5", 0, 32), [(h8("z8", 15 - r, 143 - r), h8("ha", r, 512, 16)) for r in range(16)])
+    ts(X("ba"), X("hni"), 0.0, A.is_equal)
+    ts(X("bb"), X("hni"), 0.0, A.is_lt)
+    tt(X("t64"), X("i64"), X("tri"), A.add)
+    tt(X("t32"), X("t32"), X("tri"), A.add)
+    ts(X("bc"), X("hni"), 3072.5, A.is_lt)
+    ts(X("bd"), X("hni"), 0.5, A.is_lt)
+    cp(X("ta"), X("hni"))
+    mm(X("p0"), [(X("t64"), X("ba"))])
+    mm(X("p1"), [(X("blk"), X("ba")), (X("t64"), X("bb"))])
+    mm(X("p2"), [(X("t32"), X("bc"))])
+    mm(X("p3"), [(X("t32"), X("bc")), (X("blk"), X("bd"))])
+    wrap(X("p4", 0, 32), "bd", 512)
+    wrap(X("p4", 32, 64), "bc", 512)
+    act(X("tc"), X("p0"), F.Copy)
+    act(X("tb"), X("p3"), F.Identity, bias=cb(-31.0))
+    act(X("ng"), X("ta"), F.Abs, scale=256.0)
+    act(X("ta"), X("ta"), F.Abs, scale=1.0 / 4096)
+    act(X("opp"), X("p2"), F.Identity, bias=cb(-160.0))
+    act(X("l16"), X("colf", 0, 256), F.Copy, scale=16.0)
+    act(X("pay"), X("colf", 0, 256), F.Copy)
+    act(X("nm1"), X("colf"), F.Identity, bias=cb(256.0 * (V * me + 1) - 64), scale=256.0)
+    act(X("xw", 256, 512), X("colf", 0, 256), F.Identity, bias=cb(VOID), scale=0.0)
+    act(X("xw", 512), X("colf"), F.Copy, scale=0.0)
+    ts(X("hh", 0, 32), X("p5", 0, 32), 1024.0, A.add)
+    ts(X("hw"), X("p5", 0, 32), 2048.0, A.is_equal)
+    cp(X("nu"), X("hh", 0, 32))
+    ts(col1("pf", 5), col1("rm", 0), 65536.0, A.mult)
+    ts(col1("pf", 8), col1("rm", 1), 65536.0, A.mult)
+    ts(col1("pf", 6), col1("rm", 1), 255.0, A.mult, 1.0, A.add)
+    ts(X("xp", 0, 256), X("xp", 0, 256), col1("pf", 5), A.mult)
+    ts(X("xp", 256), X("xp", 256), col1("pf", 5), A.mult, col1("pf", 8), A.add)
+    tt(X("mp"), X("mp"), X("tri"), A.add)
+    tt(X("mp"), X("mp"), X("blk"), A.subtract)
+    mm(X("p6"), [(X("idb"), X("xp")), (X("i4k"), X("utb"))])
+    ts(X("dj"), X("colf", 0, 32), 16.0, A.mult, rr, A.add)
+    ts(X("dl"), X("dj", 0, 16), float(AW), A.add)
+    ts(X("dj"), X("dj"), 512.0, A.add)
+    tt(X("p1"), X("p1"), X("tc"), A.min)
+    tt(X("p1"), X("p1"), X("tb"), A.min)
+    tt(mine("qt"), X("p1"), X("ng"), A.add)
+    big1("qt", "q")
+    tt(X("comb"), X("p6"), X("fti"), A.add)
+
+    def positions(t):
+        if t > 0:
+            wrap(X("p0", 0, 32), "hit", 512)
+            act(X("hw"), X("p0", 0, 32), F.Copy)
+        if t < RO:
+            mm(X("p7", 0, 32), [(X("blk"), X("hw"))])
+            mm(X("p7", 32, 64), [(X("mp"), X("hw"))])
+
+    def lanes(t):
+        if t % 2 == 0:
+            scan(X("s1"), X("ones"), X("p7", 0, 32), 1023.0, A.mult, A.add)
+        else:
+            scan(X("s1", 16, 32), X("ones", 0, 16), X("p7", 16, 32), 1023.0, A.mult, A.add)
+            scan(X("s1", 0, 16), X("ones", 0, 16), X("p7", 0, 16), col1("s1", 31), A.mult, A.add)
+        tt(X("s2"), X("p7", 32, 64), X("s1"), A.add)
+        tt(X("ps"), X("s2"), X("dj"), A.min)
+        cp(X("posw"), X("ps"))
+        cp(IND(X("lt"), X("posw")), X("comb"))
+        L = X("lt", 0, 256)
+        ts(X("fi"), L, 4095, A.bitwise_and)
+        cp(X("fu"), X("fi"))
+        ts(X("ui"), L, 12, A.arith_shift_right, 15, A.bitwise_and)
+        cp(X("uh"), X("ui"))
+
+    def lanes2():
+        L = X("lt", 0, 256)
+        ts(X("ia", 0, 256), L, 16, A.arith_shift_right)
+        ts(X("fm"), X("fi"), -1024.0, A.add)
+        ts(X("xb"), X("ia", 0, 256), col1("pf", 6), A.mult)
+        ms(L, 4096 + W)
+
+    positions(0)
+    for k in range(16):
+        ts(selT(k), X("blk"), col1("rm", k), A.mult)
+    tt(X("vv"), X("p1"), X("ta"), A.add)
+    act(X("ba"), X("p1"), F.Identity, bias=cb(64.0))
+    act(X("bb"), X("p1"), F.Abs, bias=cb(63.0))
+    mm(X("p2"), [(X("t32"), X("bc")), (X("blk"), X("bd")), (X("i64"), X("ba"))])
+    mm(X("p3"), [(X("t32"), X("bc")), (X("blk"), X("bd")), (X("i64"), X("bb"))])
+    act(X("ba"), X("p2"), F.Relu, bias=cb(33.0))
+    act(X("bb"), X("p3"), F.Relu, bias=cb(32.0))
+    wrap(X("p4", 64, 96), "ba", 512)
+    wrap(X("p4", 96, 128), "bb", 512)
+    gdp = lambda q: R("gd", T["gd"][:, q, :], q, q + 1)
+    act(gdp(me), X("p4", 0, 128), F.Copy)
+    gather_all(gdp, "gdr", "gdr")
+    big2("qt", "q")
+    lanes(0)
+    lanes2()
+    ms(X("keep", 0, 1024, 16), 0.0)
+    ms(X("keep64", 0, 1024, 64), 0.0)
+    ts(X("pd"), X("j16"), rr, A.not_equal, POIS, A.mult)
+    ts(X("pv"), X("pd"), VOID, A.add)
+    ts(X("rs"), X("j16"), 0.0, A.is_equal, 2.0 ** 20, A.mult)
+    for q in range(4):
+        ts(col1("pf", 16 + q), rr, 16.0 * q - 0.5, A.add)
+    for q in range(4):
+        ts(X("pa", 256 * q, 256 * q + 256), X("j64"), col1("pf", 16 + q), A.is_gt, POIS, A.mult)
+    tt(X("dm"), X("dm"), X("blk"), A.subtract)
+    ts(X("kw"), X("blk"), rr, A.mult, 0.5, A.mult)
+    cp(X("blk16"), X("blk"))
+    cp(X("z16"), X("zz"))
+    ts(col1("pf", 7), rr, -LNR, A.mult, -128 * LNR, A.add)
+    ts(col1("pf", 12), rr, 5.5, A.is_gt, 1.0e6, A.mult)
+    ts(col1("pf", 13), rr, -512.0, A.mult, 1024 - 255.5, A.add)
+    ts(col1("pf", 14), rr, -1.0, A.mult)
+    tt(col1("pf", 12), col1("pf", 12), col1("pf", 13), A.add)
+
+    def first_turns():
+        act(X("ta"), X("ta"), F.Abs)
+        act(X("ba"), X("ta"), F.Relu, bias=cb(128.0), scale=-1.0)
+        wrap(X("p5", 0, 32), "ba", 512)
+
+    def first_state():
+        gdv = lambda a: R("gd", T["gd"][:, :, a:a + 32])
+        cp(X("rem"), gdv(0))
+        ts(X("nh1"), gdv(32), 1.0, A.add)
+        ms(X("aa"), 1999.0)
+        ms(X("nvt", WC), 0.0)
+        cp(X("nvt", 0, WC), gdv(64))
+        ts(X("p6", 0, WC), X("rem"), 0.0, A.is_equal)
+        ts(X("fit"), X("rem"), 1.0, A.min, 2048.0, A.mult)
+        tt(X("p6", 0, WC), X("p6", 0, WC), X("nh1"), A.mult)
+        tt(X("p6", 0, WC), X("p6", 0, WC), gdv(96), A.add)
+        tt(X("nvd"), X("p6", 0, WC), X("nvt", 0, WC), A.subtract)
+
+    def names(t):
+        dn = "dn%d" % t
+        for b in range(3):
+            bank = ("p5", "p3" if t == RO - 1 else "p6", "p7")[b]
+            unwrap(bank, R(dn, T[dn][:, 2 * b:2 * b + 2, 192:208], 8 + 2 * b, 10 + 2 * b))
+            act(X("nt", 512 * b, 512 * b + 512), X(bank), F.Identity, bias=cb(1025.0 / 4096), scale=1.0 / 4096)
+
+    def slots(t):
+        lk = own("lk%d" % (t % 2))
+        ts(X("nu"), lk, -2048.0, A.add, 1535.0, A.min)
+        ts(X("s1"), own("aa"), -1.0, A.mult, 2000.0, A.add)
+        ts(X("s2"), lk, 2047.5, A.is_gt, -1.0, A.mult)
+        ts(X("s3"), lk, NONE - 0.5, A.is_lt)
+        tt(X("th", 32, 64), X("s1"), own("rem"), A.add)
+        tt(X("s2"), X("s2"), X("s1"), A.mult)
+        tt(X("th", 0, 32), X("s2"), X("s3"), A.mult)
+
+    def slots_name():
+        act(X("ng"), IND(X("nt"), X("nu")), F.Copy)
+
+    def slots_turn(bank):
+        mm1(X(bank), X("idf"), X("vv"), True, False)
+        unwrap(bank, X("th", 0, 32), False)
+        act(X("bd"), X(bank), F.Sign, bias=cb(64.125))
+
+    def slots_new():
+        mm(X("p6"), [(X("idf"), X("ng")), (X("idb"), X("opp")), (X("i128"), X("bd"))], True, False)
+        unwrap("p6", X("th", 32, 64), False)
+
+    def last_slots():
+        slots(RO - 1)
+        slots_name()
+        unwrap("p2", X("th", 0, 32), False)
+        act(X("bd"), X("p2"), F.Sign, bias=cb(64.125))
+        mm1(X("p6"), X("idb"), X("opp"), True, False)
+        for r in range(16):
+            mm1(X("p6", r, 512, 16), selT(r), X("th", 32, 64), False, False)
+        mm(X("p6"), [(X("idf"), X("ng")), (X("i128"), X("bd"))], False, True)
+
+    def cols(q):
+        chip = sorted(same(q) + [q])
+        return WC // len(chip) * chip.index(q), WC // len(chip) * (chip.index(q) + 1)
+
+    def goods(t, lo=0, hi=WC):
+        z = lambda n: X(n, lo, hi)
+        ts(z("p7"), z("lk%d" % (t % 2)), NONE - 0.5, A.is_lt)
+        tt(z("aa"), z("aa"), z("p7"), A.subtract)
+        if t == 0:
+            ts(z("sw"), z("nvd"), 1.0, A.add)
+            tt(z("sw"), z("p7"), z("sw"), A.mult)
+            tt(z("nvt"), z("nvt"), z("sw"), A.add)
+        tt(z("sw"), z("rem"), z("p7"), A.subtract)
+        ts(z("p7"), z("sw"), 0.0, A.is_lt)
+        tt(z("p7"), z("p7"), z("nh1"), A.mult)
+        tt(z("rem"), z("p7"), z("sw"), A.add)
+        if t < RO - 1:
+            ts(z("fit"), z("rem"), 1.0, A.min, 2048.0, A.mult)
+
+    for t in range(RO):
+        fac, dn = "fac%d" % t, "dn%d" % t
+        dnp = lambda q, a=0, b=WC: R(dn, T[dn][:, q, a:b], q + 8 * (a >= WC), q + 8 * (a >= WC) + 1)
+        if t > 0:
+            dma("s", "tr%d" % t, X("tab", 0, W), X("tabc"))
+        cuts = [0, 256] + [512 * c for c in range(1, 9)]
+        for a, b in zip(cuts[:-1], cuts[1:]):
+            act(X("ag", a, b), IND(X("alpha"), X("fu", a // 16, b // 16)), F.Copy)
+        for c in range(8):
+            bank = "p%d" % (c % 3)
+            unwrap(bank, X("uh", 32 * c, 32 * c + 32))
+            if c == 4:
+                wrap(X("p4", 0, 16), "xb", 256)
+            for a, b in ([(0, 256), (256, 512)] if c == 0 else [(0, 512)]):
+                e = X("ag", 512 * c + a, 512 * c + b)
+                tt(e, e, X(bank, a, b), A.mult)
+            if c == 0 and t > 0:
+                lanes2()
+            if c == 4:
+                ts(dnp(me, 192, 208), X("p4", 0, 16), V * me - 1024.0, A.add)
+                gather_all(lambda q: dnp(q, 192, 208), "nr%d" % t, "nr%d" % t)
+            if c % 2:
+                scan(X("sc", 512 * c - 512, 512 * c + 512), X("keep"), X("ag", 512 * c - 512, 512 * c + 512),
+                     0.0, A.mult, A.max)
+        act(X("p3", 0, 192), X("sc", 15, 3072, 16), F.Copy)
+        if t > 0:
+            names(t - 1)
+            if t < 3:
+                act(X("bc"), IND(X("nvt"), X("colw")), F.Copy)
+                mm(X("p5"), [(X("idb"), X("bc")), (X("i64"), X("rd"))])
+                act(X("bc"), X("p5"), F.Relu)
+                wrap(X("p7", 256, 288), "bc", 512)
+            slots_name()
+        cp(X("p3", 192, 256), X("sc", 3072 + 15, 4096, 16))
+        for k in range(16):
+            tk = R("top", T["top"][:, k:4096:16], k, k + 1)
+            tt(tk, X("ag", k, 4096, 16), X("p3", 0, 256), A.is_equal)
+            mm1(X("p4", 0, 256), X("zz", 15 - k, 143 - k), tk, k == 0, k == 15)
+        act(X("wb"), X("p4", 0, 256), F.Exp, bias=col1("pf", 7), scale=16 * LNR)
+        mm(X("p0", 0, 256), [(X("dm"), X("wb"))])
+        if t == 0:
+            tt(X("ta"), IND(X("qt"), X("nu")), X("nm1"), A.subtract)
+        for q in range(4):
+            if q % 2 == 0:
+                mm1(X("p%d" % (2 + q // 2)), X("idb"), X("pa", 256 * q, 256 * q + 512), True, False)
+        if t > 0:
+            if t < 3:
+                ts(X("s4"), X("p7", 256, 288), -1.0, A.mult, -48.0, A.add)
+            else:
+                ts(X("s4"), X("hw2", 0, 32), -10.0, A.mult, -48.0, A.add)
+            tt(X("hh", 32), X("hh", 32), X("s4"), A.min)
+        mm(X("p7", 0, 256), [(X("idb"), X("pd")), (X("idb"), X("l16"))], True, False)
+        ts(X("p1", 0, 256), X("p0", 0, 256), 0.0, A.is_gt)
+        act(X("sg"), X("p0", 0, 256), F.Sign)
+        tt(X("sf"), X("p1", 0, 256), X("fm"), A.mult)
+        mm(X("p4", 0, 256), [(X("blk16"), X("sf"))])
+        act(X("ab"), X("p4", 0, 256), F.Abs, bias=col1("pf", 12))
+        mm1(X("p7", 0, 256), X("kw"), X("sg"), False, True)
+        mm(X("p0", 0, 256), [(X("idb"), X("pv")), (X("blk16"), X("sf"))], True, False)
+        for q in range(4):
+            mm1(X("p%d" % (2 + q // 2), 256 * (q % 2), 256 * (q % 2) + 256), X("blk16"), X("sf"), False, q % 2 == 1)
+        scan(X("ex", 0, 256), X("rs"), X("p7", 0, 256), 0.0, A.add, A.min)
+        ts(X("oh"), X("ab"), 256.0, A.is_lt)
+        scan(X("vs", 1, 257), X("oh"), X("c48"), 0.0, A.add, A.min)
+        vpair = [(X("bvn"), X("vs", 1, 257)), (X("bvp"), X("vs", 0, 256))]
+        mm(X("p0", 0, 256), vpair, False, True)
+        mm(X("p1", 0, 256), [(X("blk16"), X("sf"))] + vpair)
+        ts(X("ku"), X("ex", 15, 256, 16), 60.0, A.add)
+        fp = lambda q: X(fac, 256 * q, 256 * q + 256)
+        act(fp(me), IND(X("top"), X("ku")), F.Identity, bias=cb(1.0), scale=-1.0 / 16)
+        wait("g", "a0", total["a0"])
+        gather_all(fp, "fr%d" % t, "fr%d" % t)
+        act(X("xw", 0, 256), X("p1", 0, 256), F.Identity, bias=cb(VOID))
+        act(X("gx"), IND(X("xw"), X("posw")), F.Copy)
+        if t > 0:
+            slots_turn("p5")
+        wrap(X("p1", 0, 32), "gx", 512, "z16")
+        if t == 0:
+            first_turns()
+        scan(X("ms"), X("rs"), X("p0", 0, 256), 0.0, A.add, A.min)
+        for c in range(16):
+            q, b = c % 4, c // 4
+            lo = 256 * (q % 2) + 64 * b
+            ts(X("eq", 64 * c, 64 * c + 64), X("p%d" % (2 + q // 2), lo, lo + 64), col1("ms", 16 * c + 15), A.is_equal)
+        scan(X("es"), X("keep64"), X("eq"), 0.0, A.mult, A.max)
+        ts(X("s1", 0, 16), X("es", 63, 1024, 64), VOID, A.mult, 1024.0, A.add)
+        tt(X("s2", 0, 16), X("s1", 0, 16), X("ms", 15, 256, 16), A.add)
+        tt(X("s3", 0, 16), X("s2", 0, 16), X("dl"), A.min)
+        cp(X("xu"), X("s3", 0, 16))
+        for b in (3, 2, 1, 0):
+            cp(IND(X("tab"), X("xu", 4 * b, 4 * b + 4)), X("pay", 64 * b, 64 * b + 64))
+        wrap(X("p4", 0, WC), "tab", W)
+        if t == 0:
+            ts(X("hh", 32), X("p5", 0, 32), -176.0, A.add)
+        ts(X("s1"), X("p1", 0, 32), 1.0 / 16, A.mult, 1024.0, A.add)
+        cp(X("hw2", 0, 32), X("hw"))
+        cp(X("hw2", 32), X("hw"))
+        ts(X("s2"), X("ps"), 256.0 * me, A.add)
+        ts(X("bq", 0, 32), X("s1"), float(W), A.min)
+        ts(X("s3"), X("s1"), 8192.0, A.is_gt, 8192.0, A.mult)
+        ts(X("s4"), X("hw"), -192.0, A.mult, 192.0, A.add)
+        tt(X("bq", 32), X("s2"), X("s3"), A.max)
+        tt(X("bq"), X("bq"), X("hh"), A.subtract)
+        tt(X("bq"), X("bq"), X("hw2"), A.mult)
+        tt(X("hh"), X("hh"), X("bq"), A.add)
+        cp(X("yi"), X("hh", 0, 32))
+        cp(X("vl"), X("hh", 32))
+        ts(X("yl"), X("yi"), 15, A.bitwise_and)
+        ts(X("yc"), X("yi"), 4, A.arith_shift_right)
+        cp(X("lo"), X("yl"))
+        ts(dnp(me, 0, WC), X("p4", 0, WC), 1.0 / 16, A.mult, 256.0 * me, A.add)
+        if SPLIT:
+            send([(dnp(me, *cols(q)), [q], "df%d" % t) for q in far], "sent")
+            send([(dnp(me, *cols(q)), [q], "dn%d" % t) for q in mates], "sent")
+            lands(sum([dnp(q)[1] for q in far], []), "df%d" % t, sum(len(near) and nen(q, 0, len(near))[1] for q in far))
+            lands(sum([dnp(q)[1] for q in mates], []), "dn%d" % t, sum(nen(q, len(mates), 0)[0] for q in mates))
+        else:
+            gather_all(dnp, "dn%d" % t, "df%d" % t)
+        tt(X("s4"), X("s4"), X("yc"), A.add)
+        cp(X("colw"), X("s4"))
+        unwrap("p0", X("lo"))
+        act(X("rd"), X("p0"), F.Abs, bias=col1("pf", 14))
+        mm1(X("p2"), X("ipo"), X("rd"), True, False)
+        unwrap("p2", X("vl"), False)
+        act(X("ex"), X("p2"), F.Relu, bias=cb(2048.0))
+        if t > 0:
+            slots_new()
+            goods(t - 1)
+        else:
+            first_state()
+        last = t == RO - 1
+        lk = "lk%d" % (t % 2)
+        if last:
+            names(t)
+        c0, c1 = cols(me) if SPLIT else (0, WC)
+        w = X("p1", c0, c1)
+        qs = near + far
+        tt(w, dnp(qs[0], c0, c1), dnp(qs[1], c0, c1), A.min)
+        for q in qs[2:]:
+            tt(w, w, dnp(q, c0, c1), A.min)
+        tt(X(lk, c0, c1), w, X("fit", c0, c1), A.add)
+        if SPLIT:
+            tt(X(lk, WC + c0, WC + c1), w, X("aa", c0, c1), A.max)
+            send([(X(lk, o + c0, o + c1), mates, "lr%d" % t) for o in (0, WC)], "ls%d" % t)
+            lands([(lk, o + cols(m)[0], o + cols(m)[1]) for m in mates for o in (0, WC)], "lr%d" % t,
+                  sum(2 * nen(m, 2, 0)[0] for m in mates))
+            h = (c1 - c0) * 8
+            shares = lambda q: ([(16 * cols(q)[0], h), (16 * cols(q)[0] + h, h)] if h > 512 else [(16 * cols(q)[0], 2 * h)])
+        else:
+            kf = V * len(far) // len(near)
+            shares = lambda q: [(V * far[0] + kf * near.index(q), kf), (V * q, V)]
+        ts(X("offu", c0, c1), X(lk, c0, c1), 1536.0, A.min)
+        for j, (lo, k) in enumerate(shares(me)):
+            piece = X("alpha", lo, lo + k)
+            tt(piece, IND(X(fac), X("offu", lo // 16, (lo + k) // 16)), piece, A.mult)
+            send([(piece, mates, "ar%d" % t)], "as%d" % t)
+            if last and j == 0:
+                tt(X("vv"), X("p6"), X("vv"), A.max)
+                mm1(X("p2"), X("idf"), X("vv"), True, False)
+            if j == (len(shares(me)) - 1 if SPLIT else 0):
+                if last:
+                    last_slots()
+                if not SPLIT:
+                    tt(X(lk, WC), w, X("aa"), A.max)
+                tt(X("hit"), IND(X(lk), X("colw")), X("ex"), A.is_lt)
+                positions(t + 1)
+                if 0 < t < RO - 1:
+                    tt(X("vv"), X("p6"), X("vv"), A.max)
+        acc["alpha"] = [o[:5] + (total[o[4]],) if o[4] == "as%d" % t else o for o in acc["alpha"]]
+        lands(sum([X("alpha", lo, lo + k)[1] for m in mates for lo, k in shares(m)], []), "ar%d" % t,
+              sum(len(shares(m)) * nen(m, 1, 0)[0] for m in mates))
+        if not last:
+            if SPLIT and t == 0:
+                slots(t)
+            lanes(t + 1)
+            if not SPLIT or t > 0:
+                slots(t)
+    t = RO - 1
+    dma("s", "st0", T.yal[:], mine("alpha"))
+    goods(t, 32 * me, 32 * me + 32)
+    ts(X("s1"), own("aa"), -1.0, A.mult, 1999.0 - 64, A.add)
+    tt(X("lo"), X("s1"), own("rem"), A.add)
+    unwrap("p2", X("lo"))
+    ts(X("s1"), X("hw"), float(W), A.mult)
+    tt(X("s2"), X("s1"), X("hh", 0, 32), A.max)
+    cp(X("colw"), X("s2"))
+    tt(X("vv"), X("p6"), X("vv"), A.max)
+    tt(X("tb"), X("vv"), X("p2"), A.is_lt)
+    act(X("p1"), X("tb"), F.Identity, bias=cb(1.0), scale=-2.0)
+    ts(X("ia"), X("vv"), 4096.0, A.mult)
+    ts(X("ib"), X("ia"), 4095, A.bitwise_and)
+    tt(X("tc"), X("p1"), X("ib"), A.mult)
+    dma("s", "st2", T.yh[:], X("tc"))
+    tt(X("ta"), IND(X("alpha"), X("colw")), X("monb"), A.mult)
+    dma("a", "st1", T.yp[:], X("ta"))
+    for sem in sorted(total):
+        wait("g", sem, total[sem])

@@ -5,25 +5,31 @@ from concourse.mybir import AluOpType as A, ActivationFunctionType as F
 N, V, W, RO, CAP = 6, 512, 3072, 4, 48
 WC = W // 16
 AW = W + 8
+LK = 4 * WC + 8
+NT = 1544
+EQ = 16 * 65
 S, P = "sbuf", "psum"
 f32, b16, f16, i32, u16 = "float32", "bfloat16", "float16", "int32", "uint16"
 _B = {
     f32: dict(alpha=AW, qt=AW, ag=4096, sc=4096, colf=512, pf=24, rm=16, dl=16, dj=32, nm1=512, ta=512, tb=512,
-              tc=512, vv=512, ex=512, rem=WC, nh1=WC, fit=WC, aa=WC, nvd=WC, nvt=2 * WC, lk0=2 * WC, lk1=2 * WC, sw=WC, ab=256,
-              ms=256, s1=32, s2=32, s3=32, s4=32, nt=1536, ng=512, xw=1024, idf=128, hh=64, bq=64, hw2=64, cb=128, ps=32),
+              tc=512, vv=512, ex=512, rem=WC, nh1=WC, fit=WC, nvd=WC, sw=WC, lk0=LK, lk1=LK, ab=256,
+              ms=256, s1=32, s2=32, s3=32, s4=32, nt=2 * NT, ng=512, xw=1024, tw=1024, idf=128, cb=128, ps=32, nb=16,
+              ks=256, zf=512),
     b16: dict(top=4096, utb=512, monb=512, blk=128, nblk=128, idb=128, tri=128, dm=128, kw=128, mp=128, t64=128,
-              t32=128, bvp=128, bvn=128, i4k=128, ipo=128, i64=128, i128=128, zz=144, pd=256, pv=256, l16=256, rs=256, keep=1024,
-              keep64=1024, pa=1024, ones=32, c48=256, pay=256, tab=AW + 256, ba=512, bb=512, bc=512, bd=512,
-              opp=512, hit=512, xb=256, wb=256, sg=256, oh=256, vs=264, eq=1024, es=1024, hw=32, rd=512, j16=256,
-              j64=256, xp=512),
-    f16: dict(blk16=128, z8=144, z16=144, ha=512, uh=256, fm=256, sf=256, th=64, gx=512, lo=32, vl=32),
-    i32: dict(fti=512, hni=512, hbi=512, pi=8, comb=512, lt=1024, ia=512, ib=512, fi=256, ui=256, yi=32, yc=32, yl=32),
-    u16: dict(offu=WC, fu=256, posw=32, colw=32, ku=16, xu=16, nu=32),
+              t32=128, bvp=128, bvn=128, i128=128, ipo=128, i64=128, n128=128, n256=128, n8k=128, d0=128, d1=128,
+              zz=144, zp=144, zn=144, pd=256, l16=256, rs=256, keep=1024, em=EQ, ones=512, c48=256, pay=256,
+              tab=AW + 256, ba=512, bb=512, bc=512, bd=512, opp=512, hit=512, xb=256, wb=256, sg=256, oh=256,
+              vs=264, eq=EQ, es=EQ, hw=32, rd=512, j16=256, xl=512, xh=512),
+    f16: dict(blk16=128, z8=144, z16=144, id16=128, ha=512, uh=256, fm=256, sf=256, th=64, gx=512, vl=512, lo=32,
+              lkf=128),
+    i32: dict(fti=512, hni=512, hbi=512, pi=8, comb=512, lt=1024, ltc=256, ia=512, ib=512, ui=256, yi=32, yc=32, yl=32),
+    u16: dict(offu=WC, fu=256, posw=32, colw=32, colx=32, gw=32, ku=16, xu=16, nu=32),
 }
 _B[b16]["tabc"] = W
 WIDTH = {n: c for d in _B for n, c in _B[d].items()}
-ALIAS = dict(yc=("yi", 32), yl=("yi", 64), xu=("ku", 16), lo=("th", 64), vl=("th", 96), dl=("dj", 32), j64=("j16", 256),
-             xp=("rd", 0), hbi=("ib", 0), ps=("dj", 48))
+ALIAS = dict(yc=("yi", 32), yl=("yi", 64), xu=("ku", 16), lo=("th", 64), dl=("dj", 32), hbi=("ib", 0), ps=("dj", 48),
+             colx=("colw", 32), gw=("colw", 64), nb=("dj", 80), d1=("d0", 128), n256=("n128", 128), n8k=("n128", 256),
+             xh=("xl", 512), s2=("s1", 32), s3=("s1", 64), s4=("s1", 96), zn=("zp", 144))
 SCRATCH = {n: (S, [128, max([c] + [o + WIDTH[a] for a, (m, o) in ALIAS.items() if m == n])], d)
            for d in _B for n, c in _B[d].items() if n not in ALIAS}
 SCRATCH["selt"] = (S, [128, 16, 128], f16)
@@ -33,22 +39,48 @@ for _t in range(RO):
     SCRATCH["dn%d" % _t] = (S, [128, 6, 208], f16)
 for _t in range(8):
     SCRATCH["p%d" % _t] = (P, [128, 512], f32)
-SEMAPHORES = (["cv", "ca", "cp", "cg", "sent", "a0", "q0", "a1", "a2", "a3", "q1", "q2", "q3", "gdr", "st0", "st1",
-               "st2"] + ["ld%d" % i for i in range(6)]
-              + ["%s%d" % (n, t) for t in range(RO) for n in ("fr", "dn", "df", "ar", "as", "tr", "nr", "lr", "ls")])
-SPLIT = True
-VOID, POIS, NONE = 16384.0, 32768.0, 4096.0
+RELAYED = ["qt", "gd"] + ["fac%d" % t for t in range(RO)]
+SEMAPHORES = (["cv", "ca", "cp", "cg", "sent", "a0", "a1", "a2", "a3", "st0", "st1", "st2", "lt", "tc"]
+              + ["ld%d" % i for i in range(6)] + [p + n for n in RELAYED for p in ("r", "h")]
+              + ["%s%d" % (n, t) for t in range(RO) for n in ("dn", "df", "ar", "as", "tr", "nr", "lr", "ls")])
+BIG, POIS, NONE = 4096.0, 32768.0, 4096.0
+LEAVE = 1901.0
 LNR = math.log(1.8)
 
 
 def rank_program(g, core, T, topo):
-    me = T.rank_of(core)
-    if me is None:
-        return
     cores = list(T.cores)
     place = lambda c: (topo.host(c), topo.chip(c))
     other = lambda q: [r for r in range(N) if place(cores[r]) != place(cores[q])]
     same = lambda q: [r for r in range(N) if place(cores[r]) == place(cores[q]) and r != q]
+    dst = lambda c: DstId(rid=int(topo.addr(c, core)[0]), pnc=int(topo.addr(c, core)[1]))
+
+    def helpers(q):
+        free = [c for c in topo.cores_of(cores[q]) if c not in cores]
+        return sorted(free, key=lambda c: topo.die(c) != topo.die(cores[q]))[:2]
+
+    def piece(n, q0, q1):
+        if n == "gd":
+            return (T[n][:, q0:q1, :], [(n, q0, q1)])
+        k = V if n == "qt" else 256
+        return (T[n][:, k * q0:k * q1], [(n, k * q0, k * q1)])
+
+    me = T.rank_of(core)
+    if me is None:
+        here = [q for q in range(N) if place(cores[q]) == place(core)]
+        if not here or core not in helpers(here[0]):
+            return
+        k = len(other(here[0])) // 2
+        q0 = other(here[0])[k * helpers(here[0]).index(core)]
+        mask = topo.mask(core, cores[here[0]])
+        for n in RELAYED:
+            g.wait_ge(T.sem["h" + n], sum(len(topo.engines(cores[q], core)) for q in range(q0, q0 + k)))
+            x = piece(n, q0, q0 + k)[0]
+            g.remote_dma_fused([RemoteDMATransfer(dst_ids=[dst(cores[q]) for q in here], dma_engine_mask=mask,
+                                                  remote_sem=T.sem["r" + n], srcs=[x], dsts=[x] * len(here))],
+                               local_sem=T.sem["sent"])
+        g.wait_ge(T.sem["sent"], len(RELAYED) * len(topo.engines(core, cores[here[0]])))
+        return
     far, mates = other(me), same(me)
     near = sorted(mates + [me])
     eng = {"v": g.vector, "a": g.scalar, "p": g.tensor, "g": g, "s": g.sync}
@@ -163,6 +195,9 @@ def rank_program(g, core, T, topo):
         eng[e].dma_start(ap(o), ap(i)).then_inc(T.sem[sem], 16)
         note("d", reads, writes, sem, total.get(sem, 0) + 16)
 
+    def settle(n, sem):
+        acc[n] = [o[:5] + (total[sem],) if o[4] == sem else o for o in acc[n]]
+
     def pow2(n):
         return 1 << (n.bit_length() - 1)
 
@@ -176,41 +211,44 @@ def rank_program(g, core, T, topo):
         return (pow2(len(on) // n_near) if n_near else 0, pow2(len(off) // n_far) if n_far else 0)
 
     def send(items, lsem):
-        inn = [i for i in items if i[1][0] in near]
-        out = [i for i in items if i[1][0] in far]
+        inn = [i for i in items if place(i[1][0]) == place(core)]
+        out = [i for i in items if place(i[1][0]) != place(core)]
         on, off = share(me, len(inn), len(out))
         trs, reads, inc = [], [], 0
         for its, es in ((out, off), (inn, on)):
-            for j, (x, qs, sem) in enumerate(its):
+            for j, (x, cs, sem) in enumerate(its):
                 k = pow2(len(es) // len(its))
                 m = 0
                 for b in es[j * k:(j + 1) * k]:
                     m |= 1 << b
-                ids = [DstId(rid=int(topo.addr(cores[q], core)[0]), pnc=int(topo.addr(cores[q], core)[1])) for q in qs]
-                trs.append(RemoteDMATransfer(dst_ids=ids, dma_engine_mask=m, remote_sem=T.sem[sem],
-                                             srcs=[x[0]], dsts=[x[0]] * len(qs)))
+                trs.append(RemoteDMATransfer(dst_ids=[dst(c) for c in cs], dma_engine_mask=m, remote_sem=T.sem[sem],
+                                             srcs=[x[0]], dsts=[x[0]] * len(cs)))
                 reads += x[1]
                 inc += k
         order("g", reads, [])
         g.remote_dma_fused(trs, local_sem=T.sem[lsem])
         note("d", reads, [], lsem, total.get(lsem, 0) + inc)
 
+    at = lambda qs: [cores[q] for q in qs]
+
     def lands(regs, sem, val):
         note("d", [], regs, sem, val)
 
-    def gather_all(piece, s_near, s_far):
-        send([(piece(me), mates, s_near)] + [(piece(me), [q], s_far) for q in far], "sent")
-        kn = sum(nen(q, 1, len(far))[0] for q in mates)
-        kf = sum(nen(q, 1, len(near))[1] for q in far)
-        if s_near == s_far:
-            kn = kf = kn + kf
-        lands(sum([piece(q)[1] for q in mates], []), s_near, kn)
-        lands(sum([piece(q)[1] for q in far], []), s_far, kf)
+    def gather_all(part, sem):
+        send([(part(me), at(mates), sem)] + [(part(me), at([q]), sem) for q in far], "sent")
+        k = sum(nen(q, 1, len(far))[0] for q in mates) + sum(nen(q, 1, len(near))[1] for q in far)
+        lands(sum([part(q)[1] for q in mates + far], []), sem, k)
+
+    def relay(n):
+        h = helpers(far[0])[near.index(me) // (len(near) // 2)]
+        send([(piece(n, me, me + 1), at(mates), "r" + n), (piece(n, me, me + 1), [h], "h" + n)], "sent")
+        k = sum(nen(q, 1, 1)[0] for q in mates) + sum(len(topo.engines(c, core)) for c in helpers(me))
+        lands(sum([piece(n, q, q + 1)[1] for q in mates + far], []), "r" + n, k)
 
     def big1(n, s):
         k = V // len(far)
-        send([(X(n, V * me + k * j, V * me + k * j + k), [q], s + "1") for j, q in enumerate(far)], s + "0")
-        send([(X(n, V * me, V * me + V), mates, s + "2")], s + "0")
+        send([(X(n, V * me + k * j, V * me + k * j + k), at([q]), s + "1") for j, q in enumerate(far)], s + "0")
+        send([(X(n, V * me, V * me + V), at(mates), s + "2")], s + "0")
         k, j = V // len(near), near.index(me)
         lands(sum([X(n, V * q + k * j, V * q + k * j + k)[1] for q in far], []), s + "1",
               sum(nen(q, 0, len(near))[1] for q in far))
@@ -218,56 +256,48 @@ def rank_program(g, core, T, topo):
 
     def big2(n, s):
         k, j = V // len(near), near.index(me)
-        send([(X(n, V * q + k * j, V * q + k * j + k), mates, s + "3") for q in far], s + "0")
-        acc[n] = [o[:5] + (total[s + "0"],) if o[4] == s + "0" else o for o in acc[n]]
+        send([(X(n, V * q + k * j, V * q + k * j + k), at(mates), s + "3") for q in far], s + "0")
+        settle(n, s + "0")
         regs = [X(n, V * q + k * near.index(m), V * q + k * near.index(m) + k)[1][0] for q in far for m in mates]
         lands(regs, s + "3", sum(len(far) * nen(m, len(far), 0)[0] for m in mates))
 
     selT = lambda k: R("selt", T["selt"][:, k, :], k, k + 1)
 
-    def wrap(o, src, n, z="zz"):
-        mm(o, [(X(z, 15 - r, 143 - r), X(src, r, n, 16)) for r in range(16)])
+    def wrap(o, src, lo, hi, z="zz", first=True, last=True):
+        mm(o, [(X(z, 15 - r, 143 - r), X(src, lo + r, hi, 16)) for r in range(16)], first, last)
 
-    def unwrap(bank, rhs, first=True):
+    def unwrap(bank, rhs, first=True, last=True, n=512):
         for r in range(16):
-            mm1(X(bank, r, 512, 16), selT(r), rhs, first, first or r == 15)
+            mm1(X(bank, r, n, 16), selT(r), rhs, first, first or (last and r == 15))
 
     col1 = lambda n, c: X(n, c, c + 1)
-    own = lambda n: X(n, 32 * me, 32 * me + 32)
     mine = lambda n: X(n, V * me, V * me + V)
     h8 = lambda n, a=0, b=512, s=1: R(ALIAS.get(n, (n,))[0], T[ALIAS.get(n, (n,))[0]][0:8, a:b:s])
 
     dma("s", "ld0", mine("alpha"), T.al[:])
-    dma("a", "ld1", X("hni"), T.hn[:])
-    dma("s", "ld2", h8("hbi"), T.hb[:])
-    dma("a", "ld3", X("fti"), T.ft[:])
-    dma("s", "ld4", X("utb"), T.ut[:])
+    dma("a", "ld2", h8("hbi"), T.hb[:])
+    dma("s", "ld1", X("hni"), T.hn[:])
+    dma("a", "ld4", X("utb"), T.ut[:])
+    dma("s", "ld3", X("fti"), T.ft[:])
     dma("a", "ld5", X("monb"), T.mon[:])
     iota(col1("pi", 0), [[0, 1]], 0, 1)
-    iota(X("colf"), [[1, 512]], 0, 0)
     iota(X("ab", 0, 128), [[1, 8], [0, 16]], 0, 0)
+    iota(X("colf"), [[1, 512]], 0, 0)
+    iota(X("ltc"), [[0, 256]], 4096 * W + 128, 0)
     big1("alpha", "a")
-    iota(X("xp"), [[0, 2], [1, 256]], 0, 0)
-    iota(X("lt"), [[0, 1024]], 4096 + W, 0)
+    iota(X("xl"), [[0, 8], [1, 64]], 0, 0)
+    iota(X("xh"), [[1, 8], [0, 64]], 0, 0)
+    iota(X("lt"), [[0, 1024]], 4096 * W + 128, 0)
     iota(X("j16"), [[0, 16], [1, 16]], 0, 0)
-    iota(X("j64"), [[0, 4], [1, 64]], 0, 0)
+    iota(X("es"), [[0, 4], [-16, 4], [1, 65]], -1, 0)
     big2("alpha", "a")
-    ms(X("alpha", W), 0.0)
-    ms(X("qt", W), 0.0)
     ms(X("ones"), 1.0)
-    ms(X("keep"), 1.0)
-    for c in (NONE, 1.0, VOID, 256.0 * (V * me + 1) - 64, -31.0, -160.0, 64.0, 63.0, 33.0, 32.0, 128.0, 64.125, 2048.0,
-              1025.0 / 4096, 64 + 1.0 / 8192):
+    for c in (NONE, 1.0, W - 1024.0, -31.0, -160.0, 64.0, 63.0, 33.0, 32.0):
         cb(c)
-    for n, c, w in (("tab", NONE, AW + 256), ("keep64", 1.0, 1024)):
-        for a in range(0, w, 1024):
-            b = min(w, a + 1024)
-            act(X(n, a, b), X("keep", 0, b - a), F.Identity, bias=cb(c), scale=0.0)
-    dma("s", "tr0", X("tabc"), X("tab", 0, W))
-    ms(X("c48"), float(CAP))
-    ms(X("vs"), 0.0)
-    for t in range(RO):
-        ms(X("fac%d" % t, 1536), 1.0)
+    act(col1("pf", 15), cb(1.0), F.Exp, scale=14.0)
+    for a in range(0, AW + 256, 512):
+        b = min(AW + 256, a + 512)
+        act(X("tab", a, b), X("ones", 0, b - a), F.Identity, bias=cb(NONE), scale=0.0)
     ts(col1("pi", 1), col1("pi", 0), 15, A.bitwise_and)
     ts(col1("pi", 2), col1("pi", 0), 4, A.arith_shift_right)
     cp(X("pf", 0, 3), X("pi", 0, 3))
@@ -275,73 +305,68 @@ def rank_program(g, core, T, topo):
     ts(col1("pf", 3), gg, 16.0, A.mult, 15.0, A.add)
     ts(col1("pf", 4), pp, 16.0, A.mult, 15.0, A.add)
     ts(X("blk"), X("ab", 0, 128), gg, A.is_equal)
+    ts(X("z8"), X("colf", 0, 144), col1("pf", 4), A.is_equal)
     ts(X("idb"), X("colf", 0, 128), pp, A.is_equal)
     ts(X("tri"), X("colf", 0, 128), pp, A.is_gt)
     ts(X("zz"), X("colf", 0, 144), col1("pf", 3), A.is_equal)
-    ts(X("z8"), X("colf", 0, 144), col1("pf", 4), A.is_equal)
     ts(X("rm"), X("colf", 0, 16), rr, A.is_equal)
     tt(X("tri"), X("tri"), X("blk"), A.mult)
-    for n, c in (("i64", -64.0), ("t32", -32.0), ("mp", -1023.0), ("dm", 2.5), ("i4k", 4096.0), ("ipo", -POIS),
-                 ("i128", -128.0), ("idf", 1.0)):
+    for n, c in (("i64", -64.0), ("t32", -32.0), ("mp", -1023.0), ("i128", 128.0), ("d0", col1("rm", 0)),
+                 ("d1", col1("rm", 1))):
         act(X(n), X("idb"), F.Copy, scale=c)
-    for n, c in (("nblk", -1.0), ("bvp", VOID), ("bvn", -VOID)):
-        act(X(n), X("blk"), F.Copy, scale=c)
     ts(h8("ha"), h8("hbi"), -1024.0, A.add)
-    mm(X("p5", 0, 32), [(h8("z8", 15 - r, 143 - r), h8("ha", r, 512, 16)) for r in range(16)])
     ts(X("ba"), X("hni"), 0.0, A.is_equal)
     ts(X("bb"), X("hni"), 0.0, A.is_lt)
     tt(X("t64"), X("i64"), X("tri"), A.add)
     tt(X("t32"), X("t32"), X("tri"), A.add)
     ts(X("bc"), X("hni"), 3072.5, A.is_lt)
     ts(X("bd"), X("hni"), 0.5, A.is_lt)
-    cp(X("ta"), X("hni"))
+    cp(X("ex"), X("hni"))
     mm(X("p0"), [(X("t64"), X("ba"))])
-    mm(X("p1"), [(X("blk"), X("ba")), (X("t64"), X("bb"))])
+    mm(X("p7"), [(X("blk"), X("ba")), (X("t64"), X("bb"))])
     mm(X("p2"), [(X("t32"), X("bc"))])
     mm(X("p3"), [(X("t32"), X("bc")), (X("blk"), X("bd"))])
-    wrap(X("p4", 0, 32), "bd", 512)
-    wrap(X("p4", 32, 64), "bc", 512)
     act(X("tc"), X("p0"), F.Copy)
     act(X("tb"), X("p3"), F.Identity, bias=cb(-31.0))
-    act(X("ng"), X("ta"), F.Abs, scale=256.0)
-    act(X("ta"), X("ta"), F.Abs, scale=1.0 / 4096)
+    act(X("ng"), X("ex"), F.Abs, scale=256.0)
+    act(X("ex"), X("ex"), F.Abs, scale=1.0 / 4096)
     act(X("opp"), X("p2"), F.Identity, bias=cb(-160.0))
-    act(X("l16"), X("colf", 0, 256), F.Copy, scale=16.0)
-    act(X("pay"), X("colf", 0, 256), F.Copy)
-    act(X("nm1"), X("colf"), F.Identity, bias=cb(256.0 * (V * me + 1) - 64), scale=256.0)
-    act(X("xw", 256, 512), X("colf", 0, 256), F.Identity, bias=cb(VOID), scale=0.0)
-    act(X("xw", 512), X("colf"), F.Copy, scale=0.0)
-    ts(X("hh", 0, 32), X("p5", 0, 32), 1024.0, A.add)
-    ts(X("hw"), X("p5", 0, 32), 2048.0, A.is_equal)
-    cp(X("nu"), X("hh", 0, 32))
-    ts(col1("pf", 5), col1("rm", 0), 65536.0, A.mult)
-    ts(col1("pf", 8), col1("rm", 1), 65536.0, A.mult)
-    ts(col1("pf", 6), col1("rm", 1), 255.0, A.mult, 1.0, A.add)
-    ts(X("xp", 0, 256), X("xp", 0, 256), col1("pf", 5), A.mult)
-    ts(X("xp", 256), X("xp", 256), col1("pf", 5), A.mult, col1("pf", 8), A.add)
+    mm(X("p5", 0, 32), [(h8("z8", 15 - r, 143 - r), h8("ha", r, 512, 16)) for r in range(16)])
+    mm(X("p1"), [(h8("z8", 15, 143), h8("ha"))], True, False)
+    for r in range(1, 16):
+        mm1(X("p1"), h8("z8", 15 - r, 143 - r), h8("ha"), False, r == 15)
     tt(X("mp"), X("mp"), X("tri"), A.add)
     tt(X("mp"), X("mp"), X("blk"), A.subtract)
-    mm(X("p6"), [(X("idb"), X("xp")), (X("i4k"), X("utb"))])
     ts(X("dj"), X("colf", 0, 32), 16.0, A.mult, rr, A.add)
-    ts(X("dl"), X("dj", 0, 16), float(AW), A.add)
+    ts(X("hw"), X("p5", 0, 32), 2048.0, A.is_equal)
+    ts(X("nu"), X("p5", 0, 32), 1024.0, A.add)
+    ts(X("dl"), X("dj", 0, 16), AW - 1024.0 - BIG, A.add)
     ts(X("dj"), X("dj"), 512.0, A.add)
-    tt(X("p1"), X("p1"), X("tc"), A.min)
-    tt(X("p1"), X("p1"), X("tb"), A.min)
-    tt(mine("qt"), X("p1"), X("ng"), A.add)
-    big1("qt", "q")
-    tt(X("comb"), X("p6"), X("fti"), A.add)
+    ts(X("ta"), X("fti"), 4096.0, A.mult)
+    wrap(X("p4", 0, 32), "bd", 0, 512)
+    wrap(X("p4", 32, 64), "bc", 0, 512)
+    mm(X("p6"), [(X("d0"), X("xl")), (X("d1"), X("xh")), (X("i128"), X("utb"))])
+    tt(X("p7"), X("p7"), X("tc"), A.min)
+    tt(X("p7"), X("p7"), X("tb"), A.min)
+    tt(mine("qt"), X("p7"), X("ng"), A.add)
+    relay("qt")
+    tt(X("vv"), X("p7"), X("ex"), A.add)
+    act(X("xw", 512), X("p1"), F.Identity, bias=cb(W - 1024.0), scale=-1.0)
+    act(X("ba"), X("p7"), F.Identity, bias=cb(64.0))
+    act(X("bb"), X("p7"), F.Abs, bias=cb(63.0))
+    for k in range(16):
+        act(selT(k), X("blk"), F.Copy, scale=col1("rm", k))
 
     def positions(t):
         if t > 0:
-            wrap(X("p0", 0, 32), "hit", 512)
+            wrap(X("p0", 0, 32), "hit", 0, 512)
             act(X("hw"), X("p0", 0, 32), F.Copy)
-        if t < RO:
-            mm(X("p7", 0, 32), [(X("blk"), X("hw"))])
-            mm(X("p7", 32, 64), [(X("mp"), X("hw"))])
+        mm(X("p7", 0, 32), [(X("blk"), X("hw"))])
+        mm(X("p7", 32, 64), [(X("mp"), X("hw"))])
 
     def lanes(t):
         if t % 2 == 0:
-            scan(X("s1"), X("ones"), X("p7", 0, 32), 1023.0, A.mult, A.add)
+            scan(X("s1"), X("ones", 0, 32), X("p7", 0, 32), 1023.0, A.mult, A.add)
         else:
             scan(X("s1", 16, 32), X("ones", 0, 16), X("p7", 16, 32), 1023.0, A.mult, A.add)
             scan(X("s1", 0, 16), X("ones", 0, 16), X("p7", 0, 16), col1("s1", 31), A.mult, A.add)
@@ -350,134 +375,128 @@ def rank_program(g, core, T, topo):
         cp(X("posw"), X("ps"))
         cp(IND(X("lt"), X("posw")), X("comb"))
         L = X("lt", 0, 256)
-        ts(X("fi"), L, 4095, A.bitwise_and)
-        cp(X("fu"), X("fi"))
-        ts(X("ui"), L, 12, A.arith_shift_right, 15, A.bitwise_and)
+        ts(X("fu"), L, 1.0 / 4096, A.mult)
+        ts(X("ui"), L, 7, A.arith_shift_right, 15, A.bitwise_and)
         cp(X("uh"), X("ui"))
-
-    def lanes2():
-        L = X("lt", 0, 256)
-        ts(X("ia", 0, 256), L, 16, A.arith_shift_right)
-        ts(X("fm"), X("fi"), -1024.0, A.add)
+        ts(X("ia", 0, 256), L, 63, A.bitwise_and)
+        ts(X("fm"), X("fu"), -1024.0, A.add)
         ts(X("xb"), X("ia", 0, 256), col1("pf", 6), A.mult)
-        ms(L, 4096 + W)
+        if t < RO - 1:
+            dma("s", "lt", L, X("ltc"))
 
     positions(0)
-    for k in range(16):
-        ts(selT(k), X("blk"), col1("rm", k), A.mult)
-    tt(X("vv"), X("p1"), X("ta"), A.add)
-    act(X("ba"), X("p1"), F.Identity, bias=cb(64.0))
-    act(X("bb"), X("p1"), F.Abs, bias=cb(63.0))
+    tt(X("comb"), X("p6"), X("ta"), A.add)
+    ts(col1("pf", 6), col1("rm", 1), 63.0, A.mult, 1.0, A.add)
     mm(X("p2"), [(X("t32"), X("bc")), (X("blk"), X("bd")), (X("i64"), X("ba"))])
     mm(X("p3"), [(X("t32"), X("bc")), (X("blk"), X("bd")), (X("i64"), X("bb"))])
     act(X("ba"), X("p2"), F.Relu, bias=cb(33.0))
     act(X("bb"), X("p3"), F.Relu, bias=cb(32.0))
-    wrap(X("p4", 64, 96), "ba", 512)
-    wrap(X("p4", 96, 128), "bb", 512)
-    gdp = lambda q: R("gd", T["gd"][:, q, :], q, q + 1)
-    act(gdp(me), X("p4", 0, 128), F.Copy)
-    gather_all(gdp, "gdr", "gdr")
-    big2("qt", "q")
+    wrap(X("p4", 64, 96), "ba", 0, 512)
+    wrap(X("p4", 96, 128), "bb", 0, 512)
+    act(piece("gd", me, me + 1), X("p4", 0, 128), F.Copy)
+    relay("gd")
     lanes(0)
-    lanes2()
+    dma("s", "tc", X("tabc"), X("tab", 0, W))
+    for c in (256.0 * (V * me + 1) - 64, 128.0, 64.125 - 2000, 63.125 - 2000, 1025.0 / 4096 - 100, 1025.0,
+              165 + 1.0 / 8192, LEAVE, -29.0, W - 1024.0 - BIG, -1024.0, 1024.0, 256.0 * me + 2048 - LEAVE):
+        cb(c)
+    for n, c, w in (("keep", 1.0, 1024), ("eq", BIG, EQ)):
+        for a in range(0, w, 512):
+            b = min(w, a + 512)
+            act(X(n, a, b), X("ones", 0, b - a), F.Identity, bias=cb(c), scale=0.0)
     ms(X("keep", 0, 1024, 16), 0.0)
-    ms(X("keep64", 0, 1024, 64), 0.0)
+    ms(X("alpha", W), 0.0)
+    ms(X("qt", W), 0.0)
+    ms(X("c48"), float(CAP))
+    ms(X("vs"), 0.0)
+    for t in range(RO):
+        ms(X("fac%d" % t, 1536), 1.0)
+    for n in ("lk0", "lk1"):
+        ms(X(n, 4 * WC), 0.0)
+    ms(X("nt", 0, 2 * NT, NT), -16384.0)
+    for a in (0, NT):
+        ms(X("nt", a + 1537, a + NT), -4096.0)
+    ts(X("em"), X("es"), rr, A.is_equal, -BIG, A.mult)
     ts(X("pd"), X("j16"), rr, A.not_equal, POIS, A.mult)
-    ts(X("pv"), X("pd"), VOID, A.add)
     ts(X("rs"), X("j16"), 0.0, A.is_equal, 2.0 ** 20, A.mult)
-    for q in range(4):
-        ts(col1("pf", 16 + q), rr, 16.0 * q - 0.5, A.add)
-    for q in range(4):
-        ts(X("pa", 256 * q, 256 * q + 256), X("j64"), col1("pf", 16 + q), A.is_gt, POIS, A.mult)
-    tt(X("dm"), X("dm"), X("blk"), A.subtract)
+    ms(X("em", 0, EQ, 65), 2.0 ** 20)
     ts(X("kw"), X("blk"), rr, A.mult, 0.5, A.mult)
-    cp(X("blk16"), X("blk"))
-    cp(X("z16"), X("zz"))
     ts(col1("pf", 7), rr, -LNR, A.mult, -128 * LNR, A.add)
-    ts(col1("pf", 12), rr, 5.5, A.is_gt, 1.0e6, A.mult)
+    ts(col1("pf", 12), rr, 5.5, A.is_gt, col1("pf", 15), A.mult)
     ts(col1("pf", 13), rr, -512.0, A.mult, 1024 - 255.5, A.add)
     ts(col1("pf", 14), rr, -1.0, A.mult)
     tt(col1("pf", 12), col1("pf", 12), col1("pf", 13), A.add)
 
-    def first_turns():
-        act(X("ta"), X("ta"), F.Abs)
-        act(X("ba"), X("ta"), F.Relu, bias=cb(128.0), scale=-1.0)
-        wrap(X("p5", 0, 32), "ba", 512)
-
-    def first_state():
-        gdv = lambda a: R("gd", T["gd"][:, :, a:a + 32])
-        cp(X("rem"), gdv(0))
-        ts(X("nh1"), gdv(32), 1.0, A.add)
-        ms(X("aa"), 1999.0)
-        ms(X("nvt", WC), 0.0)
-        cp(X("nvt", 0, WC), gdv(64))
-        ts(X("p6", 0, WC), X("rem"), 0.0, A.is_equal)
-        ts(X("fit"), X("rem"), 1.0, A.min, 2048.0, A.mult)
-        tt(X("p6", 0, WC), X("p6", 0, WC), X("nh1"), A.mult)
-        tt(X("p6", 0, WC), X("p6", 0, WC), gdv(96), A.add)
-        tt(X("nvd"), X("p6", 0, WC), X("nvt", 0, WC), A.subtract)
-
-    def names(t):
-        dn = "dn%d" % t
-        for b in range(3):
-            bank = ("p5", "p3" if t == RO - 1 else "p6", "p7")[b]
-            unwrap(bank, R(dn, T[dn][:, 2 * b:2 * b + 2, 192:208], 8 + 2 * b, 10 + 2 * b))
-            act(X("nt", 512 * b, 512 * b + 512), X(bank), F.Identity, bias=cb(1025.0 / 4096), scale=1.0 / 4096)
-
-    def slots(t):
-        lk = own("lk%d" % (t % 2))
-        ts(X("nu"), lk, -2048.0, A.add, 1535.0, A.min)
-        ts(X("s1"), own("aa"), -1.0, A.mult, 2000.0, A.add)
-        ts(X("s2"), lk, 2047.5, A.is_gt, -1.0, A.mult)
-        ts(X("s3"), lk, NONE - 0.5, A.is_lt)
-        tt(X("th", 32, 64), X("s1"), own("rem"), A.add)
-        tt(X("s2"), X("s2"), X("s1"), A.mult)
-        tt(X("th", 0, 32), X("s2"), X("s3"), A.mult)
-
-    def slots_name():
-        act(X("ng"), IND(X("nt"), X("nu")), F.Copy)
-
-    def slots_turn(bank):
-        mm1(X(bank), X("idf"), X("vv"), True, False)
-        unwrap(bank, X("th", 0, 32), False)
-        act(X("bd"), X(bank), F.Sign, bias=cb(64.125))
-
-    def slots_new():
-        mm(X("p6"), [(X("idf"), X("ng")), (X("idb"), X("opp")), (X("i128"), X("bd"))], True, False)
-        unwrap("p6", X("th", 32, 64), False)
-
-    def last_slots():
-        slots(RO - 1)
-        slots_name()
-        unwrap("p2", X("th", 0, 32), False)
-        act(X("bd"), X("p2"), F.Sign, bias=cb(64.125))
-        mm1(X("p6"), X("idb"), X("opp"), True, False)
-        for r in range(16):
-            mm1(X("p6", r, 512, 16), selT(r), X("th", 32, 64), False, False)
-        mm(X("p6"), [(X("idf"), X("ng")), (X("i128"), X("bd"))], False, True)
+    def late_constants():
+        for n, c in (("dm", 2.5), ("ipo", -POIS), ("n128", -128.0), ("n256", -256.0), ("n8k", -8192.0), ("idf", 1.0),
+                     ("id16", 1.0)):
+            act(X(n), X("idb"), F.Copy, scale=c)
+        for n, m, c in (("nblk", "blk", -1.0), ("bvp", "blk", BIG), ("bvn", "blk", -BIG), ("blk16", "blk", 1.0),
+                        ("z16", "zz", 1.0), ("zp", "zz", BIG), ("zn", "zz", -BIG)):
+            act(X(n), X(m), F.Copy, scale=c)
+        act(X("l16"), X("colf", 0, 256), F.Copy, scale=16.0)
+        act(X("pay"), X("colf", 0, 256), F.Copy)
+        act(X("nm1"), X("colf"), F.Identity, bias=cb(256.0 * (V * me + 1) - 64), scale=256.0)
+        act(X("xw", 256, 512), X("colf", 0, 256), F.Copy, scale=0.0)
+        act(X("tw", 0, 256), X("colf", 0, 256), F.Identity, bias=cb(256.0 * me + 2048 - LEAVE))
+        act(X("tw", 256, 512), X("colf", 0, 256), F.Copy, scale=0.0)
 
     def cols(q):
         chip = sorted(same(q) + [q])
         return WC // len(chip) * chip.index(q), WC // len(chip) * (chip.index(q) + 1)
 
-    def goods(t, lo=0, hi=WC):
-        z = lambda n: X(n, lo, hi)
-        ts(z("p7"), z("lk%d" % (t % 2)), NONE - 0.5, A.is_lt)
-        tt(z("aa"), z("aa"), z("p7"), A.subtract)
+    c0, c1 = cols(me)
+    z = lambda n: X(n, c0, c1)
+    lkt = lambda t, k: X("lk%d" % (t % 2), 4 * c0 + k, 4 * c1, 4)
+    ownk = lambda t, k: X("lk%d" % (t % 2), 128 * me + k, 128 * me + 128, 4)
+
+    def first_state():
+        gdv = lambda a: R("gd", T["gd"][:, :, a:a + 32])
+        cp(X("rem"), gdv(0))
+        ts(X("nh1"), gdv(32), 1.0, A.add)
+        cp(X("sw"), gdv(64))
+        cp(X("nvd"), gdv(96))
+        ts(z("p6"), z("rem"), 0.0, A.is_equal)
+        ts(z("fit"), z("rem"), 1.0, A.min, 2048.0, A.mult)
+        ts(lkt(0, 2), z("sw"), -1.0, A.mult, 99.0, A.add)
+        ts(lkt(0, 3), z("rem"), 101.0, A.add)
+        tt(z("p6"), z("p6"), z("nh1"), A.mult)
+        tt(z("p6"), z("p6"), z("nvd"), A.add)
+        tt(z("p6"), z("p6"), z("sw"), A.subtract)
+        ts(z("nvd"), z("p6"), 1.0, A.add)
+
+    def goods(t):
+        ts(z("p7"), lkt(t, 0), NONE - 0.5, A.is_lt)
+        tt(z("sw"), z("p7"), z("rem"), A.subtract)
         if t == 0:
-            ts(z("sw"), z("nvd"), 1.0, A.add)
-            tt(z("sw"), z("p7"), z("sw"), A.mult)
-            tt(z("nvt"), z("nvt"), z("sw"), A.add)
-        tt(z("sw"), z("rem"), z("p7"), A.subtract)
-        ts(z("p7"), z("sw"), 0.0, A.is_lt)
+            tt(z("nvd"), z("p7"), z("nvd"), A.mult)
+        else:
+            ms(lkt(t + 1, 2), 50.0)
+        ts(z("p7"), z("sw"), 0.0, A.is_gt)
+        if t == 0:
+            tt(lkt(1, 2), lkt(0, 2), z("nvd"), A.subtract)
         tt(z("p7"), z("p7"), z("nh1"), A.mult)
-        tt(z("rem"), z("p7"), z("sw"), A.add)
+        tt(z("rem"), z("p7"), z("sw"), A.subtract)
+        tt(lkt(t + 1, 3), z("p7"), lkt(t, 3), A.add)
+        ts(z("fit"), z("rem"), 1.0, A.min, 2048.0, A.mult)
+
+    def names(t, b, bank):
+        dn = "dn%d" % t
+        unwrap(bank, (T[dn][:, 2 * b:2 * b + 2, 192:208], [(dn, 256 * q + 192, 256 * q + 208) for q in (2 * b, 2 * b + 1)]))
         if t < RO - 1:
-            ts(z("fit"), z("rem"), 1.0, A.min, 2048.0, A.mult)
+            act(X("nt", 1 + 512 * b, 513 + 512 * b), X(bank), F.Identity, bias=cb(1025.0 / 4096 - 100), scale=1.0 / 4096)
+        else:
+            act(X("nt", NT + 1 + 512 * b, NT + 513 + 512 * b), X(bank), F.Identity, bias=cb(1025.0))
+
+    def turn(bank, rhs, o, bias):
+        mm1(X(bank), X("idf"), X("vv"), True, False)
+        unwrap(bank, rhs, False)
+        act(o, X(bank), F.Sign, bias=cb(bias))
 
     for t in range(RO):
-        fac, dn = "fac%d" % t, "dn%d" % t
-        dnp = lambda q, a=0, b=WC: R(dn, T[dn][:, q, a:b], q + 8 * (a >= WC), q + 8 * (a >= WC) + 1)
+        fac, dn, lk = "fac%d" % t, "dn%d" % t, "lk%d" % (t % 2)
+        last = t == RO - 1
+        dnp = lambda q, a=0, b=WC: R(dn, T[dn][:, q, a:b], 256 * q + a, 256 * q + b)
         if t > 0:
             dma("s", "tr%d" % t, X("tab", 0, W), X("tabc"))
         cuts = [0, 256] + [512 * c for c in range(1, 9)]
@@ -486,189 +505,186 @@ def rank_program(g, core, T, topo):
         for c in range(8):
             bank = "p%d" % (c % 3)
             unwrap(bank, X("uh", 32 * c, 32 * c + 32))
-            if c == 4:
-                wrap(X("p4", 0, 16), "xb", 256)
+            if c == 2:
+                wrap(X("p4", 0, 16), "xb", 0, 256)
             for a, b in ([(0, 256), (256, 512)] if c == 0 else [(0, 512)]):
                 e = X("ag", 512 * c + a, 512 * c + b)
                 tt(e, e, X(bank, a, b), A.mult)
-            if c == 0 and t > 0:
-                lanes2()
-            if c == 4:
+            if c == 2:
                 ts(dnp(me, 192, 208), X("p4", 0, 16), V * me - 1024.0, A.add)
-                gather_all(lambda q: dnp(q, 192, 208), "nr%d" % t, "nr%d" % t)
+                gather_all(lambda q: dnp(q, 192, 208), "nr%d" % t)
             if c % 2:
                 scan(X("sc", 512 * c - 512, 512 * c + 512), X("keep"), X("ag", 512 * c - 512, 512 * c + 512),
                      0.0, A.mult, A.max)
         act(X("p3", 0, 192), X("sc", 15, 3072, 16), F.Copy)
-        if t > 0:
-            names(t - 1)
-            if t < 3:
-                act(X("bc"), IND(X("nvt"), X("colw")), F.Copy)
-                mm(X("p5"), [(X("idb"), X("bc")), (X("i64"), X("rd"))])
-                act(X("bc"), X("p5"), F.Relu)
-                wrap(X("p7", 256, 288), "bc", 512)
-            slots_name()
+        if t == 0:
+            late_constants()
+            tt(X("dm"), X("dm"), X("blk"), A.subtract)
+        else:
+            for b in range(3):
+                names(t - 1, b, "p%d" % (5 + b))
+            act(X("ng"), IND(X("nt", 0, NT), X("nu")), F.Copy)
+            turn("p5", X("lkf", 1, 128, 4), X("bd"), 64.125 - 2000)
+            mm1(X("p6"), X("idb"), X("opp"), True, False)
+            unwrap("p6", X("lkf", 3, 128, 4), False, False)
+            act(X("bc"), IND(X("lk%d" % ((t - 1) % 2)), X("colx")), F.Copy)
         cp(X("p3", 192, 256), X("sc", 3072 + 15, 4096, 16))
         for k in range(16):
             tk = R("top", T["top"][:, k:4096:16], k, k + 1)
             tt(tk, X("ag", k, 4096, 16), X("p3", 0, 256), A.is_equal)
+            if k == (1 if t > 0 else 10):
+                mm(X("p7", 0, 256), [(X("idb"), X("pd")), (X("idb"), X("l16"))], True, False)
+                mm1(X("p1", 0, 256), X("idb"), X("pd"), True, False)
+            if last and k in (3, 7, 11):
+                names(t, k // 4, ("p0", "p2", "p0")[k // 4])
             mm1(X("p4", 0, 256), X("zz", 15 - k, 143 - k), tk, k == 0, k == 15)
         act(X("wb"), X("p4", 0, 256), F.Exp, bias=col1("pf", 7), scale=16 * LNR)
         mm(X("p0", 0, 256), [(X("dm"), X("wb"))])
-        if t == 0:
-            tt(X("ta"), IND(X("qt"), X("nu")), X("nm1"), A.subtract)
-        for q in range(4):
-            if q % 2 == 0:
-                mm1(X("p%d" % (2 + q // 2)), X("idb"), X("pa", 256 * q, 256 * q + 512), True, False)
-        if t > 0:
-            if t < 3:
-                ts(X("s4"), X("p7", 256, 288), -1.0, A.mult, -48.0, A.add)
-            else:
-                ts(X("s4"), X("hw2", 0, 32), -10.0, A.mult, -48.0, A.add)
-            tt(X("hh", 32), X("hh", 32), X("s4"), A.min)
-        mm(X("p7", 0, 256), [(X("idb"), X("pd")), (X("idb"), X("l16"))], True, False)
-        ts(X("p1", 0, 256), X("p0", 0, 256), 0.0, A.is_gt)
-        act(X("sg"), X("p0", 0, 256), F.Sign)
-        tt(X("sf"), X("p1", 0, 256), X("fm"), A.mult)
-        mm(X("p4", 0, 256), [(X("blk16"), X("sf"))])
-        act(X("ab"), X("p4", 0, 256), F.Abs, bias=col1("pf", 12))
+        mm(X("p5", 0, 256), [(X("dm"), X("wb"))])
+        ts(X("p3", 256), X("p0", 0, 256), 0.0, A.is_gt)
+        act(X("sg"), X("p5", 0, 256), F.Sign)
+        tt(X("sf"), X("p3", 256), X("fm"), A.mult)
         mm1(X("p7", 0, 256), X("kw"), X("sg"), False, True)
-        mm(X("p0", 0, 256), [(X("idb"), X("pv")), (X("blk16"), X("sf"))], True, False)
-        for q in range(4):
-            mm1(X("p%d" % (2 + q // 2), 256 * (q % 2), 256 * (q % 2) + 256), X("blk16"), X("sf"), False, q % 2 == 1)
-        scan(X("ex", 0, 256), X("rs"), X("p7", 0, 256), 0.0, A.add, A.min)
+        mm1(X("p1", 0, 256), X("blk16"), X("sf"), False, True)
+        mm(X("p2", 0, 256), [(X("blk16"), X("sf"))])
+        mm(X("p0", 256), [(X("blk16"), X("sf"))])
+        wrap(X("p3", 0, 16), "sf", 0, 256, "z16", True, False)
+        scan(X("ks"), X("rs"), X("p7", 0, 256), 0.0, A.add, A.min)
+        scan(X("ms"), X("rs"), X("p1", 0, 256), 0.0, A.add, A.min)
+        act(X("ab"), X("p2", 0, 256), F.Abs, bias=col1("pf", 12))
+        act(X("nb"), X("ms", 15, 256, 16), F.Copy, scale=-BIG)
+        ts(X("ku"), X("ks", 15, 256, 16), 60.0, A.add)
         ts(X("oh"), X("ab"), 256.0, A.is_lt)
         scan(X("vs", 1, 257), X("oh"), X("c48"), 0.0, A.add, A.min)
-        vpair = [(X("bvn"), X("vs", 1, 257)), (X("bvp"), X("vs", 0, 256))]
-        mm(X("p0", 0, 256), vpair, False, True)
-        mm(X("p1", 0, 256), [(X("blk16"), X("sf"))] + vpair)
-        ts(X("ku"), X("ex", 15, 256, 16), 60.0, A.add)
-        fp = lambda q: X(fac, 256 * q, 256 * q + 256)
-        act(fp(me), IND(X("top"), X("ku")), F.Identity, bias=cb(1.0), scale=-1.0 / 16)
-        wait("g", "a0", total["a0"])
-        gather_all(fp, "fr%d" % t, "fr%d" % t)
-        act(X("xw", 0, 256), X("p1", 0, 256), F.Identity, bias=cb(VOID))
-        act(X("gx"), IND(X("xw"), X("posw")), F.Copy)
-        if t > 0:
-            slots_turn("p5")
-        wrap(X("p1", 0, 32), "gx", 512, "z16")
-        if t == 0:
-            first_turns()
-        scan(X("ms"), X("rs"), X("p0", 0, 256), 0.0, A.add, A.min)
+        wrap(X("p3", 0, 16), "vs", 1, 257, "zn", False, False)
+        wrap(X("p3", 0, 16), "vs", 0, 256, "zp", False, True)
         for c in range(16):
-            q, b = c % 4, c // 4
-            lo = 256 * (q % 2) + 64 * b
-            ts(X("eq", 64 * c, 64 * c + 64), X("p%d" % (2 + q // 2), lo, lo + 64), col1("ms", 16 * c + 15), A.is_equal)
-        scan(X("es"), X("keep64"), X("eq"), 0.0, A.mult, A.max)
-        ts(X("s1", 0, 16), X("es", 63, 1024, 64), VOID, A.mult, 1024.0, A.add)
-        tt(X("s2", 0, 16), X("s1", 0, 16), X("ms", 15, 256, 16), A.add)
+            o, b = X("eq", 65 * c + 1, 65 * c + 65), 64 * (c // 4)
+            if c < 7:
+                ts(o, X("p0", 256 + b, 320 + b), col1("ms", 16 * c + 15), A.not_equal, BIG, A.mult)
+            else:
+                act(o, X("p2", b, b + 64), F.Abs, bias=col1("nb", c), scale=BIG)
+        act(piece(fac, me, me + 1), IND(X("top"), X("ku")), F.Identity, bias=cb(1.0), scale=-1.0 / 16)
+        if t == 0:
+            wait("g", "a0", total["a0"])
+        relay(fac)
+        mm(X("p2", 256), [(X("blk16"), X("sf")), (X("bvn"), X("vs", 1, 257)), (X("bvp"), X("vs", 0, 256))])
+        if t > 0:
+            mm(X("p6"), [(X("idf"), X("ng")), (X("n128"), X("bd"))], False, True)
+        act(X("xw", 0, 256), X("p2", 256), F.Relu, bias=cb(W - 1024.0 - BIG), scale=-1.0)
+        act(X("gx"), IND(X("xw"), X("posw")), F.Identity, bias=cb(-1024.0))
+        scan(X("es"), X("em"), X("eq"), 0.0, A.add, A.min)
+        tt(X("s2", 0, 16), X("p3", 0, 16), X("es", 64, EQ, 65), A.subtract)
         tt(X("s3", 0, 16), X("s2", 0, 16), X("dl"), A.min)
-        cp(X("xu"), X("s3", 0, 16))
+        ts(X("xu"), X("s3", 0, 16), 1024.0 + BIG, A.add)
         for b in (3, 2, 1, 0):
             cp(IND(X("tab"), X("xu", 4 * b, 4 * b + 4)), X("pay", 64 * b, 64 * b + 64))
-        wrap(X("p4", 0, WC), "tab", W)
+        H, Q = WC // 2, WC // 4
+        halves = [X("p4", 0, H), X("p1", 0, H)]
+        for hf in range(2):
+            wrap(halves[hf], "tab", 16 * H * hf, 16 * H * (hf + 1))
         if t == 0:
-            ts(X("hh", 32), X("p5", 0, 32), -176.0, A.add)
-        ts(X("s1"), X("p1", 0, 32), 1.0 / 16, A.mult, 1024.0, A.add)
-        cp(X("hw2", 0, 32), X("hw"))
-        cp(X("hw2", 32), X("hw"))
-        ts(X("s2"), X("ps"), 256.0 * me, A.add)
-        ts(X("bq", 0, 32), X("s1"), float(W), A.min)
-        ts(X("s3"), X("s1"), 8192.0, A.is_gt, 8192.0, A.mult)
-        ts(X("s4"), X("hw"), -192.0, A.mult, 192.0, A.add)
-        tt(X("bq", 32), X("s2"), X("s3"), A.max)
-        tt(X("bq"), X("bq"), X("hh"), A.subtract)
-        tt(X("bq"), X("bq"), X("hw2"), A.mult)
-        tt(X("hh"), X("hh"), X("bq"), A.add)
-        cp(X("yi"), X("hh", 0, 32))
-        cp(X("vl"), X("hh", 32))
-        ts(X("yl"), X("yi"), 15, A.bitwise_and)
-        ts(X("yc"), X("yi"), 4, A.arith_shift_right)
-        cp(X("lo"), X("yl"))
-        ts(dnp(me, 0, WC), X("p4", 0, WC), 1.0 / 16, A.mult, 256.0 * me, A.add)
-        if SPLIT:
-            send([(dnp(me, *cols(q)), [q], "df%d" % t) for q in far], "sent")
-            send([(dnp(me, *cols(q)), [q], "dn%d" % t) for q in mates], "sent")
-            lands(sum([dnp(q)[1] for q in far], []), "df%d" % t, sum(len(near) and nen(q, 0, len(near))[1] for q in far))
-            lands(sum([dnp(q)[1] for q in mates], []), "dn%d" % t, sum(nen(q, len(mates), 0)[0] for q in mates))
+            tt(X("ta"), IND(X("qt"), X("nu")), X("nm1"), A.subtract)
+            act(X("ta"), X("ta"), F.Abs)
+            act(X("bc"), X("ta"), F.Relu, bias=cb(128.0), scale=-1.0)
         else:
-            gather_all(dnp, "dn%d" % t, "df%d" % t)
-        tt(X("s4"), X("s4"), X("yc"), A.add)
-        cp(X("colw"), X("s4"))
-        unwrap("p0", X("lo"))
-        act(X("rd"), X("p0"), F.Abs, bias=col1("pf", 14))
-        mm1(X("p2"), X("ipo"), X("rd"), True, False)
-        unwrap("p2", X("vl"), False)
-        act(X("ex"), X("p2"), F.Relu, bias=cb(2048.0))
+            tt(X("vv"), X("p6"), X("vv"), A.max)
+        wants = lambda q, hf: [a for a in range(cols(q)[0], cols(q)[1], Q) if a // H == hf]
+        engines = lambda q, hf: nen(q, sum(len(wants(m, hf)) for m in same(q)), sum(len(wants(m, hf)) for m in other(q)))
+        for hf in range(2):
+            ts(dnp(me, H * hf, H * hf + H), halves[hf], 1.0 / 16, A.mult, 256.0 * me, A.add)
+            send([(dnp(me, a, a + Q), at([q]), ("df%d" if q in far else "dn%d") % t)
+                  for q in far + mates for a in wants(q, hf)], "sent")
+        for qs, sem, side in ((far, "df%d" % t, 1), (mates, "dn%d" % t, 0)):
+            lands(sum([dnp(q)[1] for q in qs], []), sem,
+                  sum(len(wants(me, hf)) * engines(q, hf)[side] for q in qs for hf in range(2)))
+        wrap(X("p0", 0, 32), "gx", 0, 512, "z16")
         if t > 0:
-            slots_new()
-            goods(t - 1)
-        else:
-            first_state()
-        last = t == RO - 1
-        lk = "lk%d" % (t % 2)
+            mm(X("p7"), [(X("idb"), X("bc")), (X("n256"), X("rd"))])
+            act(X("bc"), X("p7"), F.Relu)
         if last:
-            names(t)
-        c0, c1 = cols(me) if SPLIT else (0, WC)
-        w = X("p1", c0, c1)
+            turn("p3", X("lkf", 1, 128, 4), X("bd"), 63.125 - 2000)
+            ts(X("ia"), X("vv"), 4096.0, A.mult)
+        mm(X("p5"), [(X("blk"), X("bc"))])
+        ts(X("yi"), X("p0", 0, 32), -1.0 / 16, A.mult, W - 1024.0, A.add)
+        ts(X("yl"), X("yi"), 15, A.bitwise_and)
+        ts(X("yc"), X("yi"), 2, A.arith_shift_right, 4092, A.bitwise_and)
+        cp(X("lo"), X("yl"))
+        tt(X("s4"), X("yc"), X("hw"), A.subtract)
+        unwrap("p0", X("lo"))
+        ts(X("colw"), X("s4"), 1.0, A.add)
+        if not last:
+            ts(X("colx"), X("s4"), 3.0, A.add)
+        if t == 0:
+            act(X("tw", 512), X("p5"), F.Identity, bias=cb(-29.0))
+            first_state()
+        else:
+            goods(t - 1)
+            tt(X("tw", 512), X("p5"), X("vl"), A.min)
+        act(X("rd"), X("p0"), F.Abs, bias=col1("pf", 14))
+        act(X("vl"), IND(X("tw"), X("posw")), F.Copy)
+        mm(X("p2"), [(X("ipo"), X("rd")), (X("id16"), X("vl"))])
+        act(X("ex"), X("p2"), F.Relu, bias=cb(LEAVE))
+        if not last:
+            act(X("xw", 512), X("gx"), F.Identity, bias=cb(1024.0))
+        else:
+            nh = R("gd", T["gd"][:, me, 32:64], me, me + 1)
+            tt(X("s1"), ownk(t - 1, 1), ownk(t - 1, 3), A.add)
+            ts(X("s4"), nh, 1.0, A.add)
+            ts(X("s2"), X("s1"), 2100.5, A.is_lt)
+            cp(X("gw"), X("yi"))
+            tt(X("s2"), X("s2"), X("s4"), A.mult)
+            tt(X("s1"), X("s1"), X("s2"), A.add)
+            ts(X("s2"), X("s1"), 2101.5, A.is_lt)
+            ts(X("th", 32, 64), X("s2"), 32768.0, A.mult, -8192.0, A.add)
+            tt(X("s2"), X("s2"), X("s4"), A.mult)
+            tt(X("s1"), X("s1"), X("s2"), A.add)
+            tt(X("th", 0, 32), ownk(t - 1, 1), X("s1"), A.subtract)
+            turn("p6", X("th", 0, 32), X("p4"), 165 + 1.0 / 8192)
+            mm1(X("p3"), X("n8k"), X("bd"), True, False)
+            unwrap("p3", X("th", 32, 64), False)
+            ts(X("ib"), X("ia"), 4095, A.bitwise_and)
+        w = z("p1")
         qs = near + far
         tt(w, dnp(qs[0], c0, c1), dnp(qs[1], c0, c1), A.min)
         for q in qs[2:]:
             tt(w, w, dnp(q, c0, c1), A.min)
-        tt(X(lk, c0, c1), w, X("fit", c0, c1), A.add)
-        if SPLIT:
-            tt(X(lk, WC + c0, WC + c1), w, X("aa", c0, c1), A.max)
-            send([(X(lk, o + c0, o + c1), mates, "lr%d" % t) for o in (0, WC)], "ls%d" % t)
-            lands([(lk, o + cols(m)[0], o + cols(m)[1]) for m in mates for o in (0, WC)], "lr%d" % t,
-                  sum(2 * nen(m, 2, 0)[0] for m in mates))
-            h = (c1 - c0) * 8
-            shares = lambda q: ([(16 * cols(q)[0], h), (16 * cols(q)[0] + h, h)] if h > 512 else [(16 * cols(q)[0], 2 * h)])
+        ts(z("p7"), w, NONE - 0.5, A.is_lt)
+        tt(lkt(t, 0), w, z("fit"), A.add)
+        if t == 0:
+            ts(lkt(t, 1), z("p7"), -1.0, A.mult, 2000.0, A.add)
         else:
-            kf = V * len(far) // len(near)
-            shares = lambda q: [(V * far[0] + kf * near.index(q), kf), (V * q, V)]
-        ts(X("offu", c0, c1), X(lk, c0, c1), 1536.0, A.min)
+            tt(lkt(t, 1), lkt(t - 1, 1), z("p7"), A.subtract)
+        send([(X(lk, 4 * c0, 4 * c1), at(mates), "lr%d" % t)], "ls%d" % t)
+        lands([(lk, 4 * cols(m)[0], 4 * cols(m)[1]) for m in mates], "lr%d" % t, sum(nen(m, 1, 0)[0] for m in mates))
+        h = (c1 - c0) * 8
+        shares = lambda q: ([(16 * cols(q)[0], h), (16 * cols(q)[0] + h, h)] if h > 512 else [(16 * cols(q)[0], 2 * h)])
+        ts(X("offu", c0, c1), lkt(t, 0), 1536.0, A.min)
         for j, (lo, k) in enumerate(shares(me)):
-            piece = X("alpha", lo, lo + k)
-            tt(piece, IND(X(fac), X("offu", lo // 16, (lo + k) // 16)), piece, A.mult)
-            send([(piece, mates, "ar%d" % t)], "as%d" % t)
-            if last and j == 0:
-                tt(X("vv"), X("p6"), X("vv"), A.max)
-                mm1(X("p2"), X("idf"), X("vv"), True, False)
-            if j == (len(shares(me)) - 1 if SPLIT else 0):
-                if last:
-                    last_slots()
-                if not SPLIT:
-                    tt(X(lk, WC), w, X("aa"), A.max)
-                tt(X("hit"), IND(X(lk), X("colw")), X("ex"), A.is_lt)
-                positions(t + 1)
-                if 0 < t < RO - 1:
-                    tt(X("vv"), X("p6"), X("vv"), A.max)
-        acc["alpha"] = [o[:5] + (total[o[4]],) if o[4] == "as%d" % t else o for o in acc["alpha"]]
+            part = X("alpha", lo, lo + k)
+            tt(part, IND(X(fac), X("offu", lo // 16, (lo + k) // 16)), part, A.mult)
+            send([(part, at(mates), "ar%d" % t)], "as%d" % t)
+        settle("alpha", "as%d" % t)
         lands(sum([X("alpha", lo, lo + k)[1] for m in mates for lo, k in shares(m)], []), "ar%d" % t,
               sum(len(shares(m)) * nen(m, 1, 0)[0] for m in mates))
+        if last:
+            tt(X("tc"), X("p4"), X("ib"), A.mult)
+            act(X("tb"), X("tc"), F.Identity, bias=cb(BIG), scale=-1.0)
+            act(X("p0"), X("tc"), F.Copy)
+        tt(X("hit"), IND(X(lk), X("colw")), X("ex"), A.is_lt)
+        ts(X("nu"), ownk(t, 0), -2047.0, A.add, 1537.0, A.min)
         if not last:
-            if SPLIT and t == 0:
-                slots(t)
+            positions(t + 1)
+            cp(X("lkf"), X(lk, 128 * me, 128 * me + 128))
             lanes(t + 1)
-            if not SPLIT or t > 0:
-                slots(t)
-    t = RO - 1
-    dma("s", "st0", T.yal[:], mine("alpha"))
-    goods(t, 32 * me, 32 * me + 32)
-    ts(X("s1"), own("aa"), -1.0, A.mult, 1999.0 - 64, A.add)
-    tt(X("lo"), X("s1"), own("rem"), A.add)
-    unwrap("p2", X("lo"))
-    ts(X("s1"), X("hw"), float(W), A.mult)
-    tt(X("s2"), X("s1"), X("hh", 0, 32), A.max)
-    cp(X("colw"), X("s2"))
-    tt(X("vv"), X("p6"), X("vv"), A.max)
-    tt(X("tb"), X("vv"), X("p2"), A.is_lt)
-    act(X("p1"), X("tb"), F.Identity, bias=cb(1.0), scale=-2.0)
-    ts(X("ia"), X("vv"), 4096.0, A.mult)
-    ts(X("ib"), X("ia"), 4095, A.bitwise_and)
-    tt(X("tc"), X("p1"), X("ib"), A.mult)
+    mm(X("p2"), [(X("idb"), X("ones")), (X("nblk"), X("hit"))])
+    tt(X("zf"), X("p3"), X("tb"), A.min)
+    tt(X("ex"), X("p2"), X("monb"), A.mult)
+    tt(X("ng"), IND(X("nt", NT), X("nu")), X("zf"), A.add)
+    tt(X("tc"), X("p0"), X("ng"), A.max)
     dma("s", "st2", T.yh[:], X("tc"))
-    tt(X("ta"), IND(X("alpha"), X("colw")), X("monb"), A.mult)
-    dma("a", "st1", T.yp[:], X("ta"))
+    dma("a", "st0", T.yal[:], mine("alpha"))
+    tt(X("ta"), IND(X("alpha"), X("gw")), X("ex"), A.mult)
+    dma("s", "st1", T.yp[:], X("ta"))
     for sem in sorted(total):
         wait("g", sem, total[sem])

@@ -5,23 +5,23 @@ from concourse.mybir import AluOpType as A, ActivationFunctionType as F
 N, V, W, RO, CAP = 6, 512, 3072, 4, 48
 WC = W // 16
 AW = W + 8
-LK = 4 * WC + 8
+LK = 2 * WC + 8
 NT = 1544
 EQ = 16 * 65
 S, P = "sbuf", "psum"
 f32, b16, f16, i32, u16 = "float32", "bfloat16", "float16", "int32", "uint16"
 _B = {
     f32: dict(alpha=AW, qt=AW, ag=4096, sc=4096, colf=512, pf=24, rm=16, dl=16, dj=32, nm1=512, ta=512, tb=512,
-              tc=512, vv=512, ex=512, rem=WC, nh1=WC, fit=WC, nvd=WC, sw=WC, lk0=LK, lk1=LK, ab=256,
+              tc=512, vv=512, ex=512, rem=WC, nh1=WC, fit=WC, nvd=WC, sw=WC, lk0=2 * LK, lk1=2 * LK, ab=256,
               ms=256, s1=32, s2=32, s3=32, s4=32, nt=2 * NT, ng=512, xw=1024, tw=1024, idf=128, cb=128, ps=32, nb=16,
-              ks=256, zf=512),
+              ks=256, zf=512, aa=WC),
     b16: dict(top=4096, utb=512, monb=512, blk=128, nblk=128, idb=128, tri=128, dm=128, kw=128, mp=128, t64=128,
               t32=128, bvp=128, bvn=128, i128=128, ipo=128, i64=128, n128=128, n256=128, n8k=128, d0=128, d1=128,
               zz=144, zp=144, zn=144, pd=256, l16=256, rs=256, keep=1024, em=EQ, ones=512, c48=256, pay=256,
               tab=AW + 256, ba=512, bb=512, bc=512, bd=512, opp=512, hit=512, xb=256, wb=256, sg=256, oh=256,
               vs=264, eq=EQ, es=EQ, hw=32, rd=512, j16=256, xl=512, xh=512),
-    f16: dict(blk16=128, z8=144, z16=144, id16=128, ha=512, uh=256, fm=256, sf=256, th=64, gx=512, vl=512, lo=32,
-              lkf=128),
+    f16: dict(blk16=128, b8=128, z8=144, z16=144, id16=128, ha=512, uh=256, fm=256, sf=256, th=64, gx=512, vl=512, lo=32,
+              ao=32, lkn=32),
     i32: dict(fti=512, hni=512, hbi=512, pi=8, comb=512, lt=1024, ltc=256, ia=512, ib=512, ui=256, yi=32, yc=32, yl=32),
     u16: dict(offu=WC, fu=256, posw=32, colw=32, colx=32, gw=32, ku=16, xu=16, nu=32),
 }
@@ -29,7 +29,8 @@ _B[b16]["tabc"] = W
 WIDTH = {n: c for d in _B for n, c in _B[d].items()}
 ALIAS = dict(yc=("yi", 32), yl=("yi", 64), xu=("ku", 16), lo=("th", 64), dl=("dj", 32), hbi=("ib", 0), ps=("dj", 48),
              colx=("colw", 32), gw=("colw", 64), nb=("dj", 80), d1=("d0", 128), n256=("n128", 128), n8k=("n128", 256),
-             xh=("xl", 512), s2=("s1", 32), s3=("s1", 64), s4=("s1", 96), zn=("zp", 144))
+             xh=("xl", 512), s2=("s1", 32), s3=("s1", 64), s4=("s1", 96), zn=("zp", 144), ao=("th", 128),
+             lkn=("th", 96), aa=("rem", WC))
 SCRATCH = {n: (S, [128, max([c] + [o + WIDTH[a] for a, (m, o) in ALIAS.items() if m == n])], d)
            for d in _B for n, c in _B[d].items() if n not in ALIAS}
 SCRATCH["selt"] = (S, [128, 16, 128], f16)
@@ -40,12 +41,13 @@ for _t in range(RO):
 for _t in range(8):
     SCRATCH["p%d" % _t] = (P, [128, 512], f32)
 RELAYED = ["qt", "gd"] + ["fac%d" % t for t in range(RO)]
-SEMAPHORES = (["cv", "ca", "cp", "cg", "sent", "a0", "a1", "a2", "a3", "st0", "st1", "st2", "lt", "tc"]
+SEMAPHORES = (["cv", "ca", "cp", "cg", "sent", "a0", "a1", "a2", "a3", "a4", "ha", "st0", "st1", "st2", "lt", "tc"]
               + ["ld%d" % i for i in range(6)] + [p + n for n in RELAYED for p in ("r", "h")]
-              + ["%s%d" % (n, t) for t in range(RO) for n in ("dn", "df", "ar", "as", "tr", "nr", "lr", "ls")])
+              + ["%s%d" % (n, t) for t in range(RO) for n in ("dn", "df", "ar", "as", "tr", "nr", "lr", "lq", "ls")])
 BIG, POIS, NONE = 4096.0, 32768.0, 4096.0
 LEAVE = 1901.0
 LNR = math.log(1.8)
+VOTE, PICK = ("p4", "p5"), ("p0", "p1")
 
 
 def rank_program(g, core, T, topo):
@@ -65,6 +67,14 @@ def rank_program(g, core, T, topo):
         k = V if n == "qt" else 256
         return (T[n][:, k * q0:k * q1], [(n, k * q0, k * q1)])
 
+    def route(q, j):
+        chip, there = sorted(same(q) + [q]), other(q)
+        if len(chip) <= len(there) or topo.die(helpers(q)[0]) == topo.die(cores[q]):
+            return 0, there[j * len(there) // 4]
+        if j < 2:
+            return 0, there[j]
+        return (1, there[chip.index(q) // 2]) if j == 3 else (2, there[chip.index(q) % len(there)])
+
     me = T.rank_of(core)
     if me is None:
         here = [q for q in range(N) if place(cores[q]) == place(core)]
@@ -73,6 +83,17 @@ def rank_program(g, core, T, topo):
         k = len(other(here[0])) // 2
         q0 = other(here[0])[k * helpers(here[0]).index(core)]
         mask = topo.mask(core, cores[here[0]])
+        to = other(here[0])[helpers(here[0]).index(core)]
+        via = [q for q in here if route(q, 3) == (1, to)]
+        if via:
+            es = topo.engines(core, cores[to])
+            n = len(es) // len(via)
+            g.wait_ge(T.sem["ha"], len(via) * (len(topo.engines(core, cores[via[0]])) - len(es)))
+            g.remote_dma_fused([RemoteDMATransfer(
+                dst_ids=[dst(cores[to])], dma_engine_mask=sum(1 << e for e in es[n * j:n * j + n]), remote_sem=T.sem["a4"],
+                srcs=[T.alpha[:, V * q + 384:V * q + V]], dsts=[T.alpha[:, V * q + 384:V * q + V]])
+                for j, q in enumerate(via)], local_sem=T.sem["a0"])
+            g.wait_ge(T.sem["a0"], len(es))
         for n in RELAYED:
             g.wait_ge(T.sem["h" + n], sum(len(topo.engines(cores[q], core)) for q in range(q0, q0 + k)))
             x = piece(n, q0, q0 + k)[0]
@@ -210,10 +231,10 @@ def rank_program(g, core, T, topo):
         on, off = share(q, n_near, n_far)
         return (pow2(len(on) // n_near) if n_near else 0, pow2(len(off) // n_far) if n_far else 0)
 
-    def send(items, lsem):
+    def send(items, lsem, beside=False):
         inn = [i for i in items if place(i[1][0]) == place(core)]
         out = [i for i in items if place(i[1][0]) != place(core)]
-        on, off = share(me, len(inn), len(out))
+        on, off = share(me, len(inn), len(out) or beside)
         trs, reads, inc = [], [], 0
         for its, es in ((out, off), (inn, on)):
             for j, (x, cs, sem) in enumerate(its):
@@ -245,21 +266,33 @@ def rank_program(g, core, T, topo):
         k = sum(nen(q, 1, 1)[0] for q in mates) + sum(len(topo.engines(c, core)) for c in helpers(me))
         lands(sum([piece(n, q, q + 1)[1] for q in mates + far], []), "r" + n, k)
 
-    def big1(n, s):
-        k = V // len(far)
-        send([(X(n, V * me + k * j, V * me + k * j + k), at([q]), s + "1") for j, q in enumerate(far)], s + "0")
-        send([(X(n, V * me, V * me + V), at(mates), s + "2")], s + "0")
-        k, j = V // len(near), near.index(me)
-        lands(sum([X(n, V * q + k * j, V * q + k * j + k)[1] for q in far], []), s + "1",
-              sum(nen(q, 0, len(near))[1] for q in far))
-        lands(sum([X(n, V * q, V * q + V)[1] for q in mates], []), s + "2", sum(nen(q, 1, 0)[0] for q in mates))
+    quarter = lambda q, j: X("alpha", V * q + 128 * j, V * q + 128 * j + 128)
+    got = lambda r, way: [(q, j) for q in other(r) for j in range(4) if route(q, j) == (way, r)]
 
-    def big2(n, s):
-        k, j = V // len(near), near.index(me)
-        send([(X(n, V * q + k * j, V * q + k * j + k), at(mates), s + "3") for q in far], s + "0")
-        settle(n, s + "0")
-        regs = [X(n, V * q + k * near.index(m), V * q + k * near.index(m) + k)[1][0] for q in far for m in mates]
-        lands(regs, s + "3", sum(len(far) * nen(m, len(far), 0)[0] for m in mates))
+    def prices1():
+        ways = lambda q, way: [j for j in range(4) if route(q, j)[0] == way]
+        outs = lambda way, sem: [(quarter(me, j), at([route(me, j)[1]]), sem) for j in ways(me, way)]
+        via = [(quarter(me, j), [helpers(me)[far.index(route(me, j)[1])]], "ha") for j in ways(me, 1)]
+        send(outs(0, "a1") + via, "a0")
+        if via:
+            send(outs(2, "a4"), "a0")
+        send([(mine("alpha"), at(mates), "a2")], "a0", True)
+        lands(sum([quarter(q, j)[1] for q, j in got(me, 0)], []), "a1",
+              sum(nen(q, 0, len(ways(q, 0)))[1] for q, j in got(me, 0)))
+        if got(me, 1):
+            lands(sum([quarter(q, j)[1] for q, j in got(me, 1) + got(me, 2)], []), "a4",
+                  len(topo.engines(helpers(far[0])[0], core)) + sum(nen(q, 0, 1)[1] for q, j in got(me, 2)))
+        lands(sum([X("alpha", V * q, V * q + V)[1] for q in mates], []), "a2", sum(nen(q, 1, 1)[0] for q in mates))
+
+    def prices2():
+        k = 0
+        stage = lambda r, late: got(r, 1) + got(r, 2) if late else got(r, 0)
+        for late in range(2):
+            if stage(me, late):
+                send([(quarter(q, j), at(mates), "a3") for q, j in stage(me, late)], "a0")
+                k += sum(len(stage(m, late)) * nen(m, len(stage(m, late)), 0)[0] for m in mates)
+        settle("alpha", "a0")
+        lands([quarter(q, j)[1][0] for m in mates for late in range(2) for q, j in stage(m, late)], "a3", k)
 
     selT = lambda k: R("selt", T["selt"][:, k, :], k, k + 1)
 
@@ -284,13 +317,14 @@ def rank_program(g, core, T, topo):
     iota(X("ab", 0, 128), [[1, 8], [0, 16]], 0, 0)
     iota(X("colf"), [[1, 512]], 0, 0)
     iota(X("ltc"), [[0, 256]], 4096 * W + 128, 0)
-    big1("alpha", "a")
+    prices1()
     iota(X("xl"), [[0, 8], [1, 64]], 0, 0)
     iota(X("xh"), [[1, 8], [0, 64]], 0, 0)
     iota(X("lt"), [[0, 1024]], 4096 * W + 128, 0)
     iota(X("j16"), [[0, 16], [1, 16]], 0, 0)
+    prices2()
     iota(X("es"), [[0, 4], [-16, 4], [1, 65]], -1, 0)
-    big2("alpha", "a")
+    wait("g", "a3", total["a3"])
     ms(X("ones"), 1.0)
     for c in (NONE, 1.0, W - 1024.0, -31.0, -160.0, 64.0, 63.0, 33.0, 32.0):
         cb(c)
@@ -306,6 +340,7 @@ def rank_program(g, core, T, topo):
     ts(col1("pf", 4), pp, 16.0, A.mult, 15.0, A.add)
     ts(X("blk"), X("ab", 0, 128), gg, A.is_equal)
     ts(X("z8"), X("colf", 0, 144), col1("pf", 4), A.is_equal)
+    ts(X("b8"), X("ab", 0, 128), pp, A.is_equal)
     ts(X("idb"), X("colf", 0, 128), pp, A.is_equal)
     ts(X("tri"), X("colf", 0, 128), pp, A.is_gt)
     ts(X("zz"), X("colf", 0, 144), col1("pf", 3), A.is_equal)
@@ -317,6 +352,14 @@ def rank_program(g, core, T, topo):
     ts(h8("ha"), h8("hbi"), -1024.0, A.add)
     ts(X("ba"), X("hni"), 0.0, A.is_equal)
     ts(X("bb"), X("hni"), 0.0, A.is_lt)
+    for t in range(RO):
+        ms(X("fac%d" % t, 1536), 1.0)
+    for n in ("lk0", "lk1"):
+        for a in (LK, 2 * LK):
+            ms(X(n, a - 8, a), 0.0)
+    ms(X("nt", 0, 2 * NT, NT), -16384.0)
+    for a in (0, NT):
+        ms(X("nt", a + 1537, a + NT), -4096.0)
     tt(X("t64"), X("i64"), X("tri"), A.add)
     tt(X("t32"), X("t32"), X("tri"), A.add)
     ts(X("bc"), X("hni"), 3072.5, A.is_lt)
@@ -332,9 +375,7 @@ def rank_program(g, core, T, topo):
     act(X("ex"), X("ex"), F.Abs, scale=1.0 / 4096)
     act(X("opp"), X("p2"), F.Identity, bias=cb(-160.0))
     mm(X("p5", 0, 32), [(h8("z8", 15 - r, 143 - r), h8("ha", r, 512, 16)) for r in range(16)])
-    mm(X("p1"), [(h8("z8", 15, 143), h8("ha"))], True, False)
-    for r in range(1, 16):
-        mm1(X("p1"), h8("z8", 15 - r, 143 - r), h8("ha"), False, r == 15)
+    mm(X("p1"), [(h8("b8", 0, 128), h8("ha"))])
     tt(X("mp"), X("mp"), X("tri"), A.add)
     tt(X("mp"), X("mp"), X("blk"), A.subtract)
     ts(X("dj"), X("colf", 0, 32), 16.0, A.mult, rr, A.add)
@@ -352,10 +393,11 @@ def rank_program(g, core, T, topo):
     relay("qt")
     tt(X("vv"), X("p7"), X("ex"), A.add)
     act(X("xw", 512), X("p1"), F.Identity, bias=cb(W - 1024.0), scale=-1.0)
-    act(X("ba"), X("p7"), F.Identity, bias=cb(64.0))
-    act(X("bb"), X("p7"), F.Abs, bias=cb(63.0))
     for k in range(16):
         act(selT(k), X("blk"), F.Copy, scale=col1("rm", k))
+        if k == 7:
+            act(X("ba"), X("p7"), F.Identity, bias=cb(64.0))
+            act(X("bb"), X("p7"), F.Abs, bias=cb(63.0))
 
     def positions(t):
         if t > 0:
@@ -395,39 +437,41 @@ def rank_program(g, core, T, topo):
     wrap(X("p4", 96, 128), "bb", 0, 512)
     act(piece("gd", me, me + 1), X("p4", 0, 128), F.Copy)
     relay("gd")
-    lanes(0)
-    dma("s", "tc", X("tabc"), X("tab", 0, W))
-    for c in (256.0 * (V * me + 1) - 64, 128.0, 64.125 - 2000, 63.125 - 2000, 1025.0 / 4096 - 100, 1025.0,
-              165 + 1.0 / 8192, LEAVE, -29.0, W - 1024.0 - BIG, -1024.0, 1024.0, 256.0 * me + 2048 - LEAVE):
+    for c in (64.125 - 2000, 63.125 - 2000, 1025.0 / 4096 - 100, 1025.0, 165 + 1.0 / 8192, BIG + 1024):
         cb(c)
-    for n, c, w in (("keep", 1.0, 1024), ("eq", BIG, EQ)):
-        for a in range(0, w, 512):
-            b = min(w, a + 512)
-            act(X(n, a, b), X("ones", 0, b - a), F.Identity, bias=cb(c), scale=0.0)
-    ms(X("keep", 0, 1024, 16), 0.0)
+    ms(X("aa"), 1999.0)
+    ms(X("ao"), 2000.0)
+    lanes(0)
+    for a in (0, 512):
+        act(X("keep", a, a + 512), X("ones"), F.Copy)
     ms(X("alpha", W), 0.0)
-    ms(X("qt", W), 0.0)
-    ms(X("c48"), float(CAP))
-    ms(X("vs"), 0.0)
-    for t in range(RO):
-        ms(X("fac%d" % t, 1536), 1.0)
-    for n in ("lk0", "lk1"):
-        ms(X(n, 4 * WC), 0.0)
-    ms(X("nt", 0, 2 * NT, NT), -16384.0)
-    for a in (0, NT):
-        ms(X("nt", a + 1537, a + NT), -4096.0)
-    ts(X("em"), X("es"), rr, A.is_equal, -BIG, A.mult)
+    for c in (256.0 * (V * me + 1) - 64, W - 1024.0 - BIG, -1024.0, 256.0 * me + 2048 - LEAVE):
+        cb(c)
     ts(X("pd"), X("j16"), rr, A.not_equal, POIS, A.mult)
     ts(X("rs"), X("j16"), 0.0, A.is_equal, 2.0 ** 20, A.mult)
-    ms(X("em", 0, EQ, 65), 2.0 ** 20)
     ts(X("kw"), X("blk"), rr, A.mult, 0.5, A.mult)
     ts(col1("pf", 7), rr, -LNR, A.mult, -128 * LNR, A.add)
     ts(col1("pf", 12), rr, 5.5, A.is_gt, col1("pf", 15), A.mult)
     ts(col1("pf", 13), rr, -512.0, A.mult, 1024 - 255.5, A.add)
-    ts(col1("pf", 14), rr, -1.0, A.mult)
+    ms(X("keep", 0, 1024, 16), 0.0)
     tt(col1("pf", 12), col1("pf", 12), col1("pf", 13), A.add)
 
+    ts(X("em"), X("es"), rr, A.is_equal, -BIG, A.mult)
+    ms(X("c48"), float(CAP))
+    ms(X("vs"), 0.0)
+    ms(X("em", 0, EQ, 65), 2.0 ** 20)
+    ms(X("qt", W), 0.0)
+
+    def fills(part):
+        for c in (128.0, LEAVE, -29.0, 1024.0):
+            cb(c)
+        ts(col1("pf", 14), rr, -1.0, A.mult)
+
     def late_constants():
+        dma("s", "tc", X("tabc"), X("tab", 0, W))
+        for a in range(0, EQ, 512):
+            b = min(EQ, a + 512)
+            act(X("eq", a, b), X("ones", 0, b - a), F.Copy, scale=BIG)
         for n, c in (("dm", 2.5), ("ipo", -POIS), ("n128", -128.0), ("n256", -256.0), ("n8k", -8192.0), ("idf", 1.0),
                      ("id16", 1.0)):
             act(X(n), X("idb"), F.Copy, scale=c)
@@ -447,15 +491,23 @@ def rank_program(g, core, T, topo):
 
     c0, c1 = cols(me)
     z = lambda n: X(n, c0, c1)
-    lkt = lambda t, k: X("lk%d" % (t % 2), 4 * c0 + k, 4 * c1, 4)
-    ownk = lambda t, k: X("lk%d" % (t % 2), 128 * me + k, 128 * me + 128, 4)
+    table = lambda t, k, a, b: X("lk%d" % (t % 2), LK * (k // 2) + 2 * a + k % 2, LK * (k // 2) + 2 * b, 2)
+    lkt = lambda t, k: table(t, k, c0, c1)
+    ownk = lambda t, k: table(t, k, 32 * me, 32 * me + 32)
+
+    def tables(t, pair, sem):
+        part = lambda q: X("lk%d" % (t % 2), LK * pair + 2 * cols(q)[0], LK * pair + 2 * cols(q)[1])
+        send([(part(me), at(mates), sem + str(t))], "ls%d" % t, pair == 1)
+        settle("lk%d" % (t % 2), "ls%d" % t)
+        lands(sum([part(m)[1] for m in mates], []), sem + str(t), sum(nen(m, 1, pair)[0] for m in mates))
 
     def first_state():
-        gdv = lambda a: R("gd", T["gd"][:, :, a:a + 32])
-        cp(X("rem"), gdv(0))
-        ts(X("nh1"), gdv(32), 1.0, A.add)
-        cp(X("sw"), gdv(64))
-        cp(X("nvd"), gdv(96))
+        q0, q1 = c0 // 32, -(-c1 // 32)
+        gdv = lambda a: R("gd", T["gd"][:, q0:q1, a:a + 32])
+        cp(X("rem", 32 * q0, 32 * q1), gdv(0))
+        ts(X("nh1"), R("gd", T["gd"][:, :, 32:64]), 1.0, A.add)
+        cp(X("sw", 32 * q0, 32 * q1), gdv(64))
+        cp(X("nvd", 32 * q0, 32 * q1), gdv(96))
         ts(z("p6"), z("rem"), 0.0, A.is_equal)
         ts(z("fit"), z("rem"), 1.0, A.min, 2048.0, A.mult)
         ts(lkt(0, 2), z("sw"), -1.0, A.mult, 99.0, A.add)
@@ -465,20 +517,35 @@ def rank_program(g, core, T, topo):
         tt(z("p6"), z("p6"), z("sw"), A.subtract)
         ts(z("nvd"), z("p6"), 1.0, A.add)
 
-    def goods(t):
-        ts(z("p7"), lkt(t, 0), NONE - 0.5, A.is_lt)
-        tt(z("sw"), z("p7"), z("rem"), A.subtract)
-        if t == 0:
-            tt(z("nvd"), z("p7"), z("nvd"), A.mult)
-        else:
+    def goods(t, bank):
+        a, b = z(bank), X(bank, 192 + c0, 192 + c1)
+        ts(a, lkt(t, 0), NONE - 0.5, A.is_lt)
+        if t == 1:
             ms(lkt(t + 1, 2), 50.0)
-        ts(z("p7"), z("sw"), 0.0, A.is_gt)
+        tt(z("sw"), a, z("rem"), A.subtract)
+        tt(z("aa"), z("aa"), a, A.subtract)
+        ts(b, z("sw"), 0.0, A.is_gt)
         if t == 0:
-            tt(lkt(1, 2), lkt(0, 2), z("nvd"), A.subtract)
-        tt(z("p7"), z("p7"), z("nh1"), A.mult)
-        tt(z("rem"), z("p7"), z("sw"), A.subtract)
-        tt(lkt(t + 1, 3), z("p7"), lkt(t, 3), A.add)
+            tt(a, a, z("nvd"), A.mult)
+        tt(b, b, z("nh1"), A.mult)
+        if t == 0:
+            tt(lkt(1, 2), lkt(0, 2), a, A.subtract)
+        tt(z("rem"), b, z("sw"), A.subtract)
+        if t < RO - 2:
+            tt(lkt(t + 1, 3), b, lkt(t, 3), A.add)
         ts(z("fit"), z("rem"), 1.0, A.min, 2048.0, A.mult)
+
+    def last_turns():
+        nh = X("nh1", 32 * me, 32 * me + 32)
+        tt(X("s3"), X("ao"), ownk(RO - 2, 3), A.add)
+        ts(X("s4"), X("s3"), 2100.5, A.is_lt)
+        tt(X("s4"), X("s4"), nh, A.mult)
+        tt(X("s3"), X("s3"), X("s4"), A.add)
+        ts(X("s4"), X("s3"), 2101.5, A.is_lt)
+        tt(X("s3"), X("ao"), X("s3"), A.subtract)
+        ts(X("th", 32, 64), X("s4"), 32768.0, A.mult, 1024.0 - 8192, A.add)
+        tt(X("s4"), X("s4"), nh, A.mult)
+        tt(X("th", 0, 32), X("s3"), X("s4"), A.subtract)
 
     def names(t, b, bank):
         dn = "dn%d" % t
@@ -498,6 +565,7 @@ def rank_program(g, core, T, topo):
         last = t == RO - 1
         dnp = lambda q, a=0, b=WC: R(dn, T[dn][:, q, a:b], 256 * q + a, 256 * q + b)
         if t > 0:
+            wait("s", "cv", cnt["v"])
             dma("s", "tr%d" % t, X("tab", 0, W), X("tabc"))
         cuts = [0, 256] + [512 * c for c in range(1, 9)]
         for a, b in zip(cuts[:-1], cuts[1:]):
@@ -507,60 +575,73 @@ def rank_program(g, core, T, topo):
             unwrap(bank, X("uh", 32 * c, 32 * c + 32))
             if c == 2:
                 wrap(X("p4", 0, 16), "xb", 0, 256)
+            if c == 4 and t > 0:
+                mm(X("p6"), [(X("idb"), X("opp")), (X("idf"), X("ng")), (X("n128"), X("bd"))], True, False)
+            if c == 6 and t > 0:
+                unwrap("p6", X("lkn"), False)
             for a, b in ([(0, 256), (256, 512)] if c == 0 else [(0, 512)]):
                 e = X("ag", 512 * c + a, 512 * c + b)
                 tt(e, e, X(bank, a, b), A.mult)
-            if c == 2:
+            if c == 3:
                 ts(dnp(me, 192, 208), X("p4", 0, 16), V * me - 1024.0, A.add)
+                if t > 0:
+                    cp(X("lkn"), ownk(t - 1, 3))
                 gather_all(lambda q: dnp(q, 192, 208), "nr%d" % t)
-            if c % 2:
-                scan(X("sc", 512 * c - 512, 512 * c + 512), X("keep"), X("ag", 512 * c - 512, 512 * c + 512),
-                     0.0, A.mult, A.max)
-        act(X("p3", 0, 192), X("sc", 15, 3072, 16), F.Copy)
+            for d in {1: [0], 4: [2], 6: [4], 7: [6]}.get(c, []):
+                if d == 6:
+                    act(X("p3", 0, 192), X("sc", 15, 3072, 16), F.Copy)
+                scan(X("sc", 512 * d, 512 * d + 1024), X("keep"), X("ag", 512 * d, 512 * d + 1024), 0.0, A.mult, A.max)
         if t == 0:
             late_constants()
             tt(X("dm"), X("dm"), X("blk"), A.subtract)
         else:
-            for b in range(3):
-                names(t - 1, b, "p%d" % (5 + b))
-            act(X("ng"), IND(X("nt", 0, NT), X("nu")), F.Copy)
-            turn("p5", X("lkf", 1, 128, 4), X("bd"), 64.125 - 2000)
-            mm1(X("p6"), X("idb"), X("opp"), True, False)
-            unwrap("p6", X("lkf", 3, 128, 4), False, False)
-            act(X("bc"), IND(X("lk%d" % ((t - 1) % 2)), X("colx")), F.Copy)
+            act(X("bc"), IND(X("lk%d" % ((t - 1) % 2), LK), X("colw")), F.Copy)
+            mm(X("p7"), [(X("idb"), X("bc")), (X("n256"), X("rd"))])
+            act(X("bc"), X("p7"), F.Relu)
         cp(X("p3", 192, 256), X("sc", 3072 + 15, 4096, 16))
         for k in range(16):
             tk = R("top", T["top"][:, k:4096:16], k, k + 1)
             tt(tk, X("ag", k, 4096, 16), X("p3", 0, 256), A.is_equal)
-            if k == (1 if t > 0 else 10):
-                mm(X("p7", 0, 256), [(X("idb"), X("pd")), (X("idb"), X("l16"))], True, False)
-                mm1(X("p1", 0, 256), X("idb"), X("pd"), True, False)
-            if last and k in (3, 7, 11):
-                names(t, k // 4, ("p0", "p2", "p0")[k // 4])
-            mm1(X("p4", 0, 256), X("zz", 15 - k, 143 - k), tk, k == 0, k == 15)
-        act(X("wb"), X("p4", 0, 256), F.Exp, bias=col1("pf", 7), scale=16 * LNR)
-        mm(X("p0", 0, 256), [(X("dm"), X("wb"))])
-        mm(X("p5", 0, 256), [(X("dm"), X("wb"))])
-        ts(X("p3", 256), X("p0", 0, 256), 0.0, A.is_gt)
-        act(X("sg"), X("p5", 0, 256), F.Sign)
-        tt(X("sf"), X("p3", 256), X("fm"), A.mult)
-        mm1(X("p7", 0, 256), X("kw"), X("sg"), False, True)
-        mm1(X("p1", 0, 256), X("blk16"), X("sf"), False, True)
+            if t > 0 and k == 6:
+                mm(X("p7"), [(X("blk"), X("bc"))])
+            if last and k < 3:
+                names(t, k, ("p0", "p2", "p0")[k])
+            for h in range(2):
+                th = R("top", T["top"][:, 2048 * h + k:2048 * h + 2048:16], k, k + 1)
+                mm1(X(VOTE[h], 0, 128), X("zz", 15 - k, 143 - k), th, k == 0, k == 15)
+        half = lambda n, h: X(n, 128 * h, 128 * h + 128)
+        for h in range(2):
+            act(half("wb", h), X(VOTE[h], 0, 128), F.Exp, bias=col1("pf", 7), scale=16 * LNR)
+            mm(X(PICK[h], 0, 128), [(X("dm"), half("wb", h))])
+        mm(X("p2", 256), [(X("dm"), X("wb"))])
+        for h in range(2):
+            mm1(X(VOTE[h], 0, 128), X("idb"), half("pd", h), True, False)
+        mm(X("p3", 0, 256), [(X("idb"), X("pd")), (X("idb"), X("l16"))], True, False)
+        if t > 0:
+            tt(X("vv"), X("p6"), X("vv"), A.max)
+        act(X("sg"), X("p2", 256), F.Sign)
+        for h in range(2):
+            ts(X(PICK[h], 0, 128), X(PICK[h], 0, 128), 0.0, A.is_gt)
+        for h in range(2):
+            tt(half("sf", h), X(PICK[h], 0, 128), half("fm", h), A.mult)
+            mm1(X(VOTE[h], 0, 128), X("blk16"), half("sf", h), False, True)
         mm(X("p2", 0, 256), [(X("blk16"), X("sf"))])
+        mm1(X("p3", 0, 256), X("kw"), X("sg"), False, True)
         mm(X("p0", 256), [(X("blk16"), X("sf"))])
-        wrap(X("p3", 0, 16), "sf", 0, 256, "z16", True, False)
-        scan(X("ks"), X("rs"), X("p7", 0, 256), 0.0, A.add, A.min)
-        scan(X("ms"), X("rs"), X("p1", 0, 256), 0.0, A.add, A.min)
+        wrap(X("p6", 0, 16), "sf", 0, 256, "z16", True, False)
+        for h in range(2):
+            scan(half("ms", h), half("rs", h), X(VOTE[h], 0, 128), 0.0, A.add, A.min)
+        scan(X("ks"), X("rs"), X("p3", 0, 256), 0.0, A.add, A.min)
         act(X("ab"), X("p2", 0, 256), F.Abs, bias=col1("pf", 12))
         act(X("nb"), X("ms", 15, 256, 16), F.Copy, scale=-BIG)
-        ts(X("ku"), X("ks", 15, 256, 16), 60.0, A.add)
         ts(X("oh"), X("ab"), 256.0, A.is_lt)
+        ts(X("ku"), X("ks", 15, 256, 16), 60.0, A.add)
         scan(X("vs", 1, 257), X("oh"), X("c48"), 0.0, A.add, A.min)
-        wrap(X("p3", 0, 16), "vs", 1, 257, "zn", False, False)
-        wrap(X("p3", 0, 16), "vs", 0, 256, "zp", False, True)
+        wrap(X("p6", 0, 16), "vs", 1, 257, "zn", False, False)
+        wrap(X("p6", 0, 16), "vs", 0, 256, "zp", False, True)
         for c in range(16):
             o, b = X("eq", 65 * c + 1, 65 * c + 65), 64 * (c // 4)
-            if c < 7:
+            if c < 6:
                 ts(o, X("p0", 256 + b, 320 + b), col1("ms", 16 * c + 15), A.not_equal, BIG, A.mult)
             else:
                 act(o, X("p2", b, b + 64), F.Abs, bias=col1("nb", c), scale=BIG)
@@ -569,12 +650,12 @@ def rank_program(g, core, T, topo):
             wait("g", "a0", total["a0"])
         relay(fac)
         mm(X("p2", 256), [(X("blk16"), X("sf")), (X("bvn"), X("vs", 1, 257)), (X("bvp"), X("vs", 0, 256))])
-        if t > 0:
-            mm(X("p6"), [(X("idf"), X("ng")), (X("n128"), X("bd"))], False, True)
+        if last:
+            turn("p5", X("ao"), X("bd"), 63.125 - 2000)
         act(X("xw", 0, 256), X("p2", 256), F.Relu, bias=cb(W - 1024.0 - BIG), scale=-1.0)
         act(X("gx"), IND(X("xw"), X("posw")), F.Identity, bias=cb(-1024.0))
         scan(X("es"), X("em"), X("eq"), 0.0, A.add, A.min)
-        tt(X("s2", 0, 16), X("p3", 0, 16), X("es", 64, EQ, 65), A.subtract)
+        tt(X("s2", 0, 16), X("p6", 0, 16), X("es", 64, EQ, 65), A.subtract)
         tt(X("s3", 0, 16), X("s2", 0, 16), X("dl"), A.min)
         ts(X("xu"), X("s3", 0, 16), 1024.0 + BIG, A.add)
         for b in (3, 2, 1, 0):
@@ -585,105 +666,104 @@ def rank_program(g, core, T, topo):
             wrap(halves[hf], "tab", 16 * H * hf, 16 * H * (hf + 1))
         if t == 0:
             tt(X("ta"), IND(X("qt"), X("nu")), X("nm1"), A.subtract)
-            act(X("ta"), X("ta"), F.Abs)
-            act(X("bc"), X("ta"), F.Relu, bias=cb(128.0), scale=-1.0)
+        elif last:
+            last_turns()
         else:
-            tt(X("vv"), X("p6"), X("vv"), A.max)
+            tt(X("tw", 512), X("p7"), X("vl"), A.min)
         wants = lambda q, hf: [a for a in range(cols(q)[0], cols(q)[1], Q) if a // H == hf]
         engines = lambda q, hf: nen(q, sum(len(wants(m, hf)) for m in same(q)), sum(len(wants(m, hf)) for m in other(q)))
         for hf in range(2):
             ts(dnp(me, H * hf, H * hf + H), halves[hf], 1.0 / 16, A.mult, 256.0 * me, A.add)
             send([(dnp(me, a, a + Q), at([q]), ("df%d" if q in far else "dn%d") % t)
                   for q in far + mates for a in wants(q, hf)], "sent")
+            if hf == 0 and t == 0:
+                fills(1)
+                act(X("ta"), X("ta"), F.Abs)
+                act(X("bc"), X("ta"), F.Relu, bias=cb(128.0), scale=-1.0)
+            elif hf == 0 and last:
+                tt(X("tw", 512), X("p7"), X("vl"), A.min)
         for qs, sem, side in ((far, "df%d" % t, 1), (mates, "dn%d" % t, 0)):
             lands(sum([dnp(q)[1] for q in qs], []), sem,
                   sum(len(wants(me, hf)) * engines(q, hf)[side] for q in qs for hf in range(2)))
         wrap(X("p0", 0, 32), "gx", 0, 512, "z16")
-        if t > 0:
-            mm(X("p7"), [(X("idb"), X("bc")), (X("n256"), X("rd"))])
-            act(X("bc"), X("p7"), F.Relu)
         if last:
-            turn("p3", X("lkf", 1, 128, 4), X("bd"), 63.125 - 2000)
+            turn("p6", X("th", 0, 32), X("p4"), 165 + 1.0 / 8192)
             ts(X("ia"), X("vv"), 4096.0, A.mult)
-        mm(X("p5"), [(X("blk"), X("bc"))])
+        if t == 0:
+            mm(X("p5"), [(X("blk"), X("bc"))])
         ts(X("yi"), X("p0", 0, 32), -1.0 / 16, A.mult, W - 1024.0, A.add)
         ts(X("yl"), X("yi"), 15, A.bitwise_and)
-        ts(X("yc"), X("yi"), 2, A.arith_shift_right, 4092, A.bitwise_and)
+        ts(X("yc"), X("yi"), 3, A.arith_shift_right, 4094, A.bitwise_and)
         cp(X("lo"), X("yl"))
         tt(X("s4"), X("yc"), X("hw"), A.subtract)
         unwrap("p0", X("lo"))
         ts(X("colw"), X("s4"), 1.0, A.add)
-        if not last:
-            ts(X("colx"), X("s4"), 3.0, A.add)
         if t == 0:
             act(X("tw", 512), X("p5"), F.Identity, bias=cb(-29.0))
             first_state()
         else:
-            goods(t - 1)
-            tt(X("tw", 512), X("p5"), X("vl"), A.min)
-        act(X("rd"), X("p0"), F.Abs, bias=col1("pf", 14))
+            goods(t - 1, "p7")
         act(X("vl"), IND(X("tw"), X("posw")), F.Copy)
+        act(X("rd"), X("p0"), F.Abs, bias=col1("pf", 14))
         mm(X("p2"), [(X("ipo"), X("rd")), (X("id16"), X("vl"))])
         act(X("ex"), X("p2"), F.Relu, bias=cb(LEAVE))
         if not last:
             act(X("xw", 512), X("gx"), F.Identity, bias=cb(1024.0))
+            for b in range(3):
+                names(t, b, "p%d" % (3 + b))
         else:
-            nh = R("gd", T["gd"][:, me, 32:64], me, me + 1)
-            tt(X("s1"), ownk(t - 1, 1), ownk(t - 1, 3), A.add)
-            ts(X("s4"), nh, 1.0, A.add)
-            ts(X("s2"), X("s1"), 2100.5, A.is_lt)
+            ts(X("ib"), X("ia"), 4095, A.bitwise_and)
             cp(X("gw"), X("yi"))
-            tt(X("s2"), X("s2"), X("s4"), A.mult)
-            tt(X("s1"), X("s1"), X("s2"), A.add)
-            ts(X("s2"), X("s1"), 2101.5, A.is_lt)
-            ts(X("th", 32, 64), X("s2"), 32768.0, A.mult, -8192.0, A.add)
-            tt(X("s2"), X("s2"), X("s4"), A.mult)
-            tt(X("s1"), X("s1"), X("s2"), A.add)
-            tt(X("th", 0, 32), ownk(t - 1, 1), X("s1"), A.subtract)
-            turn("p6", X("th", 0, 32), X("p4"), 165 + 1.0 / 8192)
             mm1(X("p3"), X("n8k"), X("bd"), True, False)
             unwrap("p3", X("th", 32, 64), False)
-            ts(X("ib"), X("ia"), 4095, A.bitwise_and)
+            tt(X("tc"), X("p4"), X("ib"), A.mult)
+            act(X("tb"), X("tc"), F.Identity, bias=cb(BIG + 1024), scale=-1.0)
         w = z("p1")
         qs = near + far
         tt(w, dnp(qs[0], c0, c1), dnp(qs[1], c0, c1), A.min)
         for q in qs[2:]:
             tt(w, w, dnp(q, c0, c1), A.min)
-        ts(z("p7"), w, NONE - 0.5, A.is_lt)
         tt(lkt(t, 0), w, z("fit"), A.add)
-        if t == 0:
-            ts(lkt(t, 1), z("p7"), -1.0, A.mult, 2000.0, A.add)
-        else:
-            tt(lkt(t, 1), lkt(t - 1, 1), z("p7"), A.subtract)
-        send([(X(lk, 4 * c0, 4 * c1), at(mates), "lr%d" % t)], "ls%d" % t)
-        lands([(lk, 4 * cols(m)[0], 4 * cols(m)[1]) for m in mates], "lr%d" % t, sum(nen(m, 1, 0)[0] for m in mates))
-        h = (c1 - c0) * 8
-        shares = lambda q: ([(16 * cols(q)[0], h), (16 * cols(q)[0] + h, h)] if h > 512 else [(16 * cols(q)[0], 2 * h)])
+        tt(lkt(t, 1), w, z("aa"), A.max)
+        tables(t, 0, "lr")
         ts(X("offu", c0, c1), lkt(t, 0), 1536.0, A.min)
-        for j, (lo, k) in enumerate(shares(me)):
-            part = X("alpha", lo, lo + k)
-            tt(part, IND(X(fac), X("offu", lo // 16, (lo + k) // 16)), part, A.mult)
-            send([(part, at(mates), "ar%d" % t)], "as%d" % t)
-        settle("alpha", "as%d" % t)
-        lands(sum([X("alpha", lo, lo + k)[1] for m in mates for lo, k in shares(m)], []), "ar%d" % t,
-              sum(len(shares(m)) * nen(m, 1, 0)[0] for m in mates))
+        h = (c1 - c0) * 16
+        cut = [0, h] if h <= 768 else [0, 576, 1152, h]
+        shares = lambda q: [(16 * cols(q)[0] + a, 16 * cols(q)[0] + b) for a, b in zip(cut[:-1], cut[1:])]
+
+        def rise(lo, hi):
+            tt(X("alpha", lo, hi), IND(X(fac), X("offu", lo // 16, hi // 16)), X("alpha", lo, hi), A.mult)
+            send([(X("alpha", lo, hi), at(mates), "ar%d" % t)], "as%d" % t)
+        early = 3 if last else 2
+        for j, part in enumerate(shares(me)[:early]):
+            rise(*part)
+            if last and j == len(shares(me)) // 2:
+                tt(X("zf"), X("p3"), X("tb"), A.min)
+                mm1(X("p0"), X("idf"), X("zf"), True, False)
         if last:
-            tt(X("tc"), X("p4"), X("ib"), A.mult)
-            act(X("tb"), X("tc"), F.Identity, bias=cb(BIG), scale=-1.0)
-            act(X("p0"), X("tc"), F.Copy)
-        tt(X("hit"), IND(X(lk), X("colw")), X("ex"), A.is_lt)
-        ts(X("nu"), ownk(t, 0), -2047.0, A.add, 1537.0, A.min)
+            ts(X("nu"), ownk(t, 0), -2047.0, A.add, 1537.0, A.min)
+            act(X("gx"), IND(X("nt", NT), X("nu")), F.Identity, bias=cb(-1024.0))
+        tt(X("hit"), IND(X(lk, 0, LK), X("colw")), X("ex"), A.is_lt)
         if not last:
             positions(t + 1)
-            cp(X("lkf"), X(lk, 128 * me, 128 * me + 128))
+        for part in shares(me)[early:]:
+            rise(*part)
+        settle("alpha", "as%d" % t)
+        lands(sum([X("alpha", *part)[1] for m in mates for part in shares(m)], []), "ar%d" % t,
+              sum(len(shares(m)) * nen(m, 1, 0)[0] for m in mates))
+        if not last:
+            ts(X("nu"), ownk(t, 0), -2047.0, A.add, 1537.0, A.min)
+            tt(X("ao"), X("ao"), ownk(t, 1), A.min)
+            tables(t, 1, "lq")
+            act(X("ng"), IND(X("nt", 0, NT), X("nu")), F.Copy)
+            turn("p5", X("ao"), X("bd"), 64.125 - 2000)
             lanes(t + 1)
     mm(X("p2"), [(X("idb"), X("ones")), (X("nblk"), X("hit"))])
-    tt(X("zf"), X("p3"), X("tb"), A.min)
+    mm1(X("p0"), X("id16"), X("gx"), False, True)
     tt(X("ex"), X("p2"), X("monb"), A.mult)
-    tt(X("ng"), IND(X("nt", NT), X("nu")), X("zf"), A.add)
-    tt(X("tc"), X("p0"), X("ng"), A.max)
-    dma("s", "st2", T.yh[:], X("tc"))
-    dma("a", "st0", T.yal[:], mine("alpha"))
+    dma("s", "st0", T.yal[:], mine("alpha"))
+    tt(X("ng"), X("p0"), X("tc"), A.max)
+    dma("a", "st2", T.yh[:], X("ng"))
     tt(X("ta"), IND(X("alpha"), X("gw")), X("ex"), A.mult)
     dma("s", "st1", T.yp[:], X("ta"))
     for sem in sorted(total):

import math
from concourse.bass import DstId, RemoteDMATransfer
from concourse.mybir import AluOpType as A, ActivationFunctionType as F

N, V, W, RO, CAP = 6, 512, 3072, 4, 48
WC = W // 16
AW = W + 8
LK = 2 * WC + 8
NT = 1544
EQ = 16 * 65
S, P = "sbuf", "psum"
f32, b16, f16, i32, u16 = "float32", "bfloat16", "float16", "int32", "uint16"
_B = {
    f32: dict(alpha=AW, qt=AW, ag=4096, sc=4096, colf=512, pf=24, rm=16, dl=16, dj=32, nm1=512, ta=512, tb=512,
              tc=512, vv=512, ex=512, rem=WC, nh1=WC, fit=WC, nvd=WC, sw=WC, lk0=2 * LK, lk1=2 * LK, ab=256,
              ms=256, s1=32, s2=32, s3=32, s4=32, nt=2 * NT, ng=512, xw=1024, tw=1024, idf=128, cb=128, ps=32, nb=16,
              ks=256, zf=512, aa=WC),
    b16: dict(top=4096, utb=512, monb=512, blk=128, nblk=128, idb=128, tri=128, dm=128, kw=128, mp=128, t64=128,
              t32=128, bvp=128, bvn=128, i128=128, ipo=128, i64=128, n128=128, n256=128, n8k=128, d0=128, d1=128,
              zz=144, zp=144, zn=144, pd=256, l16=256, rs=256, keep=1024, em=EQ, ones=512, c48=256, pay=256,
              tab=AW + 256, ba=512, bb=512, bc=512, bd=512, opp=512, hit=512, xb=256, wb=256, sg=256, oh=256,
              vs=264, eq=EQ, es=EQ, hw=32, rd=512, j16=256, xl=512, xh=512),
    f16: dict(blk16=128, b8=128, z8=144, z16=144, id16=128, ha=512, uh=256, fm=256, sf=256, th=64, gx=512, vl=512, lo=32,
              ao=32, lkn=32),
    i32: dict(fti=512, hni=512, hbi=512, pi=8, comb=512, lt=1024, ltc=256, ia=512, ib=512, ui=256, yi=32, yc=32, yl=32),
    u16: dict(offu=WC, fu=256, posw=32, colw=32, colx=32, gw=32, ku=16, xu=16, nu=32),
}
_B[b16]["tabc"] = W
WIDTH = {n: c for d in _B for n, c in _B[d].items()}
ALIAS = dict(yc=("yi", 32), yl=("yi", 64), xu=("ku", 16), lo=("th", 64), dl=("dj", 32), hbi=("ib", 0), ps=("dj", 48),
             colx=("colw", 32), gw=("colw", 64), nb=("dj", 80), d1=("d0", 128), n256=("n128", 128), n8k=("n128", 256),
             xh=("xl", 512), s2=("s1", 32), s3=("s1", 64), s4=("s1", 96), zn=("zp", 144), ao=("th", 128),
             lkn=("th", 96), aa=("rem", WC))
SCRATCH = {n: (S, [128, max([c] + [o + WIDTH[a] for a, (m, o) in ALIAS.items() if m == n])], d)
           for d in _B for n, c in _B[d].items() if n not in ALIAS}
SCRATCH["selt"] = (S, [128, 16, 128], f16)
SCRATCH["gd"] = (S, [128, 6, 128], b16)
for _t in range(RO):
    SCRATCH["fac%d" % _t] = (S, [128, 1544], b16)
    SCRATCH["dn%d" % _t] = (S, [128, 6, 208], f16)
for _t in range(8):
    SCRATCH["p%d" % _t] = (P, [128, 512], f32)
RELAYED = ["qt", "gd"] + ["fac%d" % t for t in range(RO)]
SEMAPHORES = (["cv", "ca", "cp", "cg", "sent", "a0", "a1", "a2", "a3", "a4", "ha", "st0", "st1", "st2", "lt", "tc"]
              + ["ld%d" % i for i in range(6)] + [p + n for n in RELAYED for p in ("r", "h")]
              + ["%s%d" % (n, t) for t in range(RO) for n in ("dn", "df", "ar", "as", "tr", "nr", "lr", "lq", "ls")])
BIG, POIS, NONE = 4096.0, 32768.0, 4096.0
LEAVE = 1901.0
LNR = math.log(1.8)
VOTE, PICK = ("p4", "p5"), ("p0", "p1")


def rank_program(g, core, T, topo):
    cores = list(T.cores)
    place = lambda c: (topo.host(c), topo.chip(c))
    other = lambda q: [r for r in range(N) if place(cores[r]) != place(cores[q])]
    same = lambda q: [r for r in range(N) if place(cores[r]) == place(cores[q]) and r != q]
    dst = lambda c: DstId(rid=int(topo.addr(c, core)[0]), pnc=int(topo.addr(c, core)[1]))

    def helpers(q):
        free = [c for c in topo.cores_of(cores[q]) if c not in cores]
        return sorted(free, key=lambda c: topo.die(c) != topo.die(cores[q]))[:2]

    def piece(n, q0, q1):
        if n == "gd":
            return (T[n][:, q0:q1, :], [(n, q0, q1)])
        k = V if n == "qt" else 256
        return (T[n][:, k * q0:k * q1], [(n, k * q0, k * q1)])

    def route(q, j):
        chip, there = sorted(same(q) + [q]), other(q)
        if len(chip) <= len(there) or topo.die(helpers(q)[0]) == topo.die(cores[q]):
            return 0, there[j * len(there) // 4]
        if j < 2:
            return 0, there[j]
        return (1, there[chip.index(q) // 2]) if j == 3 else (2, there[chip.index(q) % len(there)])

    me = T.rank_of(core)
    if me is None:
        here = [q for q in range(N) if place(cores[q]) == place(core)]
        if not here or core not in helpers(here[0]):
            return
        k = len(other(here[0])) // 2
        q0 = other(here[0])[k * helpers(here[0]).index(core)]
        mask = topo.mask(core, cores[here[0]])
        to = other(here[0])[helpers(here[0]).index(core)]
        via = [q for q in here if route(q, 3) == (1, to)]
        if via:
            es = topo.engines(core, cores[to])
            n = len(es) // len(via)
            g.wait_ge(T.sem["ha"], len(via) * (len(topo.engines(core, cores[via[0]])) - len(es)))
            g.remote_dma_fused([RemoteDMATransfer(
                dst_ids=[dst(cores[to])], dma_engine_mask=sum(1 << e for e in es[n * j:n * j + n]), remote_sem=T.sem["a4"],
                srcs=[T.alpha[:, V * q + 384:V * q + V]], dsts=[T.alpha[:, V * q + 384:V * q + V]])
                for j, q in enumerate(via)], local_sem=T.sem["a0"])
            g.wait_ge(T.sem["a0"], len(es))
        for n in RELAYED:
            g.wait_ge(T.sem["h" + n], sum(len(topo.engines(cores[q], core)) for q in range(q0, q0 + k)))
            x = piece(n, q0, q0 + k)[0]
            g.remote_dma_fused([RemoteDMATransfer(dst_ids=[dst(cores[q]) for q in here], dma_engine_mask=mask,
                                                  remote_sem=T.sem["r" + n], srcs=[x], dsts=[x] * len(here))],
                               local_sem=T.sem["sent"])
        g.wait_ge(T.sem["sent"], len(RELAYED) * len(topo.engines(core, cores[here[0]])))
        return
    far, mates = other(me), same(me)
    near = sorted(mates + [me])
    eng = {"v": g.vector, "a": g.scalar, "p": g.tensor, "g": g, "s": g.sync}
    cnt = {"v": 0, "a": 0, "p": 0, "g": 0}
    seen = {e: {} for e in eng}
    acc = {}
    total = {}

    def X(n, lo=0, hi=None, st=1):
        if hi is None:
            hi = WIDTH[n] if n in WIDTH else SCRATCH[n][1][1]
        if n in ALIAS:
            n, lo, hi = ALIAS[n][0], lo + ALIAS[n][1], hi + ALIAS[n][1]
        return (T[n][:, lo:hi:st] if st > 1 else T[n][:, lo:hi], [(n, lo, hi)])

    def R(n, ap, lo=0, hi=1 << 20):
        return (ap, [(n, lo, hi)])

    def IND(win, off):
        return (win[0].indirect(off[0]), win[1], off[1])

    def wait(e, sem, val):
        if seen[e].get(sem, 0) < val:
            eng[e].wait_ge(T.sem[sem], val)
            seen[e][sem] = val

    def order(e, reads, writes):
        need = {}
        for regs, wr in ((reads, False), (writes, True)):
            for n, lo, hi in regs:
                bank = SCRATCH[n][0] == P
                for l2, h2, w2, e2, sem, val in acc.get(n, []):
                    hit = l2 < hi and lo < h2 and (wr or w2)
                    dep = (e != "p" and hit) if e2 == e else (bank or hit)
                    if dep and val > need.get(sem, 0):
                        need[sem] = val
        for sem in sorted(need):
            wait(e, sem, need[sem])

    def note(e, reads, writes, sem, val):
        for regs, wr in ((writes, True), (reads, False)):
            for n, lo, hi in regs:
                old = acc.get(n, [])
                if wr and e != "d":
                    old = [o for o in old if not (lo <= o[0] and o[1] <= hi)]
                old = [o for o in old if not (o[:5] == (lo, hi, wr, e, sem))]
                acc[n] = old + [(lo, hi, wr, e, sem, val)]
        total[sem] = max(total.get(sem, 0), val)

    def op(e, fn, outs, ins):
        reads, writes = [], []
        for o in outs:
            writes += o[1]
            if len(o) > 2:
                reads += o[2]
        for i in ins:
            if isinstance(i, tuple):
                reads += i[1] + (i[2] if len(i) > 2 else [])
        order(e, reads, writes)
        cnt[e] += 1
        fn().then_inc(T.sem["c" + e], 1)
        note(e, reads, writes, "c" + e, cnt[e])

    ap = lambda x: x[0] if isinstance(x, tuple) else x

    def tt(o, a, b, f):
        op("v", lambda: g.vector.tensor_tensor(o[0], a[0], b[0], f), [o], [a, b])

    def ts(o, a, s1, f1, s2=None, f2=None):
        if f2 is None:
            op("v", lambda: g.vector.tensor_scalar(o[0], a[0], ap(s1), None, f1), [o], [a, s1])
        else:
            op("v", lambda: g.vector.tensor_scalar(o[0], a[0], ap(s1), ap(s2), f1, f2), [o], [a, s1, s2])

    def cp(o, a):
        op("v", lambda: g.vector.tensor_copy(o[0], a[0]), [o], [a])

    def ms(o, c):
        op("v", lambda: g.vector.memset(o[0], c), [o], [])

    def scan(o, a, b, i, f0, f1):
        op("v", lambda: g.vector.tensor_tensor_scan(o[0], a[0], b[0], ap(i), f0, f1), [o], [a, b, i])

    consts = {}

    def cb(c):
        if c not in consts:
            consts[c] = len(consts)
            ms(X("cb", consts[c], consts[c] + 1), c)
        return X("cb", consts[c], consts[c] + 1)

    def act(o, a, f, bias=0.0, scale=1.0):
        op("a", lambda: g.scalar.activation(o[0], a[0], f, bias=ap(bias), scale=ap(scale)), [o], [a, bias, scale])

    def mm1(o, l, r, first, last):
        op("p", lambda: g.tensor.matmul(o[0], l[0], r[0], first, last), [o], [l, r])

    def mm(o, pairs, first=True, last=True):
        for i, (l, r) in enumerate(pairs):
            mm1(o, l, r, first and i == 0, last and i == len(pairs) - 1)

    def iota(o, pat, base, cm):
        if SCRATCH[o[1][0][0]][2] == i32:
            op("g", lambda: g.iota(o[0], pat, base, cm), [o], [])
        else:
            op("g", lambda: g.iota(o[0], pat, base, cm, allow_small_or_imprecise_dtypes=True), [o], [])

    def dma(e, sem, o, i):
        reads = i[1] if isinstance(i, tuple) else []
        writes = o[1] if isinstance(o, tuple) else []
        order(e, reads, writes)
        eng[e].dma_start(ap(o), ap(i)).then_inc(T.sem[sem], 16)
        note("d", reads, writes, sem, total.get(sem, 0) + 16)

    def settle(n, sem):
        acc[n] = [o[:5] + (total[sem],) if o[4] == sem else o for o in acc[n]]

    def pow2(n):
        return 1 << (n.bit_length() - 1)

    def share(q, n_near, n_far):
        off = topo.engines(cores[q], cores[other(q)[0]]) if n_far else []
        on = [k for k in topo.engines(cores[q], cores[same(q)[0]]) if k not in off] if n_near else []
        return on, off

    def nen(q, n_near, n_far):
        on, off = share(q, n_near, n_far)
        return (pow2(len(on) // n_near) if n_near else 0, pow2(len(off) // n_far) if n_far else 0)

    def send(items, lsem, beside=False):
        inn = [i for i in items if place(i[1][0]) == place(core)]
        out = [i for i in items if place(i[1][0]) != place(core)]
        on, off = share(me, len(inn), len(out) or beside)
        trs, reads, inc = [], [], 0
        for its, es in ((out, off), (inn, on)):
            for j, (x, cs, sem) in enumerate(its):
                k = pow2(len(es) // len(its))
                m = 0
                for b in es[j * k:(j + 1) * k]:
                    m |= 1 << b
                trs.append(RemoteDMATransfer(dst_ids=[dst(c) for c in cs], dma_engine_mask=m, remote_sem=T.sem[sem],
                                             srcs=[x[0]], dsts=[x[0]] * len(cs)))
                reads += x[1]
                inc += k
        order("g", reads, [])
        g.remote_dma_fused(trs, local_sem=T.sem[lsem])
        note("d", reads, [], lsem, total.get(lsem, 0) + inc)

    at = lambda qs: [cores[q] for q in qs]

    def lands(regs, sem, val):
        note("d", [], regs, sem, val)

    def gather_all(part, sem):
        send([(part(me), at(mates), sem)] + [(part(me), at([q]), sem) for q in far], "sent")
        k = sum(nen(q, 1, len(far))[0] for q in mates) + sum(nen(q, 1, len(near))[1] for q in far)
        lands(sum([part(q)[1] for q in mates + far], []), sem, k)

    def relay(n):
        h = helpers(far[0])[near.index(me) // (len(near) // 2)]
        send([(piece(n, me, me + 1), at(mates), "r" + n), (piece(n, me, me + 1), [h], "h" + n)], "sent")
        k = sum(nen(q, 1, 1)[0] for q in mates) + sum(len(topo.engines(c, core)) for c in helpers(me))
        lands(sum([piece(n, q, q + 1)[1] for q in mates + far], []), "r" + n, k)

    quarter = lambda q, j: X("alpha", V * q + 128 * j, V * q + 128 * j + 128)
    got = lambda r, way: [(q, j) for q in other(r) for j in range(4) if route(q, j) == (way, r)]

    def prices1():
        ways = lambda q, way: [j for j in range(4) if route(q, j)[0] == way]
        outs = lambda way, sem: [(quarter(me, j), at([route(me, j)[1]]), sem) for j in ways(me, way)]
        via = [(quarter(me, j), [helpers(me)[far.index(route(me, j)[1])]], "ha") for j in ways(me, 1)]
        send(outs(0, "a1") + via, "a0")
        if via:
            send(outs(2, "a4"), "a0")
        send([(mine("alpha"), at(mates), "a2")], "a0", True)
        lands(sum([quarter(q, j)[1] for q, j in got(me, 0)], []), "a1",
              sum(nen(q, 0, len(ways(q, 0)))[1] for q, j in got(me, 0)))
        if got(me, 1):
            lands(sum([quarter(q, j)[1] for q, j in got(me, 1) + got(me, 2)], []), "a4",
                  len(topo.engines(helpers(far[0])[0], core)) + sum(nen(q, 0, 1)[1] for q, j in got(me, 2)))
        lands(sum([X("alpha", V * q, V * q + V)[1] for q in mates], []), "a2", sum(nen(q, 1, 1)[0] for q in mates))

    def prices2():
        k = 0
        stage = lambda r, late: got(r, 1) + got(r, 2) if late else got(r, 0)
        for late in range(2):
            if stage(me, late):
                send([(quarter(q, j), at(mates), "a3") for q, j in stage(me, late)], "a0")
                k += sum(len(stage(m, late)) * nen(m, len(stage(m, late)), 0)[0] for m in mates)
        settle("alpha", "a0")
        lands([quarter(q, j)[1][0] for m in mates for late in range(2) for q, j in stage(m, late)], "a3", k)

    selT = lambda k: R("selt", T["selt"][:, k, :], k, k + 1)

    def wrap(o, src, lo, hi, z="zz", first=True, last=True):
        mm(o, [(X(z, 15 - r, 143 - r), X(src, lo + r, hi, 16)) for r in range(16)], first, last)

    def unwrap(bank, rhs, first=True, last=True, n=512):
        for r in range(16):
            mm1(X(bank, r, n, 16), selT(r), rhs, first, first or (last and r == 15))

    col1 = lambda n, c: X(n, c, c + 1)
    mine = lambda n: X(n, V * me, V * me + V)
    h8 = lambda n, a=0, b=512, s=1: R(ALIAS.get(n, (n,))[0], T[ALIAS.get(n, (n,))[0]][0:8, a:b:s])

    dma("s", "ld0", mine("alpha"), T.al[:])
    dma("a", "ld2", h8("hbi"), T.hb[:])
    dma("s", "ld1", X("hni"), T.hn[:])
    dma("a", "ld4", X("utb"), T.ut[:])
    dma("s", "ld3", X("fti"), T.ft[:])
    dma("a", "ld5", X("monb"), T.mon[:])
    iota(col1("pi", 0), [[0, 1]], 0, 1)
    iota(X("ab", 0, 128), [[1, 8], [0, 16]], 0, 0)
    iota(X("colf"), [[1, 512]], 0, 0)
    iota(X("ltc"), [[0, 256]], 4096 * W + 128, 0)
    prices1()
    iota(X("xl"), [[0, 8], [1, 64]], 0, 0)
    iota(X("xh"), [[1, 8], [0, 64]], 0, 0)
    iota(X("lt"), [[0, 1024]], 4096 * W + 128, 0)
    iota(X("j16"), [[0, 16], [1, 16]], 0, 0)
    prices2()
    iota(X("es"), [[0, 4], [-16, 4], [1, 65]], -1, 0)
    wait("g", "a3", total["a3"])
    ms(X("ones"), 1.0)
    for c in (NONE, 1.0, W - 1024.0, -31.0, -160.0, 64.0, 63.0, 33.0, 32.0):
        cb(c)
    act(col1("pf", 15), cb(1.0), F.Exp, scale=14.0)
    for a in range(0, AW + 256, 512):
        b = min(AW + 256, a + 512)
        act(X("tab", a, b), X("ones", 0, b - a), F.Identity, bias=cb(NONE), scale=0.0)
    ts(col1("pi", 1), col1("pi", 0), 15, A.bitwise_and)
    ts(col1("pi", 2), col1("pi", 0), 4, A.arith_shift_right)
    cp(X("pf", 0, 3), X("pi", 0, 3))
    pp, rr, gg = col1("pf", 0), col1("pf", 1), col1("pf", 2)
    ts(col1("pf", 3), gg, 16.0, A.mult, 15.0, A.add)
    ts(col1("pf", 4), pp, 16.0, A.mult, 15.0, A.add)
    ts(X("blk"), X("ab", 0, 128), gg, A.is_equal)
    ts(X("z8"), X("colf", 0, 144), col1("pf", 4), A.is_equal)
    ts(X("b8"), X("ab", 0, 128), pp, A.is_equal)
    ts(X("idb"), X("colf", 0, 128), pp, A.is_equal)
    ts(X("tri"), X("colf", 0, 128), pp, A.is_gt)
    ts(X("zz"), X("colf", 0, 144), col1("pf", 3), A.is_equal)
    ts(X("rm"), X("colf", 0, 16), rr, A.is_equal)
    tt(X("tri"), X("tri"), X("blk"), A.mult)
    for n, c in (("i64", -64.0), ("t32", -32.0), ("mp", -1023.0), ("i128", 128.0), ("d0", col1("rm", 0)),
                 ("d1", col1("rm", 1))):
        act(X(n), X("idb"), F.Copy, scale=c)
    ts(h8("ha"), h8("hbi"), -1024.0, A.add)
    ts(X("ba"), X("hni"), 0.0, A.is_equal)
    ts(X("bb"), X("hni"), 0.0, A.is_lt)
    for t in range(RO):
        ms(X("fac%d" % t, 1536), 1.0)
    for n in ("lk0", "lk1"):
        for a in (LK, 2 * LK):
            ms(X(n, a - 8, a), 0.0)
    ms(X("nt", 0, 2 * NT, NT), -16384.0)
    for a in (0, NT):
        ms(X("nt", a + 1537, a + NT), -4096.0)
    tt(X("t64"), X("i64"), X("tri"), A.add)
    tt(X("t32"), X("t32"), X("tri"), A.add)
    ts(X("bc"), X("hni"), 3072.5, A.is_lt)
    ts(X("bd"), X("hni"), 0.5, A.is_lt)
    cp(X("ex"), X("hni"))
    mm(X("p0"), [(X("t64"), X("ba"))])
    mm(X("p7"), [(X("blk"), X("ba")), (X("t64"), X("bb"))])
    mm(X("p2"), [(X("t32"), X("bc"))])
    mm(X("p3"), [(X("t32"), X("bc")), (X("blk"), X("bd"))])
    act(X("tc"), X("p0"), F.Copy)
    act(X("tb"), X("p3"), F.Identity, bias=cb(-31.0))
    act(X("ng"), X("ex"), F.Abs, scale=256.0)
    act(X("ex"), X("ex"), F.Abs, scale=1.0 / 4096)
    act(X("opp"), X("p2"), F.Identity, bias=cb(-160.0))
    mm(X("p5", 0, 32), [(h8("z8", 15 - r, 143 - r), h8("ha", r, 512, 16)) for r in range(16)])
    mm(X("p1"), [(h8("b8", 0, 128), h8("ha"))])
    tt(X("mp"), X("mp"), X("tri"), A.add)
    tt(X("mp"), X("mp"), X("blk"), A.subtract)
    ts(X("dj"), X("colf", 0, 32), 16.0, A.mult, rr, A.add)
    ts(X("hw"), X("p5", 0, 32), 2048.0, A.is_equal)
    ts(X("nu"), X("p5", 0, 32), 1024.0, A.add)
    ts(X("dl"), X("dj", 0, 16), AW - 1024.0 - BIG, A.add)
    ts(X("dj"), X("dj"), 512.0, A.add)
    ts(X("ta"), X("fti"), 4096.0, A.mult)
    wrap(X("p4", 0, 32), "bd", 0, 512)
    wrap(X("p4", 32, 64), "bc", 0, 512)
    mm(X("p6"), [(X("d0"), X("xl")), (X("d1"), X("xh")), (X("i128"), X("utb"))])
    tt(X("p7"), X("p7"), X("tc"), A.min)
    tt(X("p7"), X("p7"), X("tb"), A.min)
    tt(mine("qt"), X("p7"), X("ng"), A.add)
    relay("qt")
    tt(X("vv"), X("p7"), X("ex"), A.add)
    act(X("xw", 512), X("p1"), F.Identity, bias=cb(W - 1024.0), scale=-1.0)
    for k in range(16):
        act(selT(k), X("blk"), F.Copy, scale=col1("rm", k))
        if k == 7:
            act(X("ba"), X("p7"), F.Identity, bias=cb(64.0))
            act(X("bb"), X("p7"), F.Abs, bias=cb(63.0))

    def positions(t):
        if t > 0:
            wrap(X("p0", 0, 32), "hit", 0, 512)
            act(X("hw"), X("p0", 0, 32), F.Copy)
        mm(X("p7", 0, 32), [(X("blk"), X("hw"))])
        mm(X("p7", 32, 64), [(X("mp"), X("hw"))])

    def lanes(t):
        if t % 2 == 0:
            scan(X("s1"), X("ones", 0, 32), X("p7", 0, 32), 1023.0, A.mult, A.add)
        else:
            scan(X("s1", 16, 32), X("ones", 0, 16), X("p7", 16, 32), 1023.0, A.mult, A.add)
            scan(X("s1", 0, 16), X("ones", 0, 16), X("p7", 0, 16), col1("s1", 31), A.mult, A.add)
        tt(X("s2"), X("p7", 32, 64), X("s1"), A.add)
        tt(X("ps"), X("s2"), X("dj"), A.min)
        cp(X("posw"), X("ps"))
        cp(IND(X("lt"), X("posw")), X("comb"))
        L = X("lt", 0, 256)
        ts(X("fu"), L, 1.0 / 4096, A.mult)
        ts(X("ui"), L, 7, A.arith_shift_right, 15, A.bitwise_and)
        cp(X("uh"), X("ui"))
        ts(X("ia", 0, 256), L, 63, A.bitwise_and)
        ts(X("fm"), X("fu"), -1024.0, A.add)
        ts(X("xb"), X("ia", 0, 256), col1("pf", 6), A.mult)
        if t < RO - 1:
            dma("s", "lt", L, X("ltc"))

    positions(0)
    tt(X("comb"), X("p6"), X("ta"), A.add)
    ts(col1("pf", 6), col1("rm", 1), 63.0, A.mult, 1.0, A.add)
    mm(X("p2"), [(X("t32"), X("bc")), (X("blk"), X("bd")), (X("i64"), X("ba"))])
    mm(X("p3"), [(X("t32"), X("bc")), (X("blk"), X("bd")), (X("i64"), X("bb"))])
    act(X("ba"), X("p2"), F.Relu, bias=cb(33.0))
    act(X("bb"), X("p3"), F.Relu, bias=cb(32.0))
    wrap(X("p4", 64, 96), "ba", 0, 512)
    wrap(X("p4", 96, 128), "bb", 0, 512)
    act(piece("gd", me, me + 1), X("p4", 0, 128), F.Copy)
    relay("gd")
    for c in (64.125 - 2000, 63.125 - 2000, 1025.0 / 4096 - 100, 1025.0, 165 + 1.0 / 8192, BIG + 1024):
        cb(c)
    ms(X("aa"), 1999.0)
    ms(X("ao"), 2000.0)
    lanes(0)
    for a in (0, 512):
        act(X("keep", a, a + 512), X("ones"), F.Copy)
    ms(X("alpha", W), 0.0)
    for c in (256.0 * (V * me + 1) - 64, W - 1024.0 - BIG, -1024.0, 256.0 * me + 2048 - LEAVE):
        cb(c)
    ts(X("pd"), X("j16"), rr, A.not_equal, POIS, A.mult)
    ts(X("rs"), X("j16"), 0.0, A.is_equal, 2.0 ** 20, A.mult)
    ts(X("kw"), X("blk"), rr, A.mult, 0.5, A.mult)
    ts(col1("pf", 7), rr, -LNR, A.mult, -128 * LNR, A.add)
    ts(col1("pf", 12), rr, 5.5, A.is_gt, col1("pf", 15), A.mult)
    ts(col1("pf", 13), rr, -512.0, A.mult, 1024 - 255.5, A.add)
    ms(X("keep", 0, 1024, 16), 0.0)
    tt(col1("pf", 12), col1("pf", 12), col1("pf", 13), A.add)

    ts(X("em"), X("es"), rr, A.is_equal, -BIG, A.mult)
    ms(X("c48"), float(CAP))
    ms(X("vs"), 0.0)
    ms(X("em", 0, EQ, 65), 2.0 ** 20)
    ms(X("qt", W), 0.0)

    def fills(part):
        for c in (128.0, LEAVE, -29.0, 1024.0):
            cb(c)
        ts(col1("pf", 14), rr, -1.0, A.mult)

    def late_constants():
        dma("s", "tc", X("tabc"), X("tab", 0, W))
        for a in range(0, EQ, 512):
            b = min(EQ, a + 512)
            act(X("eq", a, b), X("ones", 0, b - a), F.Copy, scale=BIG)
        for n, c in (("dm", 2.5), ("ipo", -POIS), ("n128", -128.0), ("n256", -256.0), ("n8k", -8192.0), ("idf", 1.0),
                     ("id16", 1.0)):
            act(X(n), X("idb"), F.Copy, scale=c)
        for n, m, c in (("nblk", "blk", -1.0), ("bvp", "blk", BIG), ("bvn", "blk", -BIG), ("blk16", "blk", 1.0),
                        ("z16", "zz", 1.0), ("zp", "zz", BIG), ("zn", "zz", -BIG)):
            act(X(n), X(m), F.Copy, scale=c)
        act(X("l16"), X("colf", 0, 256), F.Copy, scale=16.0)
        act(X("pay"), X("colf", 0, 256), F.Copy)
        act(X("nm1"), X("colf"), F.Identity, bias=cb(256.0 * (V * me + 1) - 64), scale=256.0)
        act(X("xw", 256, 512), X("colf", 0, 256), F.Copy, scale=0.0)
        act(X("tw", 0, 256), X("colf", 0, 256), F.Identity, bias=cb(256.0 * me + 2048 - LEAVE))
        act(X("tw", 256, 512), X("colf", 0, 256), F.Copy, scale=0.0)

    def cols(q):
        chip = sorted(same(q) + [q])
        return WC // len(chip) * chip.index(q), WC // len(chip) * (chip.index(q) + 1)

    c0, c1 = cols(me)
    z = lambda n: X(n, c0, c1)
    table = lambda t, k, a, b: X("lk%d" % (t % 2), LK * (k // 2) + 2 * a + k % 2, LK * (k // 2) + 2 * b, 2)
    lkt = lambda t, k: table(t, k, c0, c1)
    ownk = lambda t, k: table(t, k, 32 * me, 32 * me + 32)

    def tables(t, pair, sem):
        part = lambda q: X("lk%d" % (t % 2), LK * pair + 2 * cols(q)[0], LK * pair + 2 * cols(q)[1])
        send([(part(me), at(mates), sem + str(t))], "ls%d" % t, pair == 1)
        settle("lk%d" % (t % 2), "ls%d" % t)
        lands(sum([part(m)[1] for m in mates], []), sem + str(t), sum(nen(m, 1, pair)[0] for m in mates))

    def first_state():
        q0, q1 = c0 // 32, -(-c1 // 32)
        gdv = lambda a: R("gd", T["gd"][:, q0:q1, a:a + 32])
        cp(X("rem", 32 * q0, 32 * q1), gdv(0))
        ts(X("nh1"), R("gd", T["gd"][:, :, 32:64]), 1.0, A.add)
        cp(X("sw", 32 * q0, 32 * q1), gdv(64))
        cp(X("nvd", 32 * q0, 32 * q1), gdv(96))
        ts(z("p6"), z("rem"), 0.0, A.is_equal)
        ts(z("fit"), z("rem"), 1.0, A.min, 2048.0, A.mult)
        ts(lkt(0, 2), z("sw"), -1.0, A.mult, 99.0, A.add)
        ts(lkt(0, 3), z("rem"), 101.0, A.add)
        tt(z("p6"), z("p6"), z("nh1"), A.mult)
        tt(z("p6"), z("p6"), z("nvd"), A.add)
        tt(z("p6"), z("p6"), z("sw"), A.subtract)
        ts(z("nvd"), z("p6"), 1.0, A.add)

    def goods(t, bank):
        a, b = z(bank), X(bank, 192 + c0, 192 + c1)
        ts(a, lkt(t, 0), NONE - 0.5, A.is_lt)
        if t == 1:
            ms(lkt(t + 1, 2), 50.0)
        tt(z("sw"), a, z("rem"), A.subtract)
        tt(z("aa"), z("aa"), a, A.subtract)
        ts(b, z("sw"), 0.0, A.is_gt)
        if t == 0:
            tt(a, a, z("nvd"), A.mult)
        tt(b, b, z("nh1"), A.mult)
        if t == 0:
            tt(lkt(1, 2), lkt(0, 2), a, A.subtract)
        tt(z("rem"), b, z("sw"), A.subtract)
        if t < RO - 2:
            tt(lkt(t + 1, 3), b, lkt(t, 3), A.add)
        ts(z("fit"), z("rem"), 1.0, A.min, 2048.0, A.mult)

    def last_turns():
        nh = X("nh1", 32 * me, 32 * me + 32)
        tt(X("s3"), X("ao"), ownk(RO - 2, 3), A.add)
        ts(X("s4"), X("s3"), 2100.5, A.is_lt)
        tt(X("s4"), X("s4"), nh, A.mult)
        tt(X("s3"), X("s3"), X("s4"), A.add)
        ts(X("s4"), X("s3"), 2101.5, A.is_lt)
        tt(X("s3"), X("ao"), X("s3"), A.subtract)
        ts(X("th", 32, 64), X("s4"), 32768.0, A.mult, 1024.0 - 8192, A.add)
        tt(X("s4"), X("s4"), nh, A.mult)
        tt(X("th", 0, 32), X("s3"), X("s4"), A.subtract)

    def names(t, b, bank):
        dn = "dn%d" % t
        unwrap(bank, (T[dn][:, 2 * b:2 * b + 2, 192:208], [(dn, 256 * q + 192, 256 * q + 208) for q in (2 * b, 2 * b + 1)]))
        if t < RO - 1:
            act(X("nt", 1 + 512 * b, 513 + 512 * b), X(bank), F.Identity, bias=cb(1025.0 / 4096 - 100), scale=1.0 / 4096)
        else:
            act(X("nt", NT + 1 + 512 * b, NT + 513 + 512 * b), X(bank), F.Identity, bias=cb(1025.0))

    def turn(bank, rhs, o, bias):
        mm1(X(bank), X("idf"), X("vv"), True, False)
        unwrap(bank, rhs, False)
        act(o, X(bank), F.Sign, bias=cb(bias))

    for t in range(RO):
        fac, dn, lk = "fac%d" % t, "dn%d" % t, "lk%d" % (t % 2)
        last = t == RO - 1
        dnp = lambda q, a=0, b=WC: R(dn, T[dn][:, q, a:b], 256 * q + a, 256 * q + b)
        if t > 0:
            wait("s", "cv", cnt["v"])
            dma("s", "tr%d" % t, X("tab", 0, W), X("tabc"))
        cuts = [0, 256] + [512 * c for c in range(1, 9)]
        for a, b in zip(cuts[:-1], cuts[1:]):
            act(X("ag", a, b), IND(X("alpha"), X("fu", a // 16, b // 16)), F.Copy)
        for c in range(8):
            bank = "p%d" % (c % 3)
            unwrap(bank, X("uh", 32 * c, 32 * c + 32))
            if c == 2:
                wrap(X("p4", 0, 16), "xb", 0, 256)
            if c == 4 and t > 0:
                mm(X("p6"), [(X("idb"), X("opp")), (X("idf"), X("ng")), (X("n128"), X("bd"))], True, False)
            if c == 6 and t > 0:
                unwrap("p6", X("lkn"), False)
            for a, b in ([(0, 256), (256, 512)] if c == 0 else [(0, 512)]):
                e = X("ag", 512 * c + a, 512 * c + b)
                tt(e, e, X(bank, a, b), A.mult)
            if c == 3:
                ts(dnp(me, 192, 208), X("p4", 0, 16), V * me - 1024.0, A.add)
                if t > 0:
                    cp(X("lkn"), ownk(t - 1, 3))
                gather_all(lambda q: dnp(q, 192, 208), "nr%d" % t)
            for d in {1: [0], 4: [2], 6: [4], 7: [6]}.get(c, []):
                if d == 6:
                    act(X("p3", 0, 192), X("sc", 15, 3072, 16), F.Copy)
                scan(X("sc", 512 * d, 512 * d + 1024), X("keep"), X("ag", 512 * d, 512 * d + 1024), 0.0, A.mult, A.max)
        if t == 0:
            late_constants()
            tt(X("dm"), X("dm"), X("blk"), A.subtract)
        else:
            act(X("bc"), IND(X("lk%d" % ((t - 1) % 2), LK), X("colw")), F.Copy)
            mm(X("p7"), [(X("idb"), X("bc")), (X("n256"), X("rd"))])
            act(X("bc"), X("p7"), F.Relu)
        cp(X("p3", 192, 256), X("sc", 3072 + 15, 4096, 16))
        for k in range(16):
            tk = R("top", T["top"][:, k:4096:16], k, k + 1)
            tt(tk, X("ag", k, 4096, 16), X("p3", 0, 256), A.is_equal)
            if t > 0 and k == 6:
                mm(X("p7"), [(X("blk"), X("bc"))])
            if last and k < 3:
                names(t, k, ("p0", "p2", "p0")[k])
            for h in range(2):
                th = R("top", T["top"][:, 2048 * h + k:2048 * h + 2048:16], k, k + 1)
                mm1(X(VOTE[h], 0, 128), X("zz", 15 - k, 143 - k), th, k == 0, k == 15)
        half = lambda n, h: X(n, 128 * h, 128 * h + 128)
        for h in range(2):
            act(half("wb", h), X(VOTE[h], 0, 128), F.Exp, bias=col1("pf", 7), scale=16 * LNR)
            mm(X(PICK[h], 0, 128), [(X("dm"), half("wb", h))])
        mm(X("p2", 256), [(X("dm"), X("wb"))])
        for h in range(2):
            mm1(X(VOTE[h], 0, 128), X("idb"), half("pd", h), True, False)
        mm(X("p3", 0, 256), [(X("idb"), X("pd")), (X("idb"), X("l16"))], True, False)
        if t > 0:
            tt(X("vv"), X("p6"), X("vv"), A.max)
        act(X("sg"), X("p2", 256), F.Sign)
        for h in range(2):
            ts(X(PICK[h], 0, 128), X(PICK[h], 0, 128), 0.0, A.is_gt)
        for h in range(2):
            tt(half("sf", h), X(PICK[h], 0, 128), half("fm", h), A.mult)
            mm1(X(VOTE[h], 0, 128), X("blk16"), half("sf", h), False, True)
        mm(X("p2", 0, 256), [(X("blk16"), X("sf"))])
        mm1(X("p3", 0, 256), X("kw"), X("sg"), False, True)
        mm(X("p0", 256), [(X("blk16"), X("sf"))])
        wrap(X("p6", 0, 16), "sf", 0, 256, "z16", True, False)
        for h in range(2):
            scan(half("ms", h), half("rs", h), X(VOTE[h], 0, 128), 0.0, A.add, A.min)
        scan(X("ks"), X("rs"), X("p3", 0, 256), 0.0, A.add, A.min)
        act(X("ab"), X("p2", 0, 256), F.Abs, bias=col1("pf", 12))
        act(X("nb"), X("ms", 15, 256, 16), F.Copy, scale=-BIG)
        ts(X("oh"), X("ab"), 256.0, A.is_lt)
        ts(X("ku"), X("ks", 15, 256, 16), 60.0, A.add)
        scan(X("vs", 1, 257), X("oh"), X("c48"), 0.0, A.add, A.min)
        wrap(X("p6", 0, 16), "vs", 1, 257, "zn", False, False)
        wrap(X("p6", 0, 16), "vs", 0, 256, "zp", False, True)
        for c in range(16):
            o, b = X("eq", 65 * c + 1, 65 * c + 65), 64 * (c // 4)
            if c < 6:
                ts(o, X("p0", 256 + b, 320 + b), col1("ms", 16 * c + 15), A.not_equal, BIG, A.mult)
            else:
                act(o, X("p2", b, b + 64), F.Abs, bias=col1("nb", c), scale=BIG)
        act(piece(fac, me, me + 1), IND(X("top"), X("ku")), F.Identity, bias=cb(1.0), scale=-1.0 / 16)
        if t == 0:
            wait("g", "a0", total["a0"])
        relay(fac)
        mm(X("p2", 256), [(X("blk16"), X("sf")), (X("bvn"), X("vs", 1, 257)), (X("bvp"), X("vs", 0, 256))])
        if last:
            turn("p5", X("ao"), X("bd"), 63.125 - 2000)
        act(X("xw", 0, 256), X("p2", 256), F.Relu, bias=cb(W - 1024.0 - BIG), scale=-1.0)
        act(X("gx"), IND(X("xw"), X("posw")), F.Identity, bias=cb(-1024.0))
        scan(X("es"), X("em"), X("eq"), 0.0, A.add, A.min)
        tt(X("s2", 0, 16), X("p6", 0, 16), X("es", 64, EQ, 65), A.subtract)
        tt(X("s3", 0, 16), X("s2", 0, 16), X("dl"), A.min)
        ts(X("xu"), X("s3", 0, 16), 1024.0 + BIG, A.add)
        for b in (3, 2, 1, 0):
            cp(IND(X("tab"), X("xu", 4 * b, 4 * b + 4)), X("pay", 64 * b, 64 * b + 64))
        H, Q = WC // 2, WC // 4
        halves = [X("p4", 0, H), X("p1", 0, H)]
        for hf in range(2):
            wrap(halves[hf], "tab", 16 * H * hf, 16 * H * (hf + 1))
        if t == 0:
            tt(X("ta"), IND(X("qt"), X("nu")), X("nm1"), A.subtract)
        elif last:
            last_turns()
        else:
            tt(X("tw", 512), X("p7"), X("vl"), A.min)
        wants = lambda q, hf: [a for a in range(cols(q)[0], cols(q)[1], Q) if a // H == hf]
        engines = lambda q, hf: nen(q, sum(len(wants(m, hf)) for m in same(q)), sum(len(wants(m, hf)) for m in other(q)))
        for hf in range(2):
            ts(dnp(me, H * hf, H * hf + H), halves[hf], 1.0 / 16, A.mult, 256.0 * me, A.add)
            send([(dnp(me, a, a + Q), at([q]), ("df%d" if q in far else "dn%d") % t)
                  for q in far + mates for a in wants(q, hf)], "sent")
            if hf == 0 and t == 0:
                fills(1)
                act(X("ta"), X("ta"), F.Abs)
                act(X("bc"), X("ta"), F.Relu, bias=cb(128.0), scale=-1.0)
            elif hf == 0 and last:
                tt(X("tw", 512), X("p7"), X("vl"), A.min)
        for qs, sem, side in ((far, "df%d" % t, 1), (mates, "dn%d" % t, 0)):
            lands(sum([dnp(q)[1] for q in qs], []), sem,
                  sum(len(wants(me, hf)) * engines(q, hf)[side] for q in qs for hf in range(2)))
        wrap(X("p0", 0, 32), "gx", 0, 512, "z16")
        if last:
            turn("p6", X("th", 0, 32), X("p4"), 165 + 1.0 / 8192)
            ts(X("ia"), X("vv"), 4096.0, A.mult)
        if t == 0:
            mm(X("p5"), [(X("blk"), X("bc"))])
        ts(X("yi"), X("p0", 0, 32), -1.0 / 16, A.mult, W - 1024.0, A.add)
        ts(X("yl"), X("yi"), 15, A.bitwise_and)
        ts(X("yc"), X("yi"), 3, A.arith_shift_right, 4094, A.bitwise_and)
        cp(X("lo"), X("yl"))
        tt(X("s4"), X("yc"), X("hw"), A.subtract)
        unwrap("p0", X("lo"))
        ts(X("colw"), X("s4"), 1.0, A.add)
        if t == 0:
            act(X("tw", 512), X("p5"), F.Identity, bias=cb(-29.0))
            first_state()
        else:
            goods(t - 1, "p7")
        act(X("vl"), IND(X("tw"), X("posw")), F.Copy)
        act(X("rd"), X("p0"), F.Abs, bias=col1("pf", 14))
        mm(X("p2"), [(X("ipo"), X("rd")), (X("id16"), X("vl"))])
        act(X("ex"), X("p2"), F.Relu, bias=cb(LEAVE))
        if not last:
            act(X("xw", 512), X("gx"), F.Identity, bias=cb(1024.0))
            for b in range(3):
                names(t, b, "p%d" % (3 + b))
        else:
            ts(X("ib"), X("ia"), 4095, A.bitwise_and)
            cp(X("gw"), X("yi"))
            mm1(X("p3"), X("n8k"), X("bd"), True, False)
            unwrap("p3", X("th", 32, 64), False)
            tt(X("tc"), X("p4"), X("ib"), A.mult)
            act(X("tb"), X("tc"), F.Identity, bias=cb(BIG + 1024), scale=-1.0)
        w = z("p1")
        qs = near + far
        tt(w, dnp(qs[0], c0, c1), dnp(qs[1], c0, c1), A.min)
        for q in qs[2:]:
            tt(w, w, dnp(q, c0, c1), A.min)
        tt(lkt(t, 0), w, z("fit"), A.add)
        tt(lkt(t, 1), w, z("aa"), A.max)
        tables(t, 0, "lr")
        ts(X("offu", c0, c1), lkt(t, 0), 1536.0, A.min)
        h = (c1 - c0) * 16
        cut = [0, h] if h <= 768 else [0, 576, 1152, h]
        shares = lambda q: [(16 * cols(q)[0] + a, 16 * cols(q)[0] + b) for a, b in zip(cut[:-1], cut[1:])]

        def rise(lo, hi):
            tt(X("alpha", lo, hi), IND(X(fac), X("offu", lo // 16, hi // 16)), X("alpha", lo, hi), A.mult)
            send([(X("alpha", lo, hi), at(mates), "ar%d" % t)], "as%d" % t)
        early = 3 if last else 2
        for j, part in enumerate(shares(me)[:early]):
            rise(*part)
            if last and j == len(shares(me)) // 2:
                tt(X("zf"), X("p3"), X("tb"), A.min)
                mm1(X("p0"), X("idf"), X("zf"), True, False)
        if last:
            ts(X("nu"), ownk(t, 0), -2047.0, A.add, 1537.0, A.min)
            act(X("gx"), IND(X("nt", NT), X("nu")), F.Identity, bias=cb(-1024.0))
        tt(X("hit"), IND(X(lk, 0, LK), X("colw")), X("ex"), A.is_lt)
        if not last:
            positions(t + 1)
        for part in shares(me)[early:]:
            rise(*part)
        settle("alpha", "as%d" % t)
        lands(sum([X("alpha", *part)[1] for m in mates for part in shares(m)], []), "ar%d" % t,
              sum(len(shares(m)) * nen(m, 1, 0)[0] for m in mates))
        if not last:
            ts(X("nu"), ownk(t, 0), -2047.0, A.add, 1537.0, A.min)
            tt(X("ao"), X("ao"), ownk(t, 1), A.min)
            tables(t, 1, "lq")
            act(X("ng"), IND(X("nt", 0, NT), X("nu")), F.Copy)
            turn("p5", X("ao"), X("bd"), 64.125 - 2000)
            lanes(t + 1)
    mm(X("p2"), [(X("idb"), X("ones")), (X("nblk"), X("hit"))])
    mm1(X("p0"), X("id16"), X("gx"), False, True)
    tt(X("ex"), X("p2"), X("monb"), A.mult)
    dma("s", "st0", T.yal[:], mine("alpha"))
    tt(X("ng"), X("p0"), X("tc"), A.max)
    dma("a", "st2", T.yh[:], X("ng"))
    tt(X("ta"), IND(X("alpha"), X("gw")), X("ex"), A.mult)
    dma("s", "st1", T.yp[:], X("ta"))
    for sem in sorted(total):
        wait("g", sem, total[sem])
